import numpy as np
import ml_dtypes


def mxq(x, axis, fmt="e4m3"):
    dtype, down = {"e4m3": (ml_dtypes.float8_e4m3fn, 7), "e5m2": (ml_dtypes.float8_e5m2, 14)}[fmt]
    v = np.moveaxis(np.asarray(x, np.float32).astype(ml_dtypes.bfloat16).astype(np.float64), axis, -1)
    blocks = v.reshape(v.shape[:-1] + (-1, 32))
    amax = np.abs(blocks).max(-1, keepdims=True)
    byte = np.maximum(np.where(amax > 0, np.frexp(amax)[1] - 1 + 127, 0) - down, 1)
    scale = np.exp2(byte - 127.0)
    codes = (blocks / scale).astype(np.float32).astype(dtype).astype(np.float64)
    return np.moveaxis((codes * scale).reshape(v.shape), -1, axis)


WIDE = False


def mx_kscale(k):
    if not WIDE:
        return np.ones(k)
    levels = np.array([18, -18])
    if k % 512:
        return np.exp2(np.random.permutation(np.resize(levels, k // 32))).repeat(32)
    a = np.empty((k // 512, 16))
    for p in range(k // 512):
        a[p, :8] = np.random.permutation(np.resize(levels, 8))
        for g in range(8):
            far = levels[np.abs(levels - a[p, g]) >= 10]
            a[p, g + 8] = far[np.random.randint(len(far))]
    return np.exp2(a.ravel()).repeat(32)


def f64(x):
    return np.asarray(x).astype(np.float64)


def striped(idx):
    return np.tile(np.asarray(idx).reshape(-1, 16).T, (8, 1)).astype(np.uint16)


def unstriped(offs):
    return offs[:16].T.reshape(-1).astype(np.int64)


E2M1 = np.array([0.0, 0.5, 1.0, 1.5, 2.0, 3.0, 4.0, 6.0, -0.0, -0.5, -1.0, -1.5, -2.0, -3.0, -4.0, -6.0])


def pack_weight(w, fmt):
    k, n = w.shape
    w = f64(np.asarray(w, np.float32).astype(ml_dtypes.bfloat16)).reshape(k // 32, 32, n)
    amax = np.abs(w).max(1)
    if fmt == "e4m3":
        byte = np.frexp(amax)[1] - 1 + 127 - 7
    else:
        mant, ex = np.frexp(amax / 6.0)
        byte = np.where(mant > 0.5, ex, ex - 1) + 127
    byte = np.clip(np.where(amax > 0, byte, 1), 1, 254)
    scaled = (w * np.exp2(127.0 - byte)[:, None, :]).reshape(k, n).astype(np.float32)
    by_word = np.ascontiguousarray(scaled.reshape(k // 512, 128, 4, n).transpose(0, 1, 3, 2))
    if fmt == "e4m3":
        words = by_word.astype(ml_dtypes.float8_e4m3fn).view(np.uint8)
    else:
        c = by_word.astype(ml_dtypes.float4_e2m1fn).view(np.uint8) & 0xF
        words = (c[..., 0::2] | (c[..., 1::2] << 4)).reshape(k // 512, 128, 2 * n)
    return np.ascontiguousarray(words), np.ascontiguousarray(byte.astype(np.uint8).reshape(k // 512, 16, n))


def unpack_weight(words, scales, fmt):
    g, _, n = scales.shape
    words = np.ascontiguousarray(words).reshape(g, 128, n, -1)
    if fmt == "e4m3":
        vals = words.view(ml_dtypes.float8_e4m3fn).astype(np.float64)
    else:
        nib = np.empty((g, 128, n, 4), np.uint8)
        nib[..., 0::2] = words & 0xF
        nib[..., 1::2] = words >> 4
        vals = E2M1[nib]
    vals = vals * np.repeat(np.exp2(scales.astype(np.float64) - 127.0), 8, axis=1)[..., None]
    return vals.transpose(0, 1, 3, 2).reshape(g * 512, n)


B, N, T, D, DV, R = 1, 512, 2048, 1024, 512, 512


def setup_inputs():
    n = np.random.standard_normal
    idx = np.random.permutation(T)[:B * N]
    s = mx_kscale(D)[:, None]
    z = mx_kscale(R)[:, None]
    q = n((B, D, R))
    do = n((B, DV, R))
    kp = pack_weight(n((D, T)) * (0.50 / np.sqrt(D)) / s, "e2m1")
    return {
        "qT": (q * s).astype(np.float32),
        "k_words": np.ascontiguousarray(kp[0].reshape(1, 2, 128, T, 2).transpose(0, 2, 3, 1, 4)).reshape(1, 128, T, 4),
        "k_scales": kp[1],
        "lse": (np.log(N) + 0.12 + 0.1 * n((B, R, 1))).astype(np.float32),
        "rw": (np.random.uniform(0.5, 1.5, (B, R, 1)) * N / np.sqrt(R) * z).astype(np.float32),
        "dom": (do.transpose(0, 2, 1) / z).astype(np.float32),
        "offs": striped(idx),
    }


def reference(qT, k_words, k_scales, lse, rw, dom, offs):
    idx = unstriped(offs)
    k = unpack_weight(k_words.reshape(1, 128, T, 2, 2).transpose(0, 3, 1, 2, 4).reshape(2, 128, 2 * T), k_scales, "e2m1")
    pick = lambda x: x[:, idx].reshape(x.shape[0], B, N).transpose(1, 0, 2)
    a = mxq(f64(qT), 1, "e4m3").transpose(0, 2, 1) @ pick(k)
    p = np.exp(a - f64(lse))
    dv = mxq(f64(dom), 1, "e5m2").transpose(0, 2, 1) @ mxq(f64(rw) * p, 1, "e4m3")
    gv = np.zeros((DV, T))
    gv[:, idx] = dv.transpose(1, 0, 2).reshape(DV, B * N)
    return gv

@@ -1,0 +1,167 @@
+from contextlib import ExitStack
+
+import concourse.mybir as mybir
+
+N, T, D, DV, R = 512, 2048, 1024, 512, 512
+FLOPS = 2 * R * N * D + 2 * DV * N * R
+
+F32 = mybir.dt.float32
+BF16 = mybir.dt.bfloat16
+I32 = mybir.dt.int32
+U32 = mybir.dt.uint32
+U16 = mybir.dt.uint16
+U8 = mybir.dt.uint8
+E4M3 = mybir.dt.float8_e4m3fn_x4
+E5M2 = mybir.dt.float8_e5m2_x4
+E2M1 = mybir.dt.float4_e2m1fn_x4
+ACT = mybir.ActivationFunctionType
+MULT = mybir.AluOpType.mult
+
+P = 128
+PACK = 4
+PASSES = D // (P * PACK)
+E_TILES = DV // P
+WINDOWS = 3
+Q_SPLIT = 88
+PW_SPLIT = 352
+
+
+def tile_attend_gat_lse_v_kernel(tc, qT, k_words, k_scales, lse, rw, dom, offs, out):
+    nc = tc.nc
+    with ExitStack() as ctx:
+        keep = ctx.enter_context(tc.tile_pool(name="keep", bufs=1))
+        psum = ctx.enter_context(tc.psum_pool(name="psum", bufs=1))
+
+        offsets = keep.tile([P, N // 16], U16, name="offsets")
+        scale_pool = keep.tile([P, PASSES * T], U8, name="scale_pool", align_bytes=64)
+        word_pool = keep.tile([P, T], U32, name="word_pool", align_bytes=64)
+        q_raw = [keep.tile([P, PACK * R], F32, name=f"q_raw{o}", align_bytes=64) for o in range(PASSES)]
+        dom_raw = keep.tile([P, PACK * DV], F32, name="dom_raw", align_bytes=64)
+        lse_sb = keep.tile([P, PACK], F32, name="lse_sb")
+        rw_sb = keep.tile([P, PACK], F32, name="rw_sb")
+        neg_lse = keep.tile([P, PACK], F32, name="neg_lse")
+        windows = [keep.tile([P, T], F32, name=f"window{w}", align_bytes=64) for w in range(WINDOWS - 1)]
+
+        nc.vector.memset(scale_pool[:].bitcast(I32), 0)
+
+        nc.sync.dma_start(offsets[:], offs)
+        q_rows = qT[0].rearrange("(o p t) r -> o p (t r)", o=PASSES, t=PACK)
+        nc.sync.dma_start(q_raw[0][:], q_rows[0])
+        nc.scalar.dma_start(
+            scale_pool[0:P:8, :].bitcast(I32).rearrange("f (o t) -> f o t", o=PASSES),
+            k_scales.bitcast(I32).rearrange("o f t -> f o t"),
+        )
+        nc.scalar.dma_start(lse_sb[:], lse[0].rearrange("(p j) one -> p (j one)", j=PACK))
+        nc.scalar.dma_start(rw_sb[:], rw[0].rearrange("(p j) one -> p (j one)", j=PACK))
+        nc.sync.dma_start(word_pool[:].bitcast(I32), k_words[0].rearrange("p t b -> p (t b)").bitcast(I32))
+        nc.sync.dma_start(q_raw[1][:], q_rows[1])
+        nc.sync.dma_start(dom_raw[:], dom[0].rearrange("(p j) e -> p (j e)", j=PACK))
+
+        nc.scalar.activation(neg_lse[:], lse_sb[:], ACT.Copy, scale=-1.0)
+        for window in windows:
+            nc.vector.memset(window[:], 0.0)
+
+        scale_picked = keep.tile([P, PASSES * N], U8, name="scale_picked", align_bytes=64)
+        k_plane = keep.tile([P, PASSES * N], U8, name="k_plane", align_bytes=64)
+        for o in range(PASSES):
+            nc.vector.tensor_copy(
+                scale_picked[:, o * N : (o + 1) * N], scale_pool[:, o * T : (o + 1) * T].indirect(offsets[:])
+            )
+        nc.vector.tensor_copy(k_plane[:].bitcast(I32), scale_picked[:].bitcast(I32))
+
+        q_bf = [keep.tile([P, PACK * R], BF16, name=f"q_bf{o}", tag=f"q_bf{o}", align_bytes=64) for o in range(PASSES)]
+        q_codes = [keep.tile([P, R], U32, name=f"q_codes{o}", align_bytes=64) for o in range(PASSES)]
+        q_plane = [keep.tile([P, R], U8, name=f"q_plane{o}", align_bytes=64) for o in range(PASSES)]
+        q_src = [q_raw[o][:].rearrange("p (t s j) -> p s t j", t=PACK, j=PACK) for o in range(PASSES)]
+        q_dst = [q_bf[o][:].rearrange("p (j s t) -> p s t j", t=PACK, j=PACK) for o in range(PASSES)]
+        nc.scalar.copy(q_dst[0][:, : P // 2], q_src[0][:, : P // 2])
+        for i in range(1, 4):
+            nc.scalar.dma_start(k_plane[i:P:32, :].bitcast(I32), scale_picked[8 * i : P : 32, :].bitcast(I32))
+        nc.scalar.copy(q_dst[0][:, P // 2 :], q_src[0][:, P // 2 :])
+
+        word_picked = keep.tile([P, N], U32, name="word_picked", align_bytes=64)
+        k_codes = keep.tile([P, PASSES * N], U16, name="k_codes", align_bytes=64)
+        nc.vector.tensor_copy(word_picked[:], word_pool[:].indirect(offsets[:]))
+        nc.vector.tensor_copy(
+            k_codes[:].rearrange("p (o n) -> p o n", o=PASSES),
+            word_picked[:].bitcast(U16).rearrange("p (n o) -> p o n", o=PASSES),
+        )
+
+        scores = [psum.tile([P, N], F32, name=f"scores{j}") for j in range(PACK)]
+
+        def score_pass(o, j):
+            cols = slice(j * P, (j + 1) * P)
+            nc.vector.quantize_mx(
+                q_codes[o][:, cols].bitcast(E4M3), q_plane[o][:, cols], q_bf[o][:, j * R : (j + 1) * R]
+            )
+            nc.tensor.matmul_mx(
+                scores[j][:],
+                lhsT=q_codes[o][:, cols].bitcast(E4M3),
+                lhsT_scale=q_plane[o][:, cols],
+                rhs=k_codes[:, o * N : (o + 1) * N].bitcast(E2M1),
+                rhs_scale=k_plane[:, o * N : (o + 1) * N],
+                start=(o == 0),
+                stop=(o == PASSES - 1),
+            )
+
+        for j in range(PACK):
+            score_pass(0, j)
+
+        nc.vector.tensor_copy(q_dst[1][:, :Q_SPLIT], q_src[1][:, :Q_SPLIT])
+        nc.scalar.copy(q_dst[1][:, Q_SPLIT:], q_src[1][:, Q_SPLIT:])
+        for j in range(PACK):
+            score_pass(1, j)
+        last_window = keep.tile([P, T], F32, name="last_window", tag="q_bf1", align_bytes=64)
+        nc.vector.memset(last_window[:], 0.0)
+        windows.append(last_window)
+
+        dom_bf = [keep.tile([P, PACK * P], BF16, name=f"dom_bf{e}", align_bytes=64) for e in range(E_TILES)]
+        dom_codes = [keep.tile([P, P], U32, name=f"dom_codes{e}", align_bytes=64) for e in range(E_TILES)]
+        dom_plane = [keep.tile([P, P], U8, name=f"dom_plane{e}", align_bytes=64) for e in range(E_TILES)]
+        dom_src = dom_raw[:].rearrange("p (j e c i) -> p e c j i", j=PACK, e=E_TILES, i=4)
+
+        def dom_interleave(e):
+            nc.vector.tensor_copy(dom_bf[e][:].rearrange("p (c i j) -> p c j i", i=4, j=PACK), dom_src[:, e])
+
+        def dom_quantize(e):
+            nc.vector.quantize_mx(dom_codes[e][:].bitcast(E5M2), dom_plane[e][:], dom_bf[e][:])
+
+        pw_rows = keep.tile([P, PACK * N], BF16, name="pw_rows", align_bytes=64)
+        for j in range(PACK):
+            p_row = keep.tile([P, N], F32, name=f"p_row{j}", align_bytes=64)
+            nc.scalar.activation(p_row[:], scores[j][:], ACT.Exp, bias=neg_lse[:, j : j + 1])
+            nc.vector.tensor_scalar(pw_rows[:, j * N : (j + 1) * N], p_row[:], rw_sb[:, j : j + 1], None, MULT)
+            if j == 1:
+                dom_interleave(0)
+            if j == 2:
+                dom_quantize(0)
+
+        pw_bf = keep.tile([P, PACK * N], BF16, name="pw_bf", align_bytes=64)
+        pw_src = pw_rows[:].rearrange("p (j c i) -> p c j i", j=PACK, i=4)
+        pw_dst = pw_bf[:].rearrange("p (c i j) -> p c j i", j=PACK, i=4)
+        nc.vector.tensor_copy(pw_dst[:, : PW_SPLIT // 4], pw_src[:, : PW_SPLIT // 4])
+        nc.scalar.copy(pw_dst[:, PW_SPLIT // 4 :], pw_src[:, PW_SPLIT // 4 :])
+        pw_codes = keep.tile([P, N], U32, name="pw_codes", align_bytes=64)
+        pw_plane = keep.tile([P, N], U8, name="pw_plane", align_bytes=64)
+        nc.vector.quantize_mx(pw_codes[:].bitcast(E4M3), pw_plane[:], pw_bf[:])
+        for e in range(1, E_TILES):
+            dom_interleave(e)
+        for e in range(1, E_TILES):
+            dom_quantize(e)
+
+        for e in range(E_TILES):
+            grad = psum.tile([P, N], F32, name=f"grad{e}")
+            nc.tensor.matmul_mx(
+                grad[:],
+                lhsT=dom_codes[e][:].bitcast(E5M2),
+                lhsT_scale=dom_plane[e][:],
+                rhs=pw_codes[:].bitcast(E4M3),
+                rhs_scale=pw_plane[:],
+                start=True,
+                stop=True,
+            )
+            grad_sb = keep.tile([P, N], F32, name=f"grad_sb{e}", align_bytes=64)
+            nc.scalar.copy(grad_sb[:], grad[:])
+            window = windows[e % WINDOWS]
+            nc.vector.tensor_copy(window[:].indirect(offsets[:]), grad_sb[:])
+            nc.sync.dma_start(out[e * P : (e + 1) * P, :], window[:])

@@ -23,7 +23,7 @@ PASSES = D // (P * PACK)
 E_TILES = DV // P
 WINDOWS = 3
 Q_SPLIT = 88
-PW_SPLIT = 352
+PW_SPLIT = 304
 
 
 def tile_attend_gat_lse_v_kernel(tc, qT, k_words, k_scales, lse, rw, dom, offs, out):
@@ -46,11 +46,13 @@ def tile_attend_gat_lse_v_kernel(tc, qT, k_words, k_scales, lse, rw, dom, offs, 
 
         nc.sync.dma_start(offsets[:], offs)
         q_rows = qT[0].rearrange("(o p t) r -> o p (t r)", o=PASSES, t=PACK)
-        nc.sync.dma_start(q_raw[0][:], q_rows[0])
-        nc.scalar.dma_start(
+        half = PACK * R // 2
+        nc.sync.dma_start(q_raw[0][:, :half], q_rows[0][:, :half])
+        nc.sync.dma_start(
             scale_pool[0:P:8, :].bitcast(I32).rearrange("f (o t) -> f o t", o=PASSES),
             k_scales.bitcast(I32).rearrange("o f t -> f o t"),
         )
+        nc.sync.dma_start(q_raw[0][:, half:], q_rows[0][:, half:])
         nc.scalar.dma_start(lse_sb[:], lse[0].rearrange("(p j) one -> p (j one)", j=PACK))
         nc.scalar.dma_start(rw_sb[:], rw[0].rearrange("(p j) one -> p (j one)", j=PACK))
         nc.sync.dma_start(word_pool[:].bitcast(I32), k_words[0].rearrange("p t b -> p (t b)").bitcast(I32))
@@ -77,7 +79,7 @@ def tile_attend_gat_lse_v_kernel(tc, qT, k_words, k_scales, lse, rw, dom, offs, 
         nc.scalar.copy(q_dst[0][:, : P // 2], q_src[0][:, : P // 2])
         for i in range(1, 4):
             nc.scalar.dma_start(k_plane[i:P:32, :].bitcast(I32), scale_picked[8 * i : P : 32, :].bitcast(I32))
-        nc.scalar.copy(q_dst[0][:, P // 2 :], q_src[0][:, P // 2 :])
+        nc.vector.tensor_copy(q_dst[0][:, P // 2 :], q_src[0][:, P // 2 :])
 
         word_picked = keep.tile([P, N], U32, name="word_picked", align_bytes=64)
         k_codes = keep.tile([P, PASSES * N], U16, name="k_codes", align_bytes=64)
@@ -89,11 +91,14 @@ def tile_attend_gat_lse_v_kernel(tc, qT, k_words, k_scales, lse, rw, dom, offs, 
 
         scores = [psum.tile([P, N], F32, name=f"scores{j}") for j in range(PACK)]
 
-        def score_pass(o, j):
+        def q_quantize(o, j):
             cols = slice(j * P, (j + 1) * P)
             nc.vector.quantize_mx(
                 q_codes[o][:, cols].bitcast(E4M3), q_plane[o][:, cols], q_bf[o][:, j * R : (j + 1) * R]
             )
+
+        def score_pass(o, j):
+            cols = slice(j * P, (j + 1) * P)
             nc.tensor.matmul_mx(
                 scores[j][:],
                 lhsT=q_codes[o][:, cols].bitcast(E4M3),
@@ -105,56 +110,65 @@ def tile_attend_gat_lse_v_kernel(tc, qT, k_words, k_scales, lse, rw, dom, offs, 
             )
 
         for j in range(PACK):
+            q_quantize(0, j)
+        for j in range(PACK - 1):
             score_pass(0, j)
 
         nc.vector.tensor_copy(q_dst[1][:, :Q_SPLIT], q_src[1][:, :Q_SPLIT])
         nc.scalar.copy(q_dst[1][:, Q_SPLIT:], q_src[1][:, Q_SPLIT:])
         for j in range(PACK):
+            q_quantize(1, j)
+        score_pass(1, 0)
+        score_pass(0, PACK - 1)
+        for j in range(1, PACK):
             score_pass(1, j)
         last_window = keep.tile([P, T], F32, name="last_window", tag="q_bf1", align_bytes=64)
         nc.vector.memset(last_window[:], 0.0)
         windows.append(last_window)
 
-        dom_bf = [keep.tile([P, PACK * P], BF16, name=f"dom_bf{e}", align_bytes=64) for e in range(E_TILES)]
-        dom_codes = [keep.tile([P, P], U32, name=f"dom_codes{e}", align_bytes=64) for e in range(E_TILES)]
-        dom_plane = [keep.tile([P, P], U8, name=f"dom_plane{e}", align_bytes=64) for e in range(E_TILES)]
-        dom_src = dom_raw[:].rearrange("p (j e c i) -> p e c j i", j=PACK, e=E_TILES, i=4)
+        dom_codes = keep.tile([P, DV], U32, name="dom_codes", align_bytes=64)
+        dom_plane = keep.tile([P, DV], U8, name="dom_plane", align_bytes=64)
+        dom_src = dom_raw[:].rearrange("p (j c i) -> p c j i", j=PACK, i=4)
 
-        def dom_interleave(e):
-            nc.vector.tensor_copy(dom_bf[e][:].rearrange("p (c i j) -> p c j i", i=4, j=PACK), dom_src[:, e])
+        def dom_interleave(lo, hi, tag):
+            dom_bf = keep.tile([P, PACK * (hi - lo)], BF16, name=f"dom_bf{lo}", tag=tag, align_bytes=64)
+            nc.vector.tensor_copy(
+                dom_bf[:].rearrange("p (c i j) -> p c j i", i=4, j=PACK), dom_src[:, lo // 4 : hi // 4]
+            )
+            return dom_bf
 
-        def dom_quantize(e):
-            nc.vector.quantize_mx(dom_codes[e][:].bitcast(E5M2), dom_plane[e][:], dom_bf[e][:])
+        def dom_quantize(lo, hi, dom_bf):
+            nc.vector.quantize_mx(dom_codes[:, lo:hi].bitcast(E5M2), dom_plane[:, lo:hi], dom_bf[:])
 
-        pw_rows = keep.tile([P, PACK * N], BF16, name="pw_rows", align_bytes=64)
+        pw_rows = keep.tile([P, PACK * N], BF16, name="pw_rows", tag="pw_rows", align_bytes=64)
         for j in range(PACK):
-            p_row = keep.tile([P, N], F32, name=f"p_row{j}", align_bytes=64)
+            p_row = keep.tile([P, N], F32, name=f"p_row{j}", tag=f"p_row{j}", align_bytes=64)
             nc.scalar.activation(p_row[:], scores[j][:], ACT.Exp, bias=neg_lse[:, j : j + 1])
             nc.vector.tensor_scalar(pw_rows[:, j * N : (j + 1) * N], p_row[:], rw_sb[:, j : j + 1], None, MULT)
             if j == 1:
-                dom_interleave(0)
+                dom_first = dom_interleave(0, P, "dom_first")
             if j == 2:
-                dom_quantize(0)
+                dom_quantize(0, P, dom_first)
 
         pw_bf = keep.tile([P, PACK * N], BF16, name="pw_bf", align_bytes=64)
         pw_src = pw_rows[:].rearrange("p (j c i) -> p c j i", j=PACK, i=4)
         pw_dst = pw_bf[:].rearrange("p (c i j) -> p c j i", j=PACK, i=4)
         nc.vector.tensor_copy(pw_dst[:, : PW_SPLIT // 4], pw_src[:, : PW_SPLIT // 4])
         nc.scalar.copy(pw_dst[:, PW_SPLIT // 4 :], pw_src[:, PW_SPLIT // 4 :])
+        dom_second = dom_interleave(P, 2 * P, f"p_row{PACK - 1}")
         pw_codes = keep.tile([P, N], U32, name="pw_codes", align_bytes=64)
         pw_plane = keep.tile([P, N], U8, name="pw_plane", align_bytes=64)
         nc.vector.quantize_mx(pw_codes[:].bitcast(E4M3), pw_plane[:], pw_bf[:])
-        for e in range(1, E_TILES):
-            dom_interleave(e)
-        for e in range(1, E_TILES):
-            dom_quantize(e)
+        dom_rest = dom_interleave(2 * P, DV, "pw_rows")
+        dom_quantize(P, 2 * P, dom_second)
+        dom_quantize(2 * P, DV, dom_rest)
 
         for e in range(E_TILES):
             grad = psum.tile([P, N], F32, name=f"grad{e}")
             nc.tensor.matmul_mx(
                 grad[:],
-                lhsT=dom_codes[e][:].bitcast(E5M2),
-                lhsT_scale=dom_plane[e][:],
+                lhsT=dom_codes[:, e * P : (e + 1) * P].bitcast(E5M2),
+                lhsT_scale=dom_plane[:, e * P : (e + 1) * P],
                 rhs=pw_codes[:].bitcast(E4M3),
                 rhs_scale=pw_plane[:],
                 start=True,

@@ -33,10 +33,9 @@ def tile_attend_gat_lse_v_kernel(tc, qT, k_words, k_scales, lse, rw, dom, offs, 
         psum = ctx.enter_context(tc.psum_pool(name="psum", bufs=1))
 
         offsets = keep.tile([P, N // 16], U16, name="offsets")
-        scale_pool = keep.tile([P, PASSES * T], U8, name="scale_pool", align_bytes=64)
-        word_pool = keep.tile([P, T], U32, name="word_pool", align_bytes=64)
-        q_raw = [keep.tile([P, PACK * R], F32, name=f"q_raw{o}", align_bytes=64) for o in range(PASSES)]
-        dom_raw = keep.tile([P, PACK * DV], F32, name="dom_raw", align_bytes=64)
+        scale_pool = keep.tile([P, PASSES * T], U8, name="scale_pool", tag="scale_pool", align_bytes=64)
+        word_pool = keep.tile([P, T], U32, name="word_pool", tag="word_pool", align_bytes=64)
+        k_plane = keep.tile([P, PASSES * N], U8, name="k_plane", align_bytes=64)
         lse_sb = keep.tile([P, PACK], F32, name="lse_sb")
         rw_sb = keep.tile([P, PACK], F32, name="rw_sb")
         neg_lse = keep.tile([P, PACK], F32, name="neg_lse")
@@ -44,42 +43,36 @@ def tile_attend_gat_lse_v_kernel(tc, qT, k_words, k_scales, lse, rw, dom, offs, 
 
         nc.vector.memset(scale_pool[:].bitcast(I32), 0)
 
+        words = k_words[0].rearrange("p t b -> p (t b)").bitcast(I32)
+        q_rows = qT[0].rearrange("(o p t) r -> o p t r", o=PASSES, t=PACK)
+        q_first = keep.tile([P, PACK, R], F32, name="q_first", align_bytes=64)
+        q_second = keep.tile([P, PACK, R // 2], F32, name="q_second", align_bytes=64)
         nc.sync.dma_start(offsets[:], offs)
-        q_rows = qT[0].rearrange("(o p t) r -> o p (t r)", o=PASSES, t=PACK)
-        half = PACK * R // 2
-        nc.sync.dma_start(q_raw[0][:, :half], q_rows[0][:, :half])
+        nc.sync.dma_start(word_pool[:, : T // 2].bitcast(I32), words[:, : T // 2])
         nc.sync.dma_start(
             scale_pool[0:P:8, :].bitcast(I32).rearrange("f (o t) -> f o t", o=PASSES),
             k_scales.bitcast(I32).rearrange("o f t -> f o t"),
         )
-        nc.sync.dma_start(q_raw[0][:, half:], q_rows[0][:, half:])
-        nc.scalar.dma_start(lse_sb[:], lse[0].rearrange("(p j) one -> p (j one)", j=PACK))
-        nc.scalar.dma_start(rw_sb[:], rw[0].rearrange("(p j) one -> p (j one)", j=PACK))
-        nc.sync.dma_start(word_pool[:].bitcast(I32), k_words[0].rearrange("p t b -> p (t b)").bitcast(I32))
-        nc.sync.dma_start(q_raw[1][:], q_rows[1])
-        nc.sync.dma_start(dom_raw[:], dom[0].rearrange("(p j) e -> p (j e)", j=PACK))
+        nc.sync.dma_start(lse_sb[:], lse[0].rearrange("(p j) one -> p (j one)", j=PACK))
+        nc.sync.dma_start(rw_sb[:], rw[0].rearrange("(p j) one -> p (j one)", j=PACK))
+        nc.sync.dma_start(word_pool[:, T // 2 :].bitcast(I32), words[:, T // 2 :])
+        nc.sync.dma_start(q_first[:], q_rows[0])
+        nc.sync.dma_start(q_second[:], q_rows[1][:, :, : R // 2])
 
         nc.scalar.activation(neg_lse[:], lse_sb[:], ACT.Copy, scale=-1.0)
+        nc.vector.memset(k_plane[:].bitcast(I32), 0)
         for window in windows:
             nc.vector.memset(window[:], 0.0)
 
         scale_picked = keep.tile([P, PASSES * N], U8, name="scale_picked", align_bytes=64)
-        k_plane = keep.tile([P, PASSES * N], U8, name="k_plane", align_bytes=64)
         for o in range(PASSES):
             nc.vector.tensor_copy(
                 scale_picked[:, o * N : (o + 1) * N], scale_pool[:, o * T : (o + 1) * T].indirect(offsets[:])
             )
-        nc.vector.tensor_copy(k_plane[:].bitcast(I32), scale_picked[:].bitcast(I32))
-
-        q_bf = [keep.tile([P, PACK * R], BF16, name=f"q_bf{o}", tag=f"q_bf{o}", align_bytes=64) for o in range(PASSES)]
-        q_codes = [keep.tile([P, R], U32, name=f"q_codes{o}", align_bytes=64) for o in range(PASSES)]
-        q_plane = [keep.tile([P, R], U8, name=f"q_plane{o}", align_bytes=64) for o in range(PASSES)]
-        q_src = [q_raw[o][:].rearrange("p (t s j) -> p s t j", t=PACK, j=PACK) for o in range(PASSES)]
-        q_dst = [q_bf[o][:].rearrange("p (j s t) -> p s t j", t=PACK, j=PACK) for o in range(PASSES)]
-        nc.scalar.copy(q_dst[0][:, : P // 2], q_src[0][:, : P // 2])
-        for i in range(1, 4):
-            nc.scalar.dma_start(k_plane[i:P:32, :].bitcast(I32), scale_picked[8 * i : P : 32, :].bitcast(I32))
-        nc.vector.tensor_copy(q_dst[0][:, P // 2 :], q_src[0][:, P // 2 :])
+        for i in range(4):
+            nc.sync.dma_start(k_plane[i:P:32, :].bitcast(I32), scale_picked[8 * i : P : 32, :].bitcast(I32))
+        q_third = keep.tile([P, PACK, R // 2], F32, name="q_third", tag="scale_pool", align_bytes=64)
+        nc.sync.dma_start(q_third[:], q_rows[1][:, :, R // 2 :])
 
         word_picked = keep.tile([P, N], U32, name="word_picked", align_bytes=64)
         k_codes = keep.tile([P, PASSES * N], U16, name="k_codes", align_bytes=64)
@@ -88,6 +81,21 @@ def tile_attend_gat_lse_v_kernel(tc, qT, k_words, k_scales, lse, rw, dom, offs, 
             k_codes[:].rearrange("p (o n) -> p o n", o=PASSES),
             word_picked[:].bitcast(U16).rearrange("p (n o) -> p o n", o=PASSES),
         )
+
+        q_bf = [keep.tile([P, PACK * R], BF16, name=f"q_bf{o}", tag=f"q_bf{o}", align_bytes=64) for o in range(PASSES)]
+        q_codes = [keep.tile([P, R], U32, name=f"q_codes{o}", align_bytes=64) for o in range(PASSES)]
+        q_plane = [keep.tile([P, R], U8, name=f"q_plane{o}", align_bytes=64) for o in range(PASSES)]
+
+        def q_interleave(o, q_raw, first, on_vector):
+            src = q_raw[:].rearrange("p t (s j) -> p s j t", j=PACK)
+            dst = q_bf[o][:].rearrange("p (j s t) -> p s j t", t=PACK, j=PACK)[:, first : first + src.shape[1]]
+            if on_vector:
+                nc.vector.tensor_copy(dst[:, :on_vector], src[:, :on_vector])
+            nc.scalar.copy(dst[:, on_vector:], src[:, on_vector:])
+
+        dom_raw = keep.tile([P, PACK * DV], F32, name="dom_raw", tag="word_pool", align_bytes=64)
+        nc.sync.dma_start(dom_raw[:], dom[0].rearrange("(p j) e -> p (j e)", j=PACK))
+        q_interleave(0, q_first, 0, 64)
 
         scores = [psum.tile([P, N], F32, name=f"scores{j}") for j in range(PACK)]
 
@@ -114,8 +122,8 @@ def tile_attend_gat_lse_v_kernel(tc, qT, k_words, k_scales, lse, rw, dom, offs, 
         for j in range(PACK - 1):
             score_pass(0, j)
 
-        nc.vector.tensor_copy(q_dst[1][:, :Q_SPLIT], q_src[1][:, :Q_SPLIT])
-        nc.scalar.copy(q_dst[1][:, Q_SPLIT:], q_src[1][:, Q_SPLIT:])
+        q_interleave(1, q_second, 0, 0)
+        q_interleave(1, q_third, P // 2, 44)
         for j in range(PACK):
             q_quantize(1, j)
         score_pass(1, 0)

@@ -21,9 +21,10 @@ P = 128
 PACK = 4
 PASSES = D // (P * PACK)
 E_TILES = DV // P
-WINDOWS = 3
-Q_SPLIT = 88
-PW_SPLIT = 304
+HALF = N // 2
+EARLY = 2
+Q_ON_VECTOR = (0, 0, 28, 44)
+PW_ON_VECTOR = 168
 
 
 def tile_attend_gat_lse_v_kernel(tc, qT, k_words, k_scales, lse, rw, dom, offs, out):
@@ -36,33 +37,43 @@ def tile_attend_gat_lse_v_kernel(tc, qT, k_words, k_scales, lse, rw, dom, offs, 
         scale_pool = keep.tile([P, PASSES * T], U8, name="scale_pool", tag="scale_pool", align_bytes=64)
         word_pool = keep.tile([P, T], U32, name="word_pool", tag="word_pool", align_bytes=64)
         k_plane = keep.tile([P, PASSES * N], U8, name="k_plane", align_bytes=64)
-        lse_sb = keep.tile([P, PACK], F32, name="lse_sb")
+        lse_sb = keep.tile([P, PACK], F32, name="lse_sb", tag="late_window", align_bytes=64)
         rw_sb = keep.tile([P, PACK], F32, name="rw_sb")
         neg_lse = keep.tile([P, PACK], F32, name="neg_lse")
-        windows = [keep.tile([P, T], F32, name=f"window{w}", align_bytes=64) for w in range(WINDOWS - 1)]
+        windows = [keep.tile([P, T], F32, name=f"window{w}", align_bytes=64) for w in range(EARLY)]
+        pw_codes = keep.tile([P, HALF + N], U32, name="pw_codes", align_bytes=64)
+        pw_plane = keep.tile([P, HALF + N], U8, name="pw_plane", align_bytes=64)
 
         nc.vector.memset(scale_pool[:].bitcast(I32), 0)
 
-        words = k_words[0].rearrange("p t b -> p (t b)").bitcast(I32)
-        q_rows = qT[0].rearrange("(o p t) r -> o p t r", o=PASSES, t=PACK)
-        q_first = keep.tile([P, PACK, R], F32, name="q_first", align_bytes=64)
-        q_second = keep.tile([P, PACK, R // 2], F32, name="q_second", align_bytes=64)
+        q_rows = qT[0].rearrange("(o p t) (h r) -> o h p t r", o=PASSES, t=PACK, h=2)
+        q_raw = {}
+
+        def q_load(o, h, tag):
+            q_raw[o, h] = keep.tile([P, PACK, R // 2], F32, name=f"q_raw{o}{h}", tag=tag, align_bytes=64)
+            nc.sync.dma_start(q_raw[o, h][:], q_rows[o][h])
+
         nc.sync.dma_start(offsets[:], offs)
-        nc.sync.dma_start(word_pool[:, : T // 2].bitcast(I32), words[:, : T // 2])
+        q_load(0, 0, "q_raw00")
         nc.sync.dma_start(
             scale_pool[0:P:8, :].bitcast(I32).rearrange("f (o t) -> f o t", o=PASSES),
             k_scales.bitcast(I32).rearrange("o f t -> f o t"),
         )
         nc.sync.dma_start(lse_sb[:], lse[0].rearrange("(p j) one -> p (j one)", j=PACK))
         nc.sync.dma_start(rw_sb[:], rw[0].rearrange("(p j) one -> p (j one)", j=PACK))
-        nc.sync.dma_start(word_pool[:, T // 2 :].bitcast(I32), words[:, T // 2 :])
-        nc.sync.dma_start(q_first[:], q_rows[0])
-        nc.sync.dma_start(q_second[:], q_rows[1][:, :, : R // 2])
+        nc.sync.dma_start(word_pool[:].bitcast(I32), k_words[0].rearrange("p t b -> p (t b)").bitcast(I32))
+        q_load(0, 1, "q_raw01")
+        q_load(1, 0, "q_raw10")
 
         nc.scalar.activation(neg_lse[:], lse_sb[:], ACT.Copy, scale=-1.0)
-        nc.vector.memset(k_plane[:].bitcast(I32), 0)
+        late_window = keep.tile([P, T], F32, name="late_window", tag="late_window", align_bytes=64)
+        nc.gpsimd.memset(late_window[:], 0.0)
         for window in windows:
             nc.vector.memset(window[:], 0.0)
+        windows.append(late_window)
+        nc.vector.memset(k_plane[:].bitcast(I32), 0)
+        nc.vector.memset(pw_codes[:, :HALF].bitcast(I32), 0)
+        nc.vector.memset(pw_plane[:, :HALF].bitcast(I32), 0)
 
         scale_picked = keep.tile([P, PASSES * N], U8, name="scale_picked", align_bytes=64)
         for o in range(PASSES):
@@ -71,8 +82,7 @@ def tile_attend_gat_lse_v_kernel(tc, qT, k_words, k_scales, lse, rw, dom, offs, 
             )
         for i in range(4):
             nc.sync.dma_start(k_plane[i:P:32, :].bitcast(I32), scale_picked[8 * i : P : 32, :].bitcast(I32))
-        q_third = keep.tile([P, PACK, R // 2], F32, name="q_third", tag="scale_pool", align_bytes=64)
-        nc.sync.dma_start(q_third[:], q_rows[1][:, :, R // 2 :])
+        q_load(1, 1, "scale_pool")
 
         word_picked = keep.tile([P, N], U32, name="word_picked", align_bytes=64)
         k_codes = keep.tile([P, PASSES * N], U16, name="k_codes", align_bytes=64)
@@ -82,28 +92,30 @@ def tile_attend_gat_lse_v_kernel(tc, qT, k_words, k_scales, lse, rw, dom, offs, 
             word_picked[:].bitcast(U16).rearrange("p (n o) -> p o n", o=PASSES),
         )
 
-        q_bf = [keep.tile([P, PACK * R], BF16, name=f"q_bf{o}", tag=f"q_bf{o}", align_bytes=64) for o in range(PASSES)]
         q_codes = [keep.tile([P, R], U32, name=f"q_codes{o}", align_bytes=64) for o in range(PASSES)]
         q_plane = [keep.tile([P, R], U8, name=f"q_plane{o}", align_bytes=64) for o in range(PASSES)]
+        dom_rows = dom[0].rearrange("(p j) (h e) -> h p j e", j=PACK, h=2)
+        dom_raw = {}
 
-        def q_interleave(o, q_raw, first, on_vector):
-            src = q_raw[:].rearrange("p t (s j) -> p s j t", j=PACK)
-            dst = q_bf[o][:].rearrange("p (j s t) -> p s j t", t=PACK, j=PACK)[:, first : first + src.shape[1]]
+        def dom_load(h, tag):
+            dom_raw[h] = keep.tile([P, PACK, DV // 2], F32, name=f"dom_raw{h}", tag=tag, align_bytes=64)
+            nc.sync.dma_start(dom_raw[h][:], dom_rows[h])
+
+        q_bf = [keep.tile([P, PACK * R], BF16, name=f"q_bf{o}", align_bytes=64) for o in range(PASSES)]
+
+        def q_interleave(o, h):
+            on_vector = Q_ON_VECTOR[2 * o + h]
+            src = q_raw[o, h][:].rearrange("p t (s j) -> p s j t", j=PACK)
+            dst = q_bf[o][:].rearrange("p (j s t) -> p s j t", t=PACK, j=PACK)[:, h * P // 2 : (h + 1) * P // 2]
             if on_vector:
                 nc.vector.tensor_copy(dst[:, :on_vector], src[:, :on_vector])
             nc.scalar.copy(dst[:, on_vector:], src[:, on_vector:])
 
-        dom_raw = keep.tile([P, PACK * DV], F32, name="dom_raw", tag="word_pool", align_bytes=64)
-        nc.sync.dma_start(dom_raw[:], dom[0].rearrange("(p j) e -> p (j e)", j=PACK))
-        q_interleave(0, q_first, 0, 64)
+        def q_quantize(o, first, last):
+            cols = slice(first * P, last * P)
+            nc.vector.quantize_mx(q_codes[o][:, cols].bitcast(E4M3), q_plane[o][:, cols], q_bf[o][:, first * R : last * R])
 
         scores = [psum.tile([P, N], F32, name=f"scores{j}") for j in range(PACK)]
-
-        def q_quantize(o, j):
-            cols = slice(j * P, (j + 1) * P)
-            nc.vector.quantize_mx(
-                q_codes[o][:, cols].bitcast(E4M3), q_plane[o][:, cols], q_bf[o][:, j * R : (j + 1) * R]
-            )
 
         def score_pass(o, j):
             cols = slice(j * P, (j + 1) * P)
@@ -117,73 +129,84 @@ def tile_attend_gat_lse_v_kernel(tc, qT, k_words, k_scales, lse, rw, dom, offs, 
                 stop=(o == PASSES - 1),
             )
 
+        dom_load(0, "word_pool")
+        q_interleave(0, 0)
+        q_interleave(0, 1)
+        q_quantize(0, 0, PACK)
+        dom_load(1, "q_raw01")
         for j in range(PACK):
-            q_quantize(0, j)
-        for j in range(PACK - 1):
             score_pass(0, j)
-
-        q_interleave(1, q_second, 0, 0)
-        q_interleave(1, q_third, P // 2, 44)
+        q_interleave(1, 0)
+        q_interleave(1, 1)
         for j in range(PACK):
-            q_quantize(1, j)
-        score_pass(1, 0)
-        score_pass(0, PACK - 1)
-        for j in range(1, PACK):
+            q_quantize(1, j, j + 1)
+        for j in range(PACK):
             score_pass(1, j)
-        last_window = keep.tile([P, T], F32, name="last_window", tag="q_bf1", align_bytes=64)
-        nc.vector.memset(last_window[:], 0.0)
-        windows.append(last_window)
 
         dom_codes = keep.tile([P, DV], U32, name="dom_codes", align_bytes=64)
         dom_plane = keep.tile([P, DV], U8, name="dom_plane", align_bytes=64)
-        dom_src = dom_raw[:].rearrange("p (j c i) -> p c j i", j=PACK, i=4)
 
-        def dom_interleave(lo, hi, tag):
-            dom_bf = keep.tile([P, PACK * (hi - lo)], BF16, name=f"dom_bf{lo}", tag=tag, align_bytes=64)
-            nc.vector.tensor_copy(
-                dom_bf[:].rearrange("p (c i j) -> p c j i", i=4, j=PACK), dom_src[:, lo // 4 : hi // 4]
-            )
-            return dom_bf
+        def dom_prepare(e, engine_copy, tag):
+            src = dom_raw[e // 2][:, :, (e % 2) * P : (e % 2 + 1) * P].rearrange("p j (c i) -> p c j i", i=4)
+            dom_bf = keep.tile([P, PACK * P], BF16, name=f"dom_bf{e}", tag=tag, align_bytes=64)
+            engine_copy(dom_bf[:].rearrange("p (c i j) -> p c j i", i=4, j=PACK), src)
+            cols = slice(e * P, (e + 1) * P)
+            nc.vector.quantize_mx(dom_codes[:, cols].bitcast(E5M2), dom_plane[:, cols], dom_bf[:])
 
-        def dom_quantize(lo, hi, dom_bf):
-            nc.vector.quantize_mx(dom_codes[:, lo:hi].bitcast(E5M2), dom_plane[:, lo:hi], dom_bf[:])
+        def weights(h):
+            pw_rows = keep.tile([P, PACK * HALF], BF16, name=f"pw_rows{h}", tag=f"pw_rows{h}", align_bytes=64)
+            for j in range(PACK):
+                p_row = keep.tile([P, HALF], F32, name=f"p_row{h}{j}", align_bytes=64)
+                nc.scalar.activation(
+                    p_row[:], scores[j][:, h * HALF : (h + 1) * HALF], ACT.Exp, bias=neg_lse[:, j : j + 1]
+                )
+                nc.vector.tensor_scalar(
+                    pw_rows[:, j * HALF : (j + 1) * HALF], p_row[:], rw_sb[:, j : j + 1], None, MULT
+                )
+            return pw_rows
 
-        pw_rows = keep.tile([P, PACK * N], BF16, name="pw_rows", tag="pw_rows", align_bytes=64)
-        for j in range(PACK):
-            p_row = keep.tile([P, N], F32, name=f"p_row{j}", tag=f"p_row{j}", align_bytes=64)
-            nc.scalar.activation(p_row[:], scores[j][:], ACT.Exp, bias=neg_lse[:, j : j + 1])
-            nc.vector.tensor_scalar(pw_rows[:, j * N : (j + 1) * N], p_row[:], rw_sb[:, j : j + 1], None, MULT)
-            if j == 1:
-                dom_first = dom_interleave(0, P, "dom_first")
-            if j == 2:
-                dom_quantize(0, P, dom_first)
+        def weights_quantize(h, pw_rows, on_vector):
+            pw_bf = keep.tile([P, PACK * HALF], BF16, name=f"pw_bf{h}", align_bytes=64)
+            src = pw_rows[:].rearrange("p (j c i) -> p c j i", j=PACK, i=4)
+            dst = pw_bf[:].rearrange("p (c i j) -> p c j i", j=PACK, i=4)
+            if on_vector:
+                nc.vector.tensor_copy(dst[:, : on_vector // 4], src[:, : on_vector // 4])
+            nc.scalar.copy(dst[:, on_vector // 4 :], src[:, on_vector // 4 :])
+            cols = slice((h + 1) * HALF, (h + 2) * HALF)
+            nc.vector.quantize_mx(pw_codes[:, cols].bitcast(E4M3), pw_plane[:, cols], pw_bf[:])
 
-        pw_bf = keep.tile([P, PACK * N], BF16, name="pw_bf", align_bytes=64)
-        pw_src = pw_rows[:].rearrange("p (j c i) -> p c j i", j=PACK, i=4)
-        pw_dst = pw_bf[:].rearrange("p (c i j) -> p c j i", j=PACK, i=4)
-        nc.vector.tensor_copy(pw_dst[:, : PW_SPLIT // 4], pw_src[:, : PW_SPLIT // 4])
-        nc.scalar.copy(pw_dst[:, PW_SPLIT // 4 :], pw_src[:, PW_SPLIT // 4 :])
-        dom_second = dom_interleave(P, 2 * P, f"p_row{PACK - 1}")
-        pw_codes = keep.tile([P, N], U32, name="pw_codes", align_bytes=64)
-        pw_plane = keep.tile([P, N], U8, name="pw_plane", align_bytes=64)
-        nc.vector.quantize_mx(pw_codes[:].bitcast(E4M3), pw_plane[:], pw_bf[:])
-        dom_rest = dom_interleave(2 * P, DV, "pw_rows")
-        dom_quantize(P, 2 * P, dom_second)
-        dom_quantize(2 * P, DV, dom_rest)
-
-        for e in range(E_TILES):
-            grad = psum.tile([P, N], F32, name=f"grad{e}")
+        def product(e, first, bank):
+            grad = psum.tile([P, N], F32, name=f"grad{e}_{first}", tag=bank)
             nc.tensor.matmul_mx(
                 grad[:],
                 lhsT=dom_codes[:, e * P : (e + 1) * P].bitcast(E5M2),
                 lhsT_scale=dom_plane[:, e * P : (e + 1) * P],
-                rhs=pw_codes[:].bitcast(E4M3),
-                rhs_scale=pw_plane[:],
+                rhs=pw_codes[:, first : first + N].bitcast(E4M3),
+                rhs_scale=pw_plane[:, first : first + N],
                 start=True,
                 stop=True,
             )
-            grad_sb = keep.tile([P, N], F32, name=f"grad_sb{e}", align_bytes=64)
-            nc.scalar.copy(grad_sb[:], grad[:])
-            window = windows[e % WINDOWS]
-            nc.vector.tensor_copy(window[:].indirect(offsets[:]), grad_sb[:])
-            nc.sync.dma_start(out[e * P : (e + 1) * P, :], window[:])
+            return grad
+
+        def scatter(e, grad, slots, tag, bank_copy=nc.scalar.copy):
+            width = slots.stop - slots.start
+            grad_sb = keep.tile([P, width], F32, name=f"grad_sb{e}_{slots.start}_{width}", tag=tag, align_bytes=64)
+            bank_copy(grad_sb[:], grad[:, N - width :])
+            window = windows[e % len(windows)]
+            nc.vector.tensor_copy(window[:].indirect(offsets[:, slots.start // 16 : slots.stop // 16]), grad_sb[:])
+
+        weights_quantize(0, weights(0), PW_ON_VECTOR)
+        dom_prepare(0, nc.vector.tensor_copy, "dom_bf0")
+        dom_prepare(1, nc.vector.tensor_copy, "dom_bf1")
+        early = [product(e, 0, f"early{e}") for e in range(EARLY)]
+        late_rows = weights(1)
+        scatter(0, early[0], slice(0, HALF), "grad_a", nc.vector.tensor_copy)
+        weights_quantize(1, late_rows, 0)
+        scatter(1, early[1], slice(0, HALF), "pw_rows1")
+        for e in range(EARLY):
+            scatter(e, product(e, HALF, f"late{e}"), slice(HALF, N), f"grad_b{e}")
+            nc.sync.dma_start(out[e * P : (e + 1) * P, :], windows[e][:])
+        for e in range(EARLY, E_TILES):
+            dom_prepare(e, nc.scalar.copy, f"pw_rows{e - EARLY}")
+            scatter(e, product(e, HALF, f"early{e - EARLY}"), slice(0, N), f"grad_w{e}")
+            nc.sync.dma_start(out[e * P : (e + 1) * P, :], windows[e % len(windows)][:])

@@ -23,7 +23,7 @@ PASSES = D // (P * PACK)
 E_TILES = DV // P
 HALF = N // 2
 EARLY = 2
-Q_ON_VECTOR = (0, 0, 28, 44)
+Q_ON_VECTOR = (0, 0, 24, 44)
 PW_ON_VECTOR = 168
 
 
@@ -37,7 +37,7 @@ def tile_attend_gat_lse_v_kernel(tc, qT, k_words, k_scales, lse, rw, dom, offs, 
         scale_pool = keep.tile([P, PASSES * T], U8, name="scale_pool", tag="scale_pool", align_bytes=64)
         word_pool = keep.tile([P, T], U32, name="word_pool", tag="word_pool", align_bytes=64)
         k_plane = keep.tile([P, PASSES * N], U8, name="k_plane", align_bytes=64)
-        lse_sb = keep.tile([P, PACK], F32, name="lse_sb", tag="late_window", align_bytes=64)
+        lse_sb = keep.tile([P, PACK], F32, name="lse_sb")
         rw_sb = keep.tile([P, PACK], F32, name="rw_sb")
         neg_lse = keep.tile([P, PACK], F32, name="neg_lse")
         windows = [keep.tile([P, T], F32, name=f"window{w}", align_bytes=64) for w in range(EARLY)]
@@ -66,14 +66,11 @@ def tile_attend_gat_lse_v_kernel(tc, qT, k_words, k_scales, lse, rw, dom, offs, 
         q_load(1, 0, "q_raw10")
 
         nc.scalar.activation(neg_lse[:], lse_sb[:], ACT.Copy, scale=-1.0)
-        late_window = keep.tile([P, T], F32, name="late_window", tag="late_window", align_bytes=64)
-        nc.gpsimd.memset(late_window[:], 0.0)
-        for window in windows:
-            nc.vector.memset(window[:], 0.0)
-        windows.append(late_window)
         nc.vector.memset(k_plane[:].bitcast(I32), 0)
         nc.vector.memset(pw_codes[:, :HALF].bitcast(I32), 0)
         nc.vector.memset(pw_plane[:, :HALF].bitcast(I32), 0)
+        for window in windows:
+            nc.vector.memset(window[:], 0.0)
 
         scale_picked = keep.tile([P, PASSES * N], U8, name="scale_picked", align_bytes=64)
         for o in range(PASSES):
@@ -105,8 +102,8 @@ def tile_attend_gat_lse_v_kernel(tc, qT, k_words, k_scales, lse, rw, dom, offs, 
 
         def q_interleave(o, h):
             on_vector = Q_ON_VECTOR[2 * o + h]
-            src = q_raw[o, h][:].rearrange("p t (s j) -> p s j t", j=PACK)
-            dst = q_bf[o][:].rearrange("p (j s t) -> p s j t", t=PACK, j=PACK)[:, h * P // 2 : (h + 1) * P // 2]
+            src = q_raw[o, h][:].rearrange("p t (s j) -> p s t j", j=PACK)
+            dst = q_bf[o][:].rearrange("p (j s t) -> p s t j", t=PACK, j=PACK)[:, h * P // 2 : (h + 1) * P // 2]
             if on_vector:
                 nc.vector.tensor_copy(dst[:, :on_vector], src[:, :on_vector])
             nc.scalar.copy(dst[:, on_vector:], src[:, on_vector:])
@@ -132,7 +129,9 @@ def tile_attend_gat_lse_v_kernel(tc, qT, k_words, k_scales, lse, rw, dom, offs, 
         dom_load(0, "word_pool")
         q_interleave(0, 0)
         q_interleave(0, 1)
-        q_quantize(0, 0, PACK)
+        q_quantize(0, 0, 1)
+        q_quantize(0, 1, 2)
+        q_quantize(0, 2, PACK)
         dom_load(1, "q_raw01")
         for j in range(PACK):
             score_pass(0, j)
@@ -153,20 +152,27 @@ def tile_attend_gat_lse_v_kernel(tc, qT, k_words, k_scales, lse, rw, dom, offs, 
             cols = slice(e * P, (e + 1) * P)
             nc.vector.quantize_mx(dom_codes[:, cols].bitcast(E5M2), dom_plane[:, cols], dom_bf[:])
 
-        def weights(h):
+        def weights(h, between=None):
+            p_rows = []
             pw_rows = keep.tile([P, PACK * HALF], BF16, name=f"pw_rows{h}", tag=f"pw_rows{h}", align_bytes=64)
             for j in range(PACK):
                 p_row = keep.tile([P, HALF], F32, name=f"p_row{h}{j}", align_bytes=64)
                 nc.scalar.activation(
                     p_row[:], scores[j][:, h * HALF : (h + 1) * HALF], ACT.Exp, bias=neg_lse[:, j : j + 1]
                 )
-                nc.vector.tensor_scalar(
-                    pw_rows[:, j * HALF : (j + 1) * HALF], p_row[:], rw_sb[:, j : j + 1], None, MULT
-                )
+                p_rows.append(p_row)
+            for j in range(PACK):
+                row = pw_rows[:, j * HALF : (j + 1) * HALF]
+                if h == 0:
+                    nc.vector.tensor_scalar(row, p_rows[j][:], rw_sb[:, j : j + 1], None, MULT)
+                else:
+                    if j == 0:
+                        between()
+                    nc.scalar.activation(row, p_rows[j][:], ACT.Copy, scale=rw_sb[:, j : j + 1])
             return pw_rows
 
         def weights_quantize(h, pw_rows, on_vector):
-            pw_bf = keep.tile([P, PACK * HALF], BF16, name=f"pw_bf{h}", align_bytes=64)
+            pw_bf = keep.tile([P, PACK * HALF], BF16, name=f"pw_bf{h}", tag=f"pw_bf{h}", align_bytes=64)
             src = pw_rows[:].rearrange("p (j c i) -> p c j i", j=PACK, i=4)
             dst = pw_bf[:].rearrange("p (c i j) -> p c j i", j=PACK, i=4)
             if on_vector:
@@ -199,8 +205,10 @@ def tile_attend_gat_lse_v_kernel(tc, qT, k_words, k_scales, lse, rw, dom, offs, 
         dom_prepare(0, nc.vector.tensor_copy, "dom_bf0")
         dom_prepare(1, nc.vector.tensor_copy, "dom_bf1")
         early = [product(e, 0, f"early{e}") for e in range(EARLY)]
-        late_rows = weights(1)
-        scatter(0, early[0], slice(0, HALF), "grad_a", nc.vector.tensor_copy)
+        late_window = keep.tile([P, T], F32, name="late_window", tag="pw_bf0", align_bytes=64)
+        nc.vector.memset(late_window[:], 0.0)
+        windows.append(late_window)
+        late_rows = weights(1, lambda: scatter(0, early[0], slice(0, HALF), "grad_a"))
         weights_quantize(1, late_rows, 0)
         scatter(1, early[1], slice(0, HALF), "pw_rows1")
         for e in range(EARLY):

@@ -23,7 +23,7 @@ PASSES = D // (P * PACK)
 E_TILES = DV // P
 HALF = N // 2
 EARLY = 2
-Q_ON_VECTOR = (0, 0, 24, 44)
+Q_ON_VECTOR = (0, 36, 44, 84)
 PW_ON_VECTOR = 168
 
 
@@ -31,14 +31,13 @@ def tile_attend_gat_lse_v_kernel(tc, qT, k_words, k_scales, lse, rw, dom, offs, 
     nc = tc.nc
     with ExitStack() as ctx:
         keep = ctx.enter_context(tc.tile_pool(name="keep", bufs=1))
+        shared = ctx.enter_context(tc.tile_pool(name="shared", bufs=1))
         psum = ctx.enter_context(tc.psum_pool(name="psum", bufs=1))
 
         offsets = keep.tile([P, N // 16], U16, name="offsets")
-        scale_pool = keep.tile([P, PASSES * T], U8, name="scale_pool", tag="scale_pool", align_bytes=64)
-        word_pool = keep.tile([P, T], U32, name="word_pool", tag="word_pool", align_bytes=64)
+        scale_pool = shared.tile([P, PASSES * T], U8, name="scale_pool", offset=4032, align_bytes=64)
+        word_pool = keep.tile([P, T], U32, name="word_pool", align_bytes=64)
         k_plane = keep.tile([P, PASSES * N], U8, name="k_plane", align_bytes=64)
-        lse_sb = keep.tile([P, PACK], F32, name="lse_sb")
-        rw_sb = keep.tile([P, PACK], F32, name="rw_sb")
         neg_lse = keep.tile([P, PACK], F32, name="neg_lse")
         windows = [keep.tile([P, T], F32, name=f"window{w}", align_bytes=64) for w in range(EARLY)]
         pw_codes = keep.tile([P, HALF + N], U32, name="pw_codes", align_bytes=64)
@@ -46,42 +45,49 @@ def tile_attend_gat_lse_v_kernel(tc, qT, k_words, k_scales, lse, rw, dom, offs, 
 
         nc.vector.memset(scale_pool[:].bitcast(I32), 0)
 
-        q_rows = qT[0].rearrange("(o p t) (h r) -> o h p t r", o=PASSES, t=PACK, h=2)
-        q_raw = {}
-
-        def q_load(o, h, tag):
-            q_raw[o, h] = keep.tile([P, PACK, R // 2], F32, name=f"q_raw{o}{h}", tag=tag, align_bytes=64)
-            nc.sync.dma_start(q_raw[o, h][:], q_rows[o][h])
+        q_rows = qT[0].rearrange("(o p h t) r -> o h p t r", o=PASSES, h=2, t=2)
+        q_first = keep.tile([P, 2, R], F32, name="q_first", align_bytes=64)
+        q_second = keep.tile([P, 2, R], F32, name="q_second", align_bytes=64)
+        q_third = keep.tile([P, 2, R], F32, name="q_third", align_bytes=64)
 
         nc.sync.dma_start(offsets[:], offs)
-        q_load(0, 0, "q_raw00")
+        nc.sync.dma_start(q_first[:], q_rows[0][0])
         nc.sync.dma_start(
             scale_pool[0:P:8, :].bitcast(I32).rearrange("f (o t) -> f o t", o=PASSES),
             k_scales.bitcast(I32).rearrange("o f t -> f o t"),
         )
-        nc.sync.dma_start(lse_sb[:], lse[0].rearrange("(p j) one -> p (j one)", j=PACK))
-        nc.sync.dma_start(rw_sb[:], rw[0].rearrange("(p j) one -> p (j one)", j=PACK))
         nc.sync.dma_start(word_pool[:].bitcast(I32), k_words[0].rearrange("p t b -> p (t b)").bitcast(I32))
-        q_load(0, 1, "q_raw01")
-        q_load(1, 0, "q_raw10")
+        nc.sync.dma_start(q_second[:], q_rows[0][1])
+        nc.sync.dma_start(q_third[:], q_rows[1][0])
 
-        nc.scalar.activation(neg_lse[:], lse_sb[:], ACT.Copy, scale=-1.0)
         nc.vector.memset(k_plane[:].bitcast(I32), 0)
         nc.vector.memset(pw_codes[:, :HALF].bitcast(I32), 0)
         nc.vector.memset(pw_plane[:, :HALF].bitcast(I32), 0)
         for window in windows:
-            nc.vector.memset(window[:], 0.0)
+            nc.vector.memset(window[:].bitcast(I32), 0)
 
-        scale_picked = keep.tile([P, PASSES * N], U8, name="scale_picked", align_bytes=64)
+        scale_picked = keep.tile([P, PASSES * N], U8, name="scale_picked", tag="scale_picked", align_bytes=64)
         for o in range(PASSES):
             nc.vector.tensor_copy(
                 scale_picked[:, o * N : (o + 1) * N], scale_pool[:, o * T : (o + 1) * T].indirect(offsets[:])
             )
         for i in range(4):
             nc.sync.dma_start(k_plane[i:P:32, :].bitcast(I32), scale_picked[8 * i : P : 32, :].bitcast(I32))
-        q_load(1, 1, "scale_pool")
+        q_last = shared.tile([P, 2, R], F32, name="q_last", offset=8064, align_bytes=64)
+        lse_sb = shared.tile([P, PACK], F32, name="lse_sb", offset=4096, align_bytes=64)
+        rw_sb = shared.tile([P, PACK], F32, name="rw_sb", offset=4160, align_bytes=64)
+        dom_raw = [
+            shared.tile([P, PACK, DV // 2], F32, name="dom_raw0", offset=0, align_bytes=64),
+            keep.tile([P, PACK, DV // 2], F32, name="dom_raw1", tag="scale_picked", align_bytes=64),
+        ]
+        dom_rows = dom[0].rearrange("(p j) (h e) -> h p j e", j=PACK, h=2)
+        nc.sync.dma_start(q_last[:], q_rows[1][1])
+        nc.sync.dma_start(lse_sb[:], lse[0].rearrange("(p j) one -> p (j one)", j=PACK))
+        nc.sync.dma_start(dom_raw[0][:], dom_rows[0])
+        nc.sync.dma_start(rw_sb[:], rw[0].rearrange("(p j) one -> p (j one)", j=PACK))
+        nc.sync.dma_start(dom_raw[1][:], dom_rows[1])
 
-        word_picked = keep.tile([P, N], U32, name="word_picked", align_bytes=64)
+        word_picked = keep.tile([P, N], U32, name="word_picked", tag="word_picked", align_bytes=64)
         k_codes = keep.tile([P, PASSES * N], U16, name="k_codes", align_bytes=64)
         nc.vector.tensor_copy(word_picked[:], word_pool[:].indirect(offsets[:]))
         nc.vector.tensor_copy(
@@ -91,19 +97,12 @@ def tile_attend_gat_lse_v_kernel(tc, qT, k_words, k_scales, lse, rw, dom, offs, 
 
         q_codes = [keep.tile([P, R], U32, name=f"q_codes{o}", align_bytes=64) for o in range(PASSES)]
         q_plane = [keep.tile([P, R], U8, name=f"q_plane{o}", align_bytes=64) for o in range(PASSES)]
-        dom_rows = dom[0].rearrange("(p j) (h e) -> h p j e", j=PACK, h=2)
-        dom_raw = {}
-
-        def dom_load(h, tag):
-            dom_raw[h] = keep.tile([P, PACK, DV // 2], F32, name=f"dom_raw{h}", tag=tag, align_bytes=64)
-            nc.sync.dma_start(dom_raw[h][:], dom_rows[h])
 
         q_bf = [keep.tile([P, PACK * R], BF16, name=f"q_bf{o}", align_bytes=64) for o in range(PASSES)]
 
-        def q_interleave(o, h):
-            on_vector = Q_ON_VECTOR[2 * o + h]
-            src = q_raw[o, h][:].rearrange("p t (s j) -> p s t j", j=PACK)
-            dst = q_bf[o][:].rearrange("p (j s t) -> p s t j", t=PACK, j=PACK)[:, h * P // 2 : (h + 1) * P // 2]
+        def q_interleave(o, raw, places, on_vector):
+            src = raw[:].rearrange("p t (s j) -> p s t j", j=PACK)
+            dst = q_bf[o][:].rearrange("p (j s t) -> p s t j", t=PACK, j=PACK)[:, :, places]
             if on_vector:
                 nc.vector.tensor_copy(dst[:, :on_vector], src[:, :on_vector])
             nc.scalar.copy(dst[:, on_vector:], src[:, on_vector:])
@@ -126,17 +125,16 @@ def tile_attend_gat_lse_v_kernel(tc, qT, k_words, k_scales, lse, rw, dom, offs, 
                 stop=(o == PASSES - 1),
             )
 
-        dom_load(0, "word_pool")
-        q_interleave(0, 0)
-        q_interleave(0, 1)
+        q_interleave(0, q_first, slice(0, 2), Q_ON_VECTOR[0])
+        q_interleave(0, q_second, slice(2, PACK), Q_ON_VECTOR[1])
         q_quantize(0, 0, 1)
         q_quantize(0, 1, 2)
         q_quantize(0, 2, PACK)
-        dom_load(1, "q_raw01")
         for j in range(PACK):
             score_pass(0, j)
-        q_interleave(1, 0)
-        q_interleave(1, 1)
+        q_interleave(1, q_third, slice(0, 2), Q_ON_VECTOR[2])
+        q_interleave(1, q_last, slice(2, PACK), Q_ON_VECTOR[3])
+        nc.scalar.activation(neg_lse[:], lse_sb[:], ACT.Copy, scale=-1.0)
         for j in range(PACK):
             q_quantize(1, j, j + 1)
         for j in range(PACK):
@@ -206,7 +204,7 @@ def tile_attend_gat_lse_v_kernel(tc, qT, k_words, k_scales, lse, rw, dom, offs, 
         dom_prepare(1, nc.vector.tensor_copy, "dom_bf1")
         early = [product(e, 0, f"early{e}") for e in range(EARLY)]
         late_window = keep.tile([P, T], F32, name="late_window", tag="pw_bf0", align_bytes=64)
-        nc.vector.memset(late_window[:], 0.0)
+        nc.vector.memset(late_window[:].bitcast(I32), 0)
         windows.append(late_window)
         late_rows = weights(1, lambda: scatter(0, early[0], slice(0, HALF), "grad_a"))
         weights_quantize(1, late_rows, 0)

@@ -23,7 +23,7 @@ PASSES = D // (P * PACK)
 E_TILES = DV // P
 HALF = N // 2
 EARLY = 2
-Q_ON_VECTOR = (0, 36, 44, 84)
+Q_ON_VECTOR = (0, 0, 0, 44)
 PW_ON_VECTOR = 168
 
 
@@ -31,78 +31,75 @@ def tile_attend_gat_lse_v_kernel(tc, qT, k_words, k_scales, lse, rw, dom, offs, 
     nc = tc.nc
     with ExitStack() as ctx:
         keep = ctx.enter_context(tc.tile_pool(name="keep", bufs=1))
-        shared = ctx.enter_context(tc.tile_pool(name="shared", bufs=1))
         psum = ctx.enter_context(tc.psum_pool(name="psum", bufs=1))
 
         offsets = keep.tile([P, N // 16], U16, name="offsets")
-        scale_pool = shared.tile([P, PASSES * T], U8, name="scale_pool", offset=4032, align_bytes=64)
-        word_pool = keep.tile([P, T], U32, name="word_pool", align_bytes=64)
-        k_plane = keep.tile([P, PASSES * N], U8, name="k_plane", align_bytes=64)
+        scale_pool = keep.tile([P, T], U8, name="scale_pool", tag="scale_pool", align_bytes=64)
+        word_pool = keep.tile([P, T], U32, name="word_pool", tag="word_pool", align_bytes=64)
+        k_plane = keep.tile([P, N], U8, name="k_plane", align_bytes=64)
         neg_lse = keep.tile([P, PACK], F32, name="neg_lse")
         windows = [keep.tile([P, T], F32, name=f"window{w}", align_bytes=64) for w in range(EARLY)]
-        pw_codes = keep.tile([P, HALF + N], U32, name="pw_codes", align_bytes=64)
-        pw_plane = keep.tile([P, HALF + N], U8, name="pw_plane", align_bytes=64)
+        late_codes = keep.tile([P, R + N], U32, name="late_codes", align_bytes=64)
+        late_plane = keep.tile([P, R + N], U8, name="late_plane", align_bytes=64)
+        pw_codes = late_codes[:, R - HALF :]
+        pw_plane = late_plane[:, R - HALF :]
 
         nc.vector.memset(scale_pool[:].bitcast(I32), 0)
 
-        q_rows = qT[0].rearrange("(o p h t) r -> o h p t r", o=PASSES, h=2, t=2)
-        q_first = keep.tile([P, 2, R], F32, name="q_first", align_bytes=64)
-        q_second = keep.tile([P, 2, R], F32, name="q_second", align_bytes=64)
-        q_third = keep.tile([P, 2, R], F32, name="q_third", align_bytes=64)
+        q_rows = qT[0].rearrange("(o p t) (h r) -> o h p t r", o=PASSES, t=PACK, h=2)
+        q_first = keep.tile([P, PACK, R // 2], F32, name="q_first", align_bytes=64)
+        q_second = keep.tile([P, PACK, R // 2], F32, name="q_second", align_bytes=64)
+        q_third = keep.tile([P, PACK, R // 2], F32, name="q_third", align_bytes=64)
+        q_last = keep.tile([P, PACK, R // 2], F32, name="q_last", align_bytes=64)
 
         nc.sync.dma_start(offsets[:], offs)
         nc.sync.dma_start(q_first[:], q_rows[0][0])
-        nc.sync.dma_start(
-            scale_pool[0:P:8, :].bitcast(I32).rearrange("f (o t) -> f o t", o=PASSES),
-            k_scales.bitcast(I32).rearrange("o f t -> f o t"),
-        )
+        scale_rows = k_scales.bitcast(I32)
+        for i in range(4):
+            nc.sync.dma_start(scale_pool[i:P:32, :].bitcast(I32), scale_rows[0].rearrange("(g i) t -> i g t", i=4)[i])
+        nc.sync.dma_start(scale_pool[4:P:8, :].bitcast(I32), scale_rows[1])
         nc.sync.dma_start(word_pool[:].bitcast(I32), k_words[0].rearrange("p t b -> p (t b)").bitcast(I32))
+        lse_sb = keep.tile([P, PACK], F32, name="lse_sb")
+        rw_sb = keep.tile([P, PACK], F32, name="rw_sb")
+        nc.sync.dma_start(lse_sb[:], lse[0].rearrange("(p j) one -> p (j one)", j=PACK))
+        nc.sync.dma_start(rw_sb[:], rw[0].rearrange("(p j) one -> p (j one)", j=PACK))
         nc.sync.dma_start(q_second[:], q_rows[0][1])
         nc.sync.dma_start(q_third[:], q_rows[1][0])
+        nc.sync.dma_start(q_last[:], q_rows[1][1])
 
         nc.vector.memset(k_plane[:].bitcast(I32), 0)
-        nc.vector.memset(pw_codes[:, :HALF].bitcast(I32), 0)
-        nc.vector.memset(pw_plane[:, :HALF].bitcast(I32), 0)
         for window in windows:
             nc.vector.memset(window[:].bitcast(I32), 0)
 
-        scale_picked = keep.tile([P, PASSES * N], U8, name="scale_picked", tag="scale_picked", align_bytes=64)
-        for o in range(PASSES):
-            nc.vector.tensor_copy(
-                scale_picked[:, o * N : (o + 1) * N], scale_pool[:, o * T : (o + 1) * T].indirect(offsets[:])
-            )
+        scale_picked = keep.tile([P, N], U8, name="scale_picked", align_bytes=64)
+        nc.vector.tensor_copy(scale_picked[:], scale_pool[:].indirect(offsets[:]))
         for i in range(4):
-            nc.sync.dma_start(k_plane[i:P:32, :].bitcast(I32), scale_picked[8 * i : P : 32, :].bitcast(I32))
-        q_last = shared.tile([P, 2, R], F32, name="q_last", offset=8064, align_bytes=64)
-        lse_sb = shared.tile([P, PACK], F32, name="lse_sb", offset=4096, align_bytes=64)
-        rw_sb = shared.tile([P, PACK], F32, name="rw_sb", offset=4160, align_bytes=64)
+            nc.sync.dma_start(k_plane[i:P:32, :].bitcast(I32), scale_picked[8 * i + 4 : P : 32, :].bitcast(I32))
+        k_planes = [scale_picked, k_plane]
         dom_raw = [
-            shared.tile([P, PACK, DV // 2], F32, name="dom_raw0", offset=0, align_bytes=64),
-            keep.tile([P, PACK, DV // 2], F32, name="dom_raw1", tag="scale_picked", align_bytes=64),
+            keep.tile([P, PACK, DV // 2], F32, name="dom_raw0", tag="scale_pool", align_bytes=64),
+            keep.tile([P, PACK, DV // 2], F32, name="dom_raw1", tag="word_pool", align_bytes=64),
         ]
         dom_rows = dom[0].rearrange("(p j) (h e) -> h p j e", j=PACK, h=2)
-        nc.sync.dma_start(q_last[:], q_rows[1][1])
-        nc.sync.dma_start(lse_sb[:], lse[0].rearrange("(p j) one -> p (j one)", j=PACK))
         nc.sync.dma_start(dom_raw[0][:], dom_rows[0])
-        nc.sync.dma_start(rw_sb[:], rw[0].rearrange("(p j) one -> p (j one)", j=PACK))
-        nc.sync.dma_start(dom_raw[1][:], dom_rows[1])
 
         word_picked = keep.tile([P, N], U32, name="word_picked", tag="word_picked", align_bytes=64)
         k_codes = keep.tile([P, PASSES * N], U16, name="k_codes", align_bytes=64)
         nc.vector.tensor_copy(word_picked[:], word_pool[:].indirect(offsets[:]))
+        nc.sync.dma_start(dom_raw[1][:], dom_rows[1])
         nc.vector.tensor_copy(
             k_codes[:].rearrange("p (o n) -> p o n", o=PASSES),
             word_picked[:].bitcast(U16).rearrange("p (n o) -> p o n", o=PASSES),
         )
 
-        q_codes = [keep.tile([P, R], U32, name=f"q_codes{o}", align_bytes=64) for o in range(PASSES)]
-        q_plane = [keep.tile([P, R], U8, name=f"q_plane{o}", align_bytes=64) for o in range(PASSES)]
+        q_codes = [keep.tile([P, R], U32, name="q_codes", align_bytes=64), late_codes]
+        q_plane = [keep.tile([P, R], U8, name="q_plane", align_bytes=64), late_plane]
 
-        q_bf = [keep.tile([P, PACK * R], BF16, name=f"q_bf{o}", align_bytes=64) for o in range(PASSES)]
+        q_bf = [keep.tile([P, PACK * R], BF16, name=f"q_bf{o}", tag=f"q_bf{o}", align_bytes=64) for o in range(PASSES)]
 
-        def q_interleave(o, raw, places, on_vector):
+        def q_interleave(o, raw, first, on_vector):
             src = raw[:].rearrange("p t (s j) -> p s t j", j=PACK)
-            dst = q_bf[o][:].rearrange("p (j s t) -> p s t j", t=PACK, j=PACK)[:, :, places]
+            dst = q_bf[o][:].rearrange("p (j s t) -> p s t j", t=PACK, j=PACK)[:, first : first + P // 2]
             if on_vector:
                 nc.vector.tensor_copy(dst[:, :on_vector], src[:, :on_vector])
             nc.scalar.copy(dst[:, on_vector:], src[:, on_vector:])
@@ -120,20 +117,19 @@ def tile_attend_gat_lse_v_kernel(tc, qT, k_words, k_scales, lse, rw, dom, offs, 
                 lhsT=q_codes[o][:, cols].bitcast(E4M3),
                 lhsT_scale=q_plane[o][:, cols],
                 rhs=k_codes[:, o * N : (o + 1) * N].bitcast(E2M1),
-                rhs_scale=k_plane[:, o * N : (o + 1) * N],
+                rhs_scale=k_planes[o][:],
                 start=(o == 0),
                 stop=(o == PASSES - 1),
             )
 
-        q_interleave(0, q_first, slice(0, 2), Q_ON_VECTOR[0])
-        q_interleave(0, q_second, slice(2, PACK), Q_ON_VECTOR[1])
-        q_quantize(0, 0, 1)
-        q_quantize(0, 1, 2)
+        q_interleave(0, q_first, 0, Q_ON_VECTOR[0])
+        q_interleave(0, q_second, P // 2, Q_ON_VECTOR[1])
+        q_quantize(0, 0, 2)
         q_quantize(0, 2, PACK)
         for j in range(PACK):
             score_pass(0, j)
-        q_interleave(1, q_third, slice(0, 2), Q_ON_VECTOR[2])
-        q_interleave(1, q_last, slice(2, PACK), Q_ON_VECTOR[3])
+        q_interleave(1, q_third, 0, Q_ON_VECTOR[2])
+        q_interleave(1, q_last, P // 2, Q_ON_VECTOR[3])
         nc.scalar.activation(neg_lse[:], lse_sb[:], ACT.Copy, scale=-1.0)
         for j in range(PACK):
             q_quantize(1, j, j + 1)
@@ -143,11 +139,14 @@ def tile_attend_gat_lse_v_kernel(tc, qT, k_words, k_scales, lse, rw, dom, offs, 
         dom_codes = keep.tile([P, DV], U32, name="dom_codes", align_bytes=64)
         dom_plane = keep.tile([P, DV], U8, name="dom_plane", align_bytes=64)
 
-        def dom_prepare(e, engine_copy, tag):
-            src = dom_raw[e // 2][:, :, (e % 2) * P : (e % 2 + 1) * P].rearrange("p j (c i) -> p c j i", i=4)
-            dom_bf = keep.tile([P, PACK * P], BF16, name=f"dom_bf{e}", tag=tag, align_bytes=64)
-            engine_copy(dom_bf[:].rearrange("p (c i j) -> p c j i", i=4, j=PACK), src)
-            cols = slice(e * P, (e + 1) * P)
+        def dom_prepare(first, last, engine_copy, tag):
+            half = first * P // (DV // 2)
+            raw = dom_raw[half][:, :, first * P - half * DV // 2 : last * P - half * DV // 2]
+            dom_bf = keep.tile([P, PACK * (last - first) * P], BF16, name=f"dom_bf{first}", tag=tag, align_bytes=64)
+            engine_copy(
+                dom_bf[:].rearrange("p (c i j) -> p c j i", i=4, j=PACK), raw.rearrange("p j (c i) -> p c j i", i=4)
+            )
+            cols = slice(first * P, last * P)
             nc.vector.quantize_mx(dom_codes[:, cols].bitcast(E5M2), dom_plane[:, cols], dom_bf[:])
 
         def weights(h, between=None):
@@ -200,19 +199,24 @@ def tile_attend_gat_lse_v_kernel(tc, qT, k_words, k_scales, lse, rw, dom, offs, 
             nc.vector.tensor_copy(window[:].indirect(offsets[:, slots.start // 16 : slots.stop // 16]), grad_sb[:])
 
         weights_quantize(0, weights(0), PW_ON_VECTOR)
-        dom_prepare(0, nc.vector.tensor_copy, "dom_bf0")
-        dom_prepare(1, nc.vector.tensor_copy, "dom_bf1")
-        early = [product(e, 0, f"early{e}") for e in range(EARLY)]
+        dom_prepare(0, 1, nc.vector.tensor_copy, "dom_bf0")
+        early = [product(0, 0, "early0")]
         late_window = keep.tile([P, T], F32, name="late_window", tag="pw_bf0", align_bytes=64)
         nc.vector.memset(late_window[:].bitcast(I32), 0)
         windows.append(late_window)
-        late_rows = weights(1, lambda: scatter(0, early[0], slice(0, HALF), "grad_a"))
+
+        def first_scatter():
+            dom_prepare(1, 2, nc.scalar.copy, "pw_rows0")
+            early.append(product(1, 0, "early1"))
+            scatter(0, early[0], slice(0, HALF), "grad_a")
+
+        late_rows = weights(1, first_scatter)
         weights_quantize(1, late_rows, 0)
         scatter(1, early[1], slice(0, HALF), "pw_rows1")
         for e in range(EARLY):
             scatter(e, product(e, HALF, f"late{e}"), slice(HALF, N), f"grad_b{e}")
             nc.sync.dma_start(out[e * P : (e + 1) * P, :], windows[e][:])
+        dom_prepare(2, 4, nc.scalar.copy, "pw_bf1")
         for e in range(EARLY, E_TILES):
-            dom_prepare(e, nc.scalar.copy, f"pw_rows{e - EARLY}")
             scatter(e, product(e, HALF, f"early{e - EARLY}"), slice(0, N), f"grad_w{e}")
             nc.sync.dma_start(out[e * P : (e + 1) * P, :], windows[e % len(windows)][:])

@@ -22,9 +22,9 @@ PACK = 4
 PASSES = D // (P * PACK)
 E_TILES = DV // P
 HALF = N // 2
-EARLY = 2
-Q_ON_VECTOR = (0, 0, 0, 44)
+WINDOWS = 3
 PW_ON_VECTOR = 168
+Q_ON_VECTOR = (0, 44, 32, 44)
 
 
 def tile_attend_gat_lse_v_kernel(tc, qT, k_words, k_scales, lse, rw, dom, offs, out):
@@ -38,7 +38,7 @@ def tile_attend_gat_lse_v_kernel(tc, qT, k_words, k_scales, lse, rw, dom, offs, 
         word_pool = keep.tile([P, T], U32, name="word_pool", tag="word_pool", align_bytes=64)
         k_plane = keep.tile([P, N], U8, name="k_plane", align_bytes=64)
         neg_lse = keep.tile([P, PACK], F32, name="neg_lse")
-        windows = [keep.tile([P, T], F32, name=f"window{w}", align_bytes=64) for w in range(EARLY)]
+        windows = [keep.tile([P, T], F32, name=f"window{w}", align_bytes=64) for w in range(WINDOWS)]
         late_codes = keep.tile([P, R + N], U32, name="late_codes", align_bytes=64)
         late_plane = keep.tile([P, R + N], U8, name="late_plane", align_bytes=64)
         pw_codes = late_codes[:, R - HALF :]
@@ -53,17 +53,19 @@ def tile_attend_gat_lse_v_kernel(tc, qT, k_words, k_scales, lse, rw, dom, offs, 
         q_last = keep.tile([P, PACK, R // 2], F32, name="q_last", align_bytes=64)
 
         nc.sync.dma_start(offsets[:], offs)
-        nc.sync.dma_start(q_first[:], q_rows[0][0])
+        words = k_words[0].rearrange("p t b -> p (t b)").bitcast(I32)
+        nc.sync.dma_start(word_pool[:, : T // 2].bitcast(I32), words[:, : T // 2])
         scale_rows = k_scales.bitcast(I32)
         for i in range(4):
             nc.sync.dma_start(scale_pool[i:P:32, :].bitcast(I32), scale_rows[0].rearrange("(g i) t -> i g t", i=4)[i])
         nc.sync.dma_start(scale_pool[4:P:8, :].bitcast(I32), scale_rows[1])
-        nc.sync.dma_start(word_pool[:].bitcast(I32), k_words[0].rearrange("p t b -> p (t b)").bitcast(I32))
+        nc.sync.dma_start(word_pool[:, T // 2 :].bitcast(I32), words[:, T // 2 :])
+        nc.sync.dma_start(q_first[:], q_rows[0][0])
+        nc.sync.dma_start(q_second[:], q_rows[0][1])
         lse_sb = keep.tile([P, PACK], F32, name="lse_sb")
         rw_sb = keep.tile([P, PACK], F32, name="rw_sb")
         nc.sync.dma_start(lse_sb[:], lse[0].rearrange("(p j) one -> p (j one)", j=PACK))
         nc.sync.dma_start(rw_sb[:], rw[0].rearrange("(p j) one -> p (j one)", j=PACK))
-        nc.sync.dma_start(q_second[:], q_rows[0][1])
         nc.sync.dma_start(q_third[:], q_rows[1][0])
         nc.sync.dma_start(q_last[:], q_rows[1][1])
 
@@ -124,7 +126,8 @@ def tile_attend_gat_lse_v_kernel(tc, qT, k_words, k_scales, lse, rw, dom, offs, 
 
         q_interleave(0, q_first, 0, Q_ON_VECTOR[0])
         q_interleave(0, q_second, P // 2, Q_ON_VECTOR[1])
-        q_quantize(0, 0, 2)
+        q_quantize(0, 0, 1)
+        q_quantize(0, 1, 2)
         q_quantize(0, 2, PACK)
         for j in range(PACK):
             score_pass(0, j)
@@ -149,32 +152,21 @@ def tile_attend_gat_lse_v_kernel(tc, qT, k_words, k_scales, lse, rw, dom, offs, 
             cols = slice(first * P, last * P)
             nc.vector.quantize_mx(dom_codes[:, cols].bitcast(E5M2), dom_plane[:, cols], dom_bf[:])
 
-        def weights(h, between=None):
-            p_rows = []
+        def weights(h):
             pw_rows = keep.tile([P, PACK * HALF], BF16, name=f"pw_rows{h}", tag=f"pw_rows{h}", align_bytes=64)
             for j in range(PACK):
                 p_row = keep.tile([P, HALF], F32, name=f"p_row{h}{j}", align_bytes=64)
                 nc.scalar.activation(
                     p_row[:], scores[j][:, h * HALF : (h + 1) * HALF], ACT.Exp, bias=neg_lse[:, j : j + 1]
                 )
-                p_rows.append(p_row)
-            for j in range(PACK):
-                row = pw_rows[:, j * HALF : (j + 1) * HALF]
-                if h == 0:
-                    nc.vector.tensor_scalar(row, p_rows[j][:], rw_sb[:, j : j + 1], None, MULT)
-                else:
-                    if j == 0:
-                        between()
-                    nc.scalar.activation(row, p_rows[j][:], ACT.Copy, scale=rw_sb[:, j : j + 1])
-            return pw_rows
-
-        def weights_quantize(h, pw_rows, on_vector):
+                nc.vector.tensor_scalar(
+                    pw_rows[:, j * HALF : (j + 1) * HALF], p_row[:], rw_sb[:, j : j + 1], None, MULT
+                )
             pw_bf = keep.tile([P, PACK * HALF], BF16, name=f"pw_bf{h}", tag=f"pw_bf{h}", align_bytes=64)
             src = pw_rows[:].rearrange("p (j c i) -> p c j i", j=PACK, i=4)
             dst = pw_bf[:].rearrange("p (c i j) -> p c j i", j=PACK, i=4)
-            if on_vector:
-                nc.vector.tensor_copy(dst[:, : on_vector // 4], src[:, : on_vector // 4])
-            nc.scalar.copy(dst[:, on_vector // 4 :], src[:, on_vector // 4 :])
+            nc.vector.tensor_copy(dst[:, : PW_ON_VECTOR // 4], src[:, : PW_ON_VECTOR // 4])
+            nc.scalar.copy(dst[:, PW_ON_VECTOR // 4 :], src[:, PW_ON_VECTOR // 4 :])
             cols = slice((h + 1) * HALF, (h + 2) * HALF)
             nc.vector.quantize_mx(pw_codes[:, cols].bitcast(E4M3), pw_plane[:, cols], pw_bf[:])
 
@@ -191,32 +183,22 @@ def tile_attend_gat_lse_v_kernel(tc, qT, k_words, k_scales, lse, rw, dom, offs, 
             )
             return grad
 
-        def scatter(e, grad, slots, tag, bank_copy=nc.scalar.copy):
+        def scatter(e, grad, slots, tag):
             width = slots.stop - slots.start
             grad_sb = keep.tile([P, width], F32, name=f"grad_sb{e}_{slots.start}_{width}", tag=tag, align_bytes=64)
-            bank_copy(grad_sb[:], grad[:, N - width :])
+            nc.scalar.copy(grad_sb[:], grad[:, N - width :])
             window = windows[e % len(windows)]
             nc.vector.tensor_copy(window[:].indirect(offsets[:, slots.start // 16 : slots.stop // 16]), grad_sb[:])
 
-        weights_quantize(0, weights(0), PW_ON_VECTOR)
+        weights(0)
         dom_prepare(0, 1, nc.vector.tensor_copy, "dom_bf0")
-        early = [product(0, 0, "early0")]
-        late_window = keep.tile([P, T], F32, name="late_window", tag="pw_bf0", align_bytes=64)
-        nc.vector.memset(late_window[:].bitcast(I32), 0)
-        windows.append(late_window)
-
-        def first_scatter():
-            dom_prepare(1, 2, nc.scalar.copy, "pw_rows0")
-            early.append(product(1, 0, "early1"))
-            scatter(0, early[0], slice(0, HALF), "grad_a")
-
-        late_rows = weights(1, first_scatter)
-        weights_quantize(1, late_rows, 0)
-        scatter(1, early[1], slice(0, HALF), "pw_rows1")
-        for e in range(EARLY):
-            scatter(e, product(e, HALF, f"late{e}"), slice(HALF, N), f"grad_b{e}")
-            nc.sync.dma_start(out[e * P : (e + 1) * P, :], windows[e][:])
+        early = product(0, 0, "early")
+        weights(1)
+        scatter(0, early, slice(0, HALF), "pw_rows1")
+        scatter(0, product(0, HALF, "grad0"), slice(HALF, N), "grad_b")
+        nc.sync.dma_start(out[:P, :], windows[0][:])
+        dom_prepare(1, 2, nc.scalar.copy, "pw_rows0")
         dom_prepare(2, 4, nc.scalar.copy, "pw_bf1")
-        for e in range(EARLY, E_TILES):
-            scatter(e, product(e, HALF, f"early{e - EARLY}"), slice(0, N), f"grad_w{e}")
-            nc.sync.dma_start(out[e * P : (e + 1) * P, :], windows[e % len(windows)][:])
+        for e in range(1, E_TILES):
+            scatter(e, product(e, HALF, f"grad{e}" if e < E_TILES - 1 else "early"), slice(0, N), f"grad_w{e}")
+            nc.sync.dma_start(out[e * P : (e + 1) * P, :], windows[e % WINDOWS][:])

@@ -23,14 +23,16 @@ PASSES = D // (P * PACK)
 E_TILES = DV // P
 HALF = N // 2
 WINDOWS = 3
-PW_ON_VECTOR = 168
-Q_ON_VECTOR = (0, 44, 32, 44)
+WINDOW_OF = (0, 1, 2, 1)
+Q_CUT = PACK * R - R // 2
+PW_ON_VECTOR = 176
 
 
 def tile_attend_gat_lse_v_kernel(tc, qT, k_words, k_scales, lse, rw, dom, offs, out):
     nc = tc.nc
     with ExitStack() as ctx:
         keep = ctx.enter_context(tc.tile_pool(name="keep", bufs=1))
+        turns = ctx.enter_context(tc.tile_pool(name="turns", bufs=1))
         psum = ctx.enter_context(tc.psum_pool(name="psum", bufs=1))
 
         offsets = keep.tile([P, N // 16], U16, name="offsets")
@@ -46,11 +48,8 @@ def tile_attend_gat_lse_v_kernel(tc, qT, k_words, k_scales, lse, rw, dom, offs, 
 
         nc.vector.memset(scale_pool[:].bitcast(I32), 0)
 
-        q_rows = qT[0].rearrange("(o p t) (h r) -> o h p t r", o=PASSES, t=PACK, h=2)
-        q_first = keep.tile([P, PACK, R // 2], F32, name="q_first", align_bytes=64)
-        q_second = keep.tile([P, PACK, R // 2], F32, name="q_second", align_bytes=64)
-        q_third = keep.tile([P, PACK, R // 2], F32, name="q_third", align_bytes=64)
-        q_last = keep.tile([P, PACK, R // 2], F32, name="q_last", align_bytes=64)
+        q_rows = qT[0].rearrange("(o p t) r -> o p (t r)", o=PASSES, t=PACK)
+        q_raw = [keep.tile([P, PACK * R], F32, name=f"q_raw{o}", align_bytes=64) for o in range(PASSES)]
 
         nc.sync.dma_start(offsets[:], offs)
         words = k_words[0].rearrange("p t b -> p (t b)").bitcast(I32)
@@ -60,14 +59,14 @@ def tile_attend_gat_lse_v_kernel(tc, qT, k_words, k_scales, lse, rw, dom, offs, 
             nc.sync.dma_start(scale_pool[i:P:32, :].bitcast(I32), scale_rows[0].rearrange("(g i) t -> i g t", i=4)[i])
         nc.sync.dma_start(scale_pool[4:P:8, :].bitcast(I32), scale_rows[1])
         nc.sync.dma_start(word_pool[:, T // 2 :].bitcast(I32), words[:, T // 2 :])
-        nc.sync.dma_start(q_first[:], q_rows[0][0])
-        nc.sync.dma_start(q_second[:], q_rows[0][1])
+        nc.sync.dma_start(q_raw[0][:, :Q_CUT], q_rows[0][:, :Q_CUT])
+        nc.sync.dma_start(q_raw[0][:, Q_CUT:], q_rows[0][:, Q_CUT:])
         lse_sb = keep.tile([P, PACK], F32, name="lse_sb")
         rw_sb = keep.tile([P, PACK], F32, name="rw_sb")
         nc.sync.dma_start(lse_sb[:], lse[0].rearrange("(p j) one -> p (j one)", j=PACK))
         nc.sync.dma_start(rw_sb[:], rw[0].rearrange("(p j) one -> p (j one)", j=PACK))
-        nc.sync.dma_start(q_third[:], q_rows[1][0])
-        nc.sync.dma_start(q_last[:], q_rows[1][1])
+        nc.sync.dma_start(q_raw[1][:, :Q_CUT], q_rows[1][:, :Q_CUT])
+        nc.sync.dma_start(q_raw[1][:, Q_CUT:], q_rows[1][:, Q_CUT:])
 
         nc.vector.memset(k_plane[:].bitcast(I32), 0)
         for window in windows:
@@ -86,29 +85,35 @@ def tile_attend_gat_lse_v_kernel(tc, qT, k_words, k_scales, lse, rw, dom, offs, 
         nc.sync.dma_start(dom_raw[0][:], dom_rows[0])
 
         word_picked = keep.tile([P, N], U32, name="word_picked", tag="word_picked", align_bytes=64)
-        k_codes = keep.tile([P, PASSES * N], U16, name="k_codes", align_bytes=64)
+        k_codes = [
+            keep.tile([P, N], U16, name="k_codes0", align_bytes=64),
+            keep.tile([P, N], U16, name="k_codes1", tag="k_codes", align_bytes=64),
+        ]
         nc.vector.tensor_copy(word_picked[:], word_pool[:].indirect(offsets[:]))
         nc.sync.dma_start(dom_raw[1][:], dom_rows[1])
-        nc.vector.tensor_copy(
-            k_codes[:].rearrange("p (o n) -> p o n", o=PASSES),
-            word_picked[:].bitcast(U16).rearrange("p (n o) -> p o n", o=PASSES),
-        )
+        word_halves = word_picked[:].bitcast(U16).rearrange("p (n o) -> p o n", o=PASSES)
+        nc.vector.tensor_copy(k_codes[0][:], word_halves[:, 0, :])
 
         q_codes = [keep.tile([P, R], U32, name="q_codes", align_bytes=64), late_codes]
         q_plane = [keep.tile([P, R], U8, name="q_plane", align_bytes=64), late_plane]
 
-        q_bf = [keep.tile([P, PACK * R], BF16, name=f"q_bf{o}", tag=f"q_bf{o}", align_bytes=64) for o in range(PASSES)]
+        q_bf = [
+            [keep.tile([P, 2 * R], BF16, name=f"q_bf{o}{u}", align_bytes=64) for u in range(2)] for o in range(PASSES)
+        ]
 
-        def q_interleave(o, raw, first, on_vector):
-            src = raw[:].rearrange("p t (s j) -> p s t j", j=PACK)
-            dst = q_bf[o][:].rearrange("p (j s t) -> p s t j", t=PACK, j=PACK)[:, first : first + P // 2]
-            if on_vector:
-                nc.vector.tensor_copy(dst[:, :on_vector], src[:, :on_vector])
-            nc.scalar.copy(dst[:, on_vector:], src[:, on_vector:])
+        def q_interleave(o, h, u, engine_copy):
+            src = q_raw[o][:].rearrange("p (t h s u v) -> p h u s t v", t=PACK, h=2, u=2, v=2)[:, h, u]
+            dst = q_bf[o][u][:].rearrange("p (v h s t) -> p h s t v", t=PACK, v=2, h=2)[:, h]
+            engine_copy(dst, src)
 
         def q_quantize(o, first, last):
             cols = slice(first * P, last * P)
-            nc.vector.quantize_mx(q_codes[o][:, cols].bitcast(E4M3), q_plane[o][:, cols], q_bf[o][:, first * R : last * R])
+            u = first // 2
+            nc.vector.quantize_mx(
+                q_codes[o][:, cols].bitcast(E4M3),
+                q_plane[o][:, cols],
+                q_bf[o][u][:, (first - 2 * u) * R : (last - 2 * u) * R],
+            )
 
         scores = [psum.tile([P, N], F32, name=f"scores{j}") for j in range(PACK)]
 
@@ -118,21 +123,25 @@ def tile_attend_gat_lse_v_kernel(tc, qT, k_words, k_scales, lse, rw, dom, offs, 
                 scores[j][:],
                 lhsT=q_codes[o][:, cols].bitcast(E4M3),
                 lhsT_scale=q_plane[o][:, cols],
-                rhs=k_codes[:, o * N : (o + 1) * N].bitcast(E2M1),
+                rhs=k_codes[o][:].bitcast(E2M1),
                 rhs_scale=k_planes[o][:],
                 start=(o == 0),
                 stop=(o == PASSES - 1),
             )
 
-        q_interleave(0, q_first, 0, Q_ON_VECTOR[0])
-        q_interleave(0, q_second, P // 2, Q_ON_VECTOR[1])
+        q_interleave(0, 0, 0, nc.scalar.copy)
+        q_interleave(0, 1, 0, nc.vector.tensor_copy)
+        for h in range(2):
+            q_interleave(0, h, 1, nc.scalar.copy)
         q_quantize(0, 0, 1)
         q_quantize(0, 1, 2)
         q_quantize(0, 2, PACK)
         for j in range(PACK):
             score_pass(0, j)
-        q_interleave(1, q_third, 0, Q_ON_VECTOR[2])
-        q_interleave(1, q_last, P // 2, Q_ON_VECTOR[3])
+        nc.vector.tensor_copy(k_codes[1][:], word_halves[:, 1, :])
+        for h in range(2):
+            q_interleave(1, h, 0, nc.vector.tensor_copy)
+            q_interleave(1, h, 1, nc.scalar.copy)
         nc.scalar.activation(neg_lse[:], lse_sb[:], ACT.Copy, scale=-1.0)
         for j in range(PACK):
             q_quantize(1, j, j + 1)
@@ -142,33 +151,73 @@ def tile_attend_gat_lse_v_kernel(tc, qT, k_words, k_scales, lse, rw, dom, offs, 
         dom_codes = keep.tile([P, DV], U32, name="dom_codes", align_bytes=64)
         dom_plane = keep.tile([P, DV], U8, name="dom_plane", align_bytes=64)
 
-        def dom_prepare(first, last, engine_copy, tag):
+        def dom_prepare(first, last, engine_copy, copies, quantizes, dom_bf):
             half = first * P // (DV // 2)
             raw = dom_raw[half][:, :, first * P - half * DV // 2 : last * P - half * DV // 2]
-            dom_bf = keep.tile([P, PACK * (last - first) * P], BF16, name=f"dom_bf{first}", tag=tag, align_bytes=64)
-            engine_copy(
-                dom_bf[:].rearrange("p (c i j) -> p c j i", i=4, j=PACK), raw.rearrange("p j (c i) -> p c j i", i=4)
-            )
-            cols = slice(first * P, last * P)
-            nc.vector.quantize_mx(dom_codes[:, cols].bitcast(E5M2), dom_plane[:, cols], dom_bf[:])
+            src = raw.rearrange("p j (c i) -> p c j i", i=4)
+            dst = dom_bf[:].rearrange("p (c i j) -> p c j i", i=4, j=PACK)
+            step = (last - first) * P // 4 // copies
+            for c in range(copies):
+                engine_copy(dst[:, c * step : (c + 1) * step], src[:, c * step : (c + 1) * step])
+            step = (last - first) * P // quantizes
+            for c in range(quantizes):
+                cols = slice(first * P + c * step, first * P + (c + 1) * step)
+                nc.vector.quantize_mx(
+                    dom_codes[:, cols].bitcast(E5M2), dom_plane[:, cols], dom_bf[:, PACK * c * step : PACK * (c + 1) * step]
+                )
 
-        def weights(h):
-            pw_rows = keep.tile([P, PACK * HALF], BF16, name=f"pw_rows{h}", tag=f"pw_rows{h}", align_bytes=64)
+        def exps(h, tag, last_pieces):
+            p_rows = keep.tile([P, PACK, HALF], F32, name=f"p_rows{h}", tag=tag, align_bytes=64)
             for j in range(PACK):
-                p_row = keep.tile([P, HALF], F32, name=f"p_row{h}{j}", align_bytes=64)
-                nc.scalar.activation(
-                    p_row[:], scores[j][:, h * HALF : (h + 1) * HALF], ACT.Exp, bias=neg_lse[:, j : j + 1]
+                width = HALF // last_pieces if j == PACK - 1 else HALF
+                for first in range(0, HALF, width):
+                    nc.scalar.activation(
+                        p_rows[:, j, first : first + width],
+                        scores[j][:, h * HALF + first : h * HALF + first + width],
+                        ACT.Exp,
+                        bias=neg_lse[:, j : j + 1],
+                    )
+            return p_rows
+
+        def weights_quantize(h, pw_bf, first, last):
+            cols = slice((h + 1) * HALF + first, (h + 1) * HALF + last)
+            nc.vector.quantize_mx(pw_codes[:, cols].bitcast(E4M3), pw_plane[:, cols], pw_bf[:, PACK * first : PACK * last])
+
+        def first_weights():
+            p_rows = exps(0, "p_rows0", 2)
+            pw_rows = turns.tile([P, PACK, HALF], BF16, name="pw_rows0", offset=PACK * HALF, align_bytes=64)
+            pieces = (slice(0, HALF // 2), slice(HALF // 2, HALF))
+            for j in range(PACK - 1):
+                nc.vector.tensor_scalar(pw_rows[:, j, :], p_rows[:, j, :], rw_sb[:, j : j + 1], None, MULT)
+            for piece in pieces:
+                nc.vector.tensor_scalar(pw_rows[:, PACK - 1, piece], p_rows[:, PACK - 1, piece], rw_sb[:, PACK - 1 :], None, MULT)
+            pw_bf = keep.tile([P, PACK * HALF], BF16, name="pw_bf0", align_bytes=64)
+            for piece in pieces:
+                nc.vector.tensor_copy(
+                    pw_bf[:, PACK * piece.start : PACK * piece.stop].rearrange("p (c i j) -> p c j i", j=PACK, i=4),
+                    pw_rows[:, :, piece].rearrange("p j (c i) -> p c j i", i=4),
                 )
-                nc.vector.tensor_scalar(
-                    pw_rows[:, j * HALF : (j + 1) * HALF], p_row[:], rw_sb[:, j : j + 1], None, MULT
-                )
-            pw_bf = keep.tile([P, PACK * HALF], BF16, name=f"pw_bf{h}", tag=f"pw_bf{h}", align_bytes=64)
-            src = pw_rows[:].rearrange("p (j c i) -> p c j i", j=PACK, i=4)
+            for piece in pieces:
+                weights_quantize(0, pw_bf, piece.start, piece.stop)
+
+        def second_weights():
+            p_rows = exps(1, "k_codes", 2)
+            pw_bf = turns.tile([P, PACK * HALF], BF16, name="pw_bf1", offset=PACK * HALF, align_bytes=64)
             dst = pw_bf[:].rearrange("p (c i j) -> p c j i", j=PACK, i=4)
-            nc.vector.tensor_copy(dst[:, : PW_ON_VECTOR // 4], src[:, : PW_ON_VECTOR // 4])
-            nc.scalar.copy(dst[:, PW_ON_VECTOR // 4 :], src[:, PW_ON_VECTOR // 4 :])
-            cols = slice((h + 1) * HALF, (h + 2) * HALF)
-            nc.vector.quantize_mx(pw_codes[:, cols].bitcast(E4M3), pw_plane[:, cols], pw_bf[:])
+            groups = PW_ON_VECTOR // 4
+            for first, last in ((0, HALF // 8), (HALF // 8, groups)):
+                nc.vector.tensor_tensor(
+                    dst[:, first:last],
+                    p_rows[:].rearrange("p j (c i) -> p c j i", i=4)[:, first:last],
+                    rw_sb[:].unsqueeze(1).unsqueeze(3).to_broadcast([P, last - first, PACK, 4]),
+                    MULT,
+                )
+            pw_rows = keep.tile([P, PACK, HALF - PW_ON_VECTOR], BF16, name="pw_rows1", tag="pw_rows", align_bytes=64)
+            for j in range(PACK):
+                nc.scalar.activation(pw_rows[:, j, :], p_rows[:, j, PW_ON_VECTOR:], ACT.Copy, scale=rw_sb[:, j : j + 1])
+            nc.scalar.copy(dst[:, groups:], pw_rows[:].rearrange("p j (c i) -> p c j i", i=4))
+            weights_quantize(1, pw_bf, 0, HALF // 2)
+            weights_quantize(1, pw_bf, HALF // 2, HALF)
 
         def product(e, first, bank):
             grad = psum.tile([P, N], F32, name=f"grad{e}_{first}", tag=bank)
@@ -187,18 +236,25 @@ def tile_attend_gat_lse_v_kernel(tc, qT, k_words, k_scales, lse, rw, dom, offs, 
             width = slots.stop - slots.start
             grad_sb = keep.tile([P, width], F32, name=f"grad_sb{e}_{slots.start}_{width}", tag=tag, align_bytes=64)
             nc.scalar.copy(grad_sb[:], grad[:, N - width :])
-            window = windows[e % len(windows)]
+            window = windows[WINDOW_OF[e]]
             nc.vector.tensor_copy(window[:].indirect(offsets[:, slots.start // 16 : slots.stop // 16]), grad_sb[:])
 
-        weights(0)
-        dom_prepare(0, 1, nc.vector.tensor_copy, "dom_bf0")
+        dom_early = turns.tile([P, 2 * PACK * P], BF16, name="dom_early", offset=PACK * HALF, align_bytes=64)
+        dom_prepare(0, 2, nc.vector.tensor_copy, 2, 2, dom_early)
+        first_weights()
         early = product(0, 0, "early")
-        weights(1)
-        scatter(0, early, slice(0, HALF), "pw_rows1")
-        scatter(0, product(0, HALF, "grad0"), slice(HALF, N), "grad_b")
-        nc.sync.dma_start(out[:P, :], windows[0][:])
-        dom_prepare(1, 2, nc.scalar.copy, "pw_rows0")
-        dom_prepare(2, 4, nc.scalar.copy, "pw_bf1")
-        for e in range(1, E_TILES):
-            scatter(e, product(e, HALF, f"grad{e}" if e < E_TILES - 1 else "early"), slice(0, N), f"grad_w{e}")
-            nc.sync.dma_start(out[e * P : (e + 1) * P, :], windows[e % WINDOWS][:])
+        second_weights()
+        scatter(0, early, slice(0, HALF), "pw_rows")
+
+        def finish(e, slots, bank):
+            scatter(e, product(e, HALF, bank), slots, f"grad_w{e}")
+            nc.sync.dma_start(out[e * P : (e + 1) * P, :], windows[WINDOW_OF[e]][:])
+
+        dom_third = turns.tile([P, PACK * P], BF16, name="dom_third", offset=PACK * HALF, align_bytes=64)
+        dom_prepare(2, 3, nc.scalar.copy, 1, 1, dom_third)
+        finish(1, slice(0, N), "grad1")
+        finish(0, slice(HALF, N), "grad0")
+        dom_last = keep.tile([P, PACK * P], BF16, name="dom_last", tag="pw_rows", align_bytes=64)
+        dom_prepare(3, 4, nc.scalar.copy, 1, 1, dom_last)
+        finish(2, slice(0, N), "grad2")
+        finish(3, slice(0, N), "early")

@@ -23,9 +23,8 @@ PASSES = D // (P * PACK)
 E_TILES = DV // P
 HALF = N // 2
 WINDOWS = 3
-WINDOW_OF = (0, 1, 2, 1)
+WINDOW_OF = (0, 1, 2, 3)
 Q_CUT = PACK * R - R // 2
-PW_ON_VECTOR = 176
 
 
 def tile_attend_gat_lse_v_kernel(tc, qT, k_words, k_scales, lse, rw, dom, offs, out):
@@ -41,10 +40,8 @@ def tile_attend_gat_lse_v_kernel(tc, qT, k_words, k_scales, lse, rw, dom, offs, 
         k_plane = keep.tile([P, N], U8, name="k_plane", align_bytes=64)
         neg_lse = keep.tile([P, PACK], F32, name="neg_lse")
         windows = [keep.tile([P, T], F32, name=f"window{w}", align_bytes=64) for w in range(WINDOWS)]
-        late_codes = keep.tile([P, R + N], U32, name="late_codes", align_bytes=64)
-        late_plane = keep.tile([P, R + N], U8, name="late_plane", align_bytes=64)
-        pw_codes = late_codes[:, R - HALF :]
-        pw_plane = late_plane[:, R - HALF :]
+        pw_codes = keep.tile([P, N], U32, name="pw_codes", align_bytes=64)
+        pw_plane = keep.tile([P, N], U8, name="pw_plane", align_bytes=64)
 
         nc.vector.memset(scale_pool[:].bitcast(I32), 0)
 
@@ -85,20 +82,18 @@ def tile_attend_gat_lse_v_kernel(tc, qT, k_words, k_scales, lse, rw, dom, offs, 
         nc.sync.dma_start(dom_raw[0][:], dom_rows[0])
 
         word_picked = keep.tile([P, N], U32, name="word_picked", tag="word_picked", align_bytes=64)
-        k_codes = [
-            keep.tile([P, N], U16, name="k_codes0", align_bytes=64),
-            keep.tile([P, N], U16, name="k_codes1", tag="k_codes", align_bytes=64),
-        ]
+        k_codes0 = keep.tile([P, N], U16, name="k_codes0", align_bytes=64)
+        k_codes1 = keep.tile([P, HALF], U16, name="k_codes1", align_bytes=64)
         nc.vector.tensor_copy(word_picked[:], word_pool[:].indirect(offsets[:]))
         nc.sync.dma_start(dom_raw[1][:], dom_rows[1])
         word_halves = word_picked[:].bitcast(U16).rearrange("p (n o) -> p o n", o=PASSES)
-        nc.vector.tensor_copy(k_codes[0][:], word_halves[:, 0, :])
+        nc.vector.tensor_copy(k_codes0[:], word_halves[:, 0, :])
 
-        q_codes = [keep.tile([P, R], U32, name="q_codes", align_bytes=64), late_codes]
-        q_plane = [keep.tile([P, R], U8, name="q_plane", align_bytes=64), late_plane]
+        q_codes = [keep.tile([P, R], U32, name=f"q_codes{o}", align_bytes=64) for o in range(PASSES)]
+        q_plane = [keep.tile([P, R], U8, name=f"q_plane{o}", align_bytes=64) for o in range(PASSES)]
 
         q_bf = [
-            [keep.tile([P, 2 * R], BF16, name=f"q_bf{o}{u}", align_bytes=64) for u in range(2)] for o in range(PASSES)
+            [keep.tile([P, 2 * R], BF16, name=f"q_bf{o}{u}", tag=f"q_bf{o}{u}", align_bytes=64) for u in range(2)] for o in range(PASSES)
         ]
 
         def q_interleave(o, h, u, engine_copy):
@@ -115,16 +110,16 @@ def tile_attend_gat_lse_v_kernel(tc, qT, k_words, k_scales, lse, rw, dom, offs, 
                 q_bf[o][u][:, (first - 2 * u) * R : (last - 2 * u) * R],
             )
 
-        scores = [psum.tile([P, N], F32, name=f"scores{j}") for j in range(PACK)]
+        scores = [[psum.tile([P, HALF], F32, name=f"scores{j}{h}", tag=f"bank{j}{h}") for h in range(2)] for j in range(PACK)]
 
-        def score_pass(o, j):
+        def score_pass(o, j, h, codes):
             cols = slice(j * P, (j + 1) * P)
             nc.tensor.matmul_mx(
-                scores[j][:],
+                scores[j][h][:],
                 lhsT=q_codes[o][:, cols].bitcast(E4M3),
                 lhsT_scale=q_plane[o][:, cols],
-                rhs=k_codes[o][:].bitcast(E2M1),
-                rhs_scale=k_planes[o][:],
+                rhs=codes.bitcast(E2M1),
+                rhs_scale=k_planes[o][:, h * HALF : (h + 1) * HALF],
                 start=(o == 0),
                 stop=(o == PASSES - 1),
             )
@@ -137,8 +132,8 @@ def tile_attend_gat_lse_v_kernel(tc, qT, k_words, k_scales, lse, rw, dom, offs, 
         q_quantize(0, 1, 2)
         q_quantize(0, 2, PACK)
         for j in range(PACK):
-            score_pass(0, j)
-        nc.vector.tensor_copy(k_codes[1][:], word_halves[:, 1, :])
+            score_pass(0, j, 0, k_codes0[:, :HALF])
+        nc.vector.tensor_copy(k_codes1[:], word_halves[:, 1, :HALF])
         for h in range(2):
             q_interleave(1, h, 0, nc.vector.tensor_copy)
             q_interleave(1, h, 1, nc.scalar.copy)
@@ -146,115 +141,152 @@ def tile_attend_gat_lse_v_kernel(tc, qT, k_words, k_scales, lse, rw, dom, offs, 
         for j in range(PACK):
             q_quantize(1, j, j + 1)
         for j in range(PACK):
-            score_pass(1, j)
+            score_pass(1, j, 0, k_codes1[:])
+        for j in range(PACK):
+            score_pass(0, j, 1, k_codes0[:, HALF:])
+        k_codes_last = keep.tile([P, HALF], U16, name="k_codes_last", tag="q_bf11", align_bytes=64)
+        nc.vector.tensor_copy(k_codes_last[:], word_halves[:, 1, HALF:])
+        for j in range(PACK):
+            score_pass(1, j, 1, k_codes_last[:])
 
-        dom_codes = keep.tile([P, DV], U32, name="dom_codes", align_bytes=64)
+        dom_codes = {}
         dom_plane = keep.tile([P, DV], U8, name="dom_plane", align_bytes=64)
 
-        def dom_prepare(first, last, engine_copy, copies, quantizes, dom_bf):
-            half = first * P // (DV // 2)
-            raw = dom_raw[half][:, :, first * P - half * DV // 2 : last * P - half * DV // 2]
-            src = raw.rearrange("p j (c i) -> p c j i", i=4)
-            dst = dom_bf[:].rearrange("p (c i j) -> p c j i", i=4, j=PACK)
-            step = (last - first) * P // 4 // copies
-            for c in range(copies):
-                engine_copy(dst[:, c * step : (c + 1) * step], src[:, c * step : (c + 1) * step])
-            step = (last - first) * P // quantizes
-            for c in range(quantizes):
-                cols = slice(first * P + c * step, first * P + (c + 1) * step)
-                nc.vector.quantize_mx(
-                    dom_codes[:, cols].bitcast(E5M2), dom_plane[:, cols], dom_bf[:, PACK * c * step : PACK * (c + 1) * step]
-                )
+        def dom_interleave(e, engine_copy, dom_bf):
+            half = e // 2
+            raw = dom_raw[half][:, :, (e - 2 * half) * P : (e - 2 * half + 1) * P]
+            engine_copy(
+                dom_bf.rearrange("p (c i j) -> p c j i", i=4, j=PACK), raw.rearrange("p j (c i) -> p c j i", i=4)
+            )
 
-        def exps(h, tag, last_pieces):
-            p_rows = keep.tile([P, PACK, HALF], F32, name=f"p_rows{h}", tag=tag, align_bytes=64)
+        def dom_quantize(e, dom_bf, codes):
+            dom_codes.setdefault(e, codes)
+            nc.vector.quantize_mx(codes[:].bitcast(E5M2), dom_plane[:, e * P : (e + 1) * P], dom_bf)
+
+        pieces = (slice(0, HALF // 2), slice(HALF // 2, HALF))
+
+        def exps(h):
+            p_rows = keep.tile([P, PACK, HALF], F32, name=f"p_rows{h}", align_bytes=64)
             for j in range(PACK):
-                width = HALF // last_pieces if j == PACK - 1 else HALF
-                for first in range(0, HALF, width):
-                    nc.scalar.activation(
-                        p_rows[:, j, first : first + width],
-                        scores[j][:, h * HALF + first : h * HALF + first + width],
-                        ACT.Exp,
-                        bias=neg_lse[:, j : j + 1],
-                    )
+                for piece in pieces if j == PACK - 1 else (slice(0, HALF),):
+                    nc.scalar.activation(p_rows[:, j, piece], scores[j][h][:, piece], ACT.Exp, bias=neg_lse[:, j : j + 1])
             return p_rows
 
-        def weights_quantize(h, pw_bf, first, last):
-            cols = slice((h + 1) * HALF + first, (h + 1) * HALF + last)
-            nc.vector.quantize_mx(pw_codes[:, cols].bitcast(E4M3), pw_plane[:, cols], pw_bf[:, PACK * first : PACK * last])
+        def weights_quantize(h, pw_bf, piece):
+            cols = slice(h * HALF + piece.start, h * HALF + piece.stop)
+            nc.vector.quantize_mx(
+                pw_codes[:, cols].bitcast(E4M3), pw_plane[:, cols], pw_bf[:, PACK * piece.start : PACK * piece.stop]
+            )
 
-        def first_weights():
-            p_rows = exps(0, "p_rows0", 2)
-            pw_rows = turns.tile([P, PACK, HALF], BF16, name="pw_rows0", offset=PACK * HALF, align_bytes=64)
-            pieces = (slice(0, HALF // 2), slice(HALF // 2, HALF))
+        def first_weights(p_rows):
+            pw_rows = turns.tile([P, PACK, HALF], BF16, name="pw_rows0", offset=1024, align_bytes=64)
             for j in range(PACK - 1):
                 nc.vector.tensor_scalar(pw_rows[:, j, :], p_rows[:, j, :], rw_sb[:, j : j + 1], None, MULT)
             for piece in pieces:
                 nc.vector.tensor_scalar(pw_rows[:, PACK - 1, piece], p_rows[:, PACK - 1, piece], rw_sb[:, PACK - 1 :], None, MULT)
-            pw_bf = keep.tile([P, PACK * HALF], BF16, name="pw_bf0", align_bytes=64)
+            pw_bf = keep.tile([P, PACK * HALF], BF16, name="pw_bf0", tag="pw_bf0", align_bytes=64)
             for piece in pieces:
                 nc.vector.tensor_copy(
                     pw_bf[:, PACK * piece.start : PACK * piece.stop].rearrange("p (c i j) -> p c j i", j=PACK, i=4),
                     pw_rows[:, :, piece].rearrange("p j (c i) -> p c j i", i=4),
                 )
             for piece in pieces:
-                weights_quantize(0, pw_bf, piece.start, piece.stop)
+                weights_quantize(0, pw_bf, piece)
 
-        def second_weights():
-            p_rows = exps(1, "k_codes", 2)
-            pw_bf = turns.tile([P, PACK * HALF], BF16, name="pw_bf1", offset=PACK * HALF, align_bytes=64)
-            dst = pw_bf[:].rearrange("p (c i j) -> p c j i", j=PACK, i=4)
-            groups = PW_ON_VECTOR // 4
-            for first, last in ((0, HALF // 8), (HALF // 8, groups)):
+        def second_weights(p_rows):
+            pw_bf = turns.tile([P, PACK * HALF], BF16, name="pw_bf1", offset=1024, align_bytes=64)
+            for piece in pieces:
                 nc.vector.tensor_tensor(
-                    dst[:, first:last],
-                    p_rows[:].rearrange("p j (c i) -> p c j i", i=4)[:, first:last],
-                    rw_sb[:].unsqueeze(1).unsqueeze(3).to_broadcast([P, last - first, PACK, 4]),
+                    pw_bf[:, PACK * piece.start : PACK * piece.stop].rearrange("p (c i j) -> p c j i", j=PACK, i=4),
+                    p_rows[:, :, piece].rearrange("p j (c i) -> p c j i", i=4),
+                    rw_sb[:].unsqueeze(1).unsqueeze(3).to_broadcast([P, HALF // 8, PACK, 4]),
                     MULT,
                 )
-            pw_rows = keep.tile([P, PACK, HALF - PW_ON_VECTOR], BF16, name="pw_rows1", tag="pw_rows", align_bytes=64)
-            for j in range(PACK):
-                nc.scalar.activation(pw_rows[:, j, :], p_rows[:, j, PW_ON_VECTOR:], ACT.Copy, scale=rw_sb[:, j : j + 1])
-            nc.scalar.copy(dst[:, groups:], pw_rows[:].rearrange("p j (c i) -> p c j i", i=4))
-            weights_quantize(1, pw_bf, 0, HALF // 2)
-            weights_quantize(1, pw_bf, HALF // 2, HALF)
+            for piece in pieces:
+                weights_quantize(1, pw_bf, piece)
 
-        def product(e, first, bank):
-            grad = psum.tile([P, N], F32, name=f"grad{e}_{first}", tag=bank)
+        def product(grad, e, slots):
             nc.tensor.matmul_mx(
-                grad[:],
-                lhsT=dom_codes[:, e * P : (e + 1) * P].bitcast(E5M2),
+                grad,
+                lhsT=dom_codes[e][:].bitcast(E5M2),
                 lhsT_scale=dom_plane[:, e * P : (e + 1) * P],
-                rhs=pw_codes[:, first : first + N].bitcast(E4M3),
-                rhs_scale=pw_plane[:, first : first + N],
+                rhs=pw_codes[:, slots].bitcast(E4M3),
+                rhs_scale=pw_plane[:, slots],
                 start=True,
                 stop=True,
             )
-            return grad
 
-        def scatter(e, grad, slots, tag):
-            width = slots.stop - slots.start
-            grad_sb = keep.tile([P, width], F32, name=f"grad_sb{e}_{slots.start}_{width}", tag=tag, align_bytes=64)
-            nc.scalar.copy(grad_sb[:], grad[:, N - width :])
-            window = windows[WINDOW_OF[e]]
-            nc.vector.tensor_copy(window[:].indirect(offsets[:, slots.start // 16 : slots.stop // 16]), grad_sb[:])
+        def places(e, slots):
+            return windows[WINDOW_OF[e]][:].indirect(offsets[:, slots.start // 16 : slots.stop // 16])
 
-        dom_early = turns.tile([P, 2 * PACK * P], BF16, name="dom_early", offset=PACK * HALF, align_bytes=64)
-        dom_prepare(0, 2, nc.vector.tensor_copy, 2, 2, dom_early)
-        first_weights()
-        early = product(0, 0, "early")
-        second_weights()
-        scatter(0, early, slice(0, HALF), "pw_rows")
-
-        def finish(e, slots, bank):
-            scatter(e, product(e, HALF, bank), slots, f"grad_w{e}")
+        def store(e):
             nc.sync.dma_start(out[e * P : (e + 1) * P, :], windows[WINDOW_OF[e]][:])
 
-        dom_third = turns.tile([P, PACK * P], BF16, name="dom_third", offset=PACK * HALF, align_bytes=64)
-        dom_prepare(2, 3, nc.scalar.copy, 1, 1, dom_third)
-        finish(1, slice(0, N), "grad1")
-        finish(0, slice(HALF, N), "grad0")
-        dom_last = keep.tile([P, PACK * P], BF16, name="dom_last", tag="pw_rows", align_bytes=64)
-        dom_prepare(3, 4, nc.scalar.copy, 1, 1, dom_last)
-        finish(2, slice(0, N), "grad2")
-        finish(3, slice(0, N), "early")
+        halves = (slice(0, HALF), slice(HALF, N))
+        whole = slice(0, N)
+
+        dom_early = turns.tile([P, 2 * PACK * P], BF16, name="dom_early", offset=1024, align_bytes=64)
+        for e in range(2):
+            dom_interleave(e, nc.vector.tensor_copy, dom_early[:, e * PACK * P : (e + 1) * PACK * P])
+        for e in range(2):
+            codes = keep.tile([P, P], U32, name=f"dom_codes{e}", align_bytes=64)
+            dom_quantize(e, dom_early[:, e * PACK * P : (e + 1) * PACK * P], codes)
+        p_first = exps(0)
+        p_second = exps(1)
+        first_weights(p_first)
+        grad00 = psum.tile([P, HALF], F32, name="grad00", tag="bank00")
+        product(grad00[:], 0, halves[0])
+        grad10 = psum.tile([P, HALF], F32, name="grad10", tag="bank10")
+        product(grad10[:], 1, halves[0])
+        second_weights(p_second)
+        dom_late = keep.tile([P, 2 * PACK * P], BF16, name="dom_late", tag="q_bf11", align_bytes=64)
+        nc.scalar.copy(
+            dom_late[:].rearrange("p (c i j) -> p c j i", i=4, j=PACK), dom_raw[1][:].rearrange("p j (c i) -> p c j i", i=4)
+        )
+        grad00_sb = keep.tile([P, HALF], F32, name="grad00_sb", align_bytes=64)
+        nc.scalar.copy(grad00_sb[:], grad00[:])
+        nc.scalar.activation(places(0, halves[0]), grad00_sb[:], ACT.Copy)
+
+        codes2 = turns.tile([P, P], U32, name="dom_codes2", offset=2560, align_bytes=64)
+        dom_quantize(2, dom_late[:, : PACK * P], codes2)
+        codes3 = turns.tile([P, P], U32, name="dom_codes3", offset=1024, align_bytes=64)
+        dom_quantize(3, dom_late[:, PACK * P :], codes3)
+        grad10_sb = turns.tile([P, HALF], F32, name="grad10_sb", offset=1536, align_bytes=64)
+        nc.vector.tensor_copy(grad10_sb[:], grad10[:])
+        nc.scalar.activation(places(1, halves[0]), grad10_sb[:], ACT.Copy)
+        windows.append(keep.tile([P, T], F32, name="window3", tag="q_bf11", align_bytes=64))
+        nc.gpsimd.memset(windows[3][:].bitcast(I32), 0)
+
+        def half_product(e, h, bank):
+            grad = psum.tile([P, HALF], F32, name=f"grad{e}{h}", tag=bank)
+            product(grad[:], e, halves[h])
+            return grad
+
+        grad01 = half_product(0, 1, "bank01")
+        grad11 = half_product(1, 1, "bank11")
+        grad20 = half_product(2, 0, "bank10")
+        grad21 = half_product(2, 1, "bank21")
+        grad30 = half_product(3, 0, "bank30")
+
+        grad01_sb = keep.tile([P, HALF], F32, name="grad01_sb", align_bytes=64)
+        nc.vector.tensor_copy(grad01_sb[:], grad01[:])
+        grad11_sb = keep.tile([P, HALF], F32, name="grad11_sb", align_bytes=64)
+        nc.vector.tensor_copy(grad11_sb[:], grad11[:])
+        nc.vector.tensor_copy(places(0, halves[1]), grad01_sb[:])
+        store(0)
+        grad2_sb = keep.tile([P, N], F32, name="grad2_sb", align_bytes=64)
+        nc.scalar.copy(grad2_sb[:, halves[0]], grad20[:])
+        nc.scalar.activation(places(1, halves[1]), grad11_sb[:], ACT.Copy)
+        store(1)
+
+        nc.vector.tensor_copy(grad2_sb[:, halves[1]], grad21[:])
+        grad3_sb = keep.tile([P, N], F32, name="grad3_sb", align_bytes=64)
+        nc.vector.tensor_copy(grad3_sb[:, halves[0]], grad30[:])
+        nc.vector.tensor_copy(places(2, whole), grad2_sb[:])
+        store(2)
+
+        grad31 = half_product(3, 1, "bank11")
+        nc.scalar.copy(grad3_sb[:, halves[1]], grad31[:])
+        for slots in halves:
+            nc.scalar.activation(places(3, slots), grad3_sb[:, slots], ACT.Copy)
+        store(3)

@@ -219,8 +219,8 @@ def tile_attend_gat_lse_v_kernel(tc, qT, k_words, k_scales, lse, rw, dom, offs, 
         def places(e, slots):
             return windows[WINDOW_OF[e]][:].indirect(offsets[:, slots.start // 16 : slots.stop // 16])
 
-        def store(e):
-            nc.sync.dma_start(out[e * P : (e + 1) * P, :], windows[WINDOW_OF[e]][:])
+        def store(e, queue):
+            queue.dma_start(out[e * P : (e + 1) * P, :], windows[WINDOW_OF[e]][:])
 
         halves = (slice(0, HALF), slice(HALF, N))
         whole = slice(0, N)
@@ -273,20 +273,20 @@ def tile_attend_gat_lse_v_kernel(tc, qT, k_words, k_scales, lse, rw, dom, offs, 
         grad11_sb = keep.tile([P, HALF], F32, name="grad11_sb", align_bytes=64)
         nc.vector.tensor_copy(grad11_sb[:], grad11[:])
         nc.vector.tensor_copy(places(0, halves[1]), grad01_sb[:])
-        store(0)
+        store(0, nc.sync)
         grad2_sb = keep.tile([P, N], F32, name="grad2_sb", align_bytes=64)
         nc.scalar.copy(grad2_sb[:, halves[0]], grad20[:])
         nc.scalar.activation(places(1, halves[1]), grad11_sb[:], ACT.Copy)
-        store(1)
+        store(1, nc.scalar)
 
         nc.vector.tensor_copy(grad2_sb[:, halves[1]], grad21[:])
         grad3_sb = keep.tile([P, N], F32, name="grad3_sb", align_bytes=64)
         nc.vector.tensor_copy(grad3_sb[:, halves[0]], grad30[:])
         nc.vector.tensor_copy(places(2, whole), grad2_sb[:])
-        store(2)
+        store(2, nc.sync)
 
         grad31 = half_product(3, 1, "bank11")
         nc.scalar.copy(grad3_sb[:, halves[1]], grad31[:])
         for slots in halves:
             nc.scalar.activation(places(3, slots), grad3_sb[:, slots], ACT.Copy)
-        store(3)
+        store(3, nc.scalar)

@@ -22,8 +22,11 @@ PACK = 4
 PASSES = D // (P * PACK)
 E_TILES = DV // P
 HALF = N // 2
-WINDOWS = 3
+WINDOWS = 2
 WINDOW_OF = (0, 1, 2, 3)
+SEAM = 4 * T - 1024
+Q_BF_AT = ((0, 2048), (4096, SEAM))
+HEAD = 8192
 Q_CUT = PACK * R - R // 2
 
 
@@ -32,12 +35,13 @@ def tile_attend_gat_lse_v_kernel(tc, qT, k_words, k_scales, lse, rw, dom, offs, 
     with ExitStack() as ctx:
         keep = ctx.enter_context(tc.tile_pool(name="keep", bufs=1))
         turns = ctx.enter_context(tc.tile_pool(name="turns", bufs=1))
+        late = ctx.enter_context(tc.tile_pool(name="late", bufs=1))
         psum = ctx.enter_context(tc.psum_pool(name="psum", bufs=1))
 
         offsets = keep.tile([P, N // 16], U16, name="offsets")
-        scale_pool = keep.tile([P, T], U8, name="scale_pool", tag="scale_pool", align_bytes=64)
+        scale_pool = turns.tile([P, T], U8, name="scale_pool", offset=HEAD, align_bytes=64)
         word_pool = keep.tile([P, T], U32, name="word_pool", tag="word_pool", align_bytes=64)
-        k_plane = keep.tile([P, N], U8, name="k_plane", align_bytes=64)
+        k_planes = [keep.tile([P, N], U8, name=f"k_plane{o}", align_bytes=64) for o in range(PASSES)]
         neg_lse = keep.tile([P, PACK], F32, name="neg_lse")
         windows = [keep.tile([P, T], F32, name=f"window{w}", align_bytes=64) for w in range(WINDOWS)]
         pw_codes = keep.tile([P, N], U32, name="pw_codes", align_bytes=64)
@@ -46,36 +50,40 @@ def tile_attend_gat_lse_v_kernel(tc, qT, k_words, k_scales, lse, rw, dom, offs, 
         nc.vector.memset(scale_pool[:].bitcast(I32), 0)
 
         q_rows = qT[0].rearrange("(o p t) r -> o p (t r)", o=PASSES, t=PACK)
-        q_raw = [keep.tile([P, PACK * R], F32, name=f"q_raw{o}", align_bytes=64) for o in range(PASSES)]
+        q_raw = [keep.tile([P, PACK * R], F32, name="q_raw0", align_bytes=64)]
 
         nc.sync.dma_start(offsets[:], offs)
         words = k_words[0].rearrange("p t b -> p (t b)").bitcast(I32)
-        nc.sync.dma_start(word_pool[:, : T // 2].bitcast(I32), words[:, : T // 2])
-        scale_rows = k_scales.bitcast(I32)
-        for i in range(4):
-            nc.sync.dma_start(scale_pool[i:P:32, :].bitcast(I32), scale_rows[0].rearrange("(g i) t -> i g t", i=4)[i])
-        nc.sync.dma_start(scale_pool[4:P:8, :].bitcast(I32), scale_rows[1])
-        nc.sync.dma_start(word_pool[:, T // 2 :].bitcast(I32), words[:, T // 2 :])
-        nc.sync.dma_start(q_raw[0][:, :Q_CUT], q_rows[0][:, :Q_CUT])
-        nc.sync.dma_start(q_raw[0][:, Q_CUT:], q_rows[0][:, Q_CUT:])
+        nc.sync.dma_start(word_pool[:, : T // 4].bitcast(I32), words[:, : T // 4])
+        scale_rows = k_scales.bitcast(I32).rearrange("o f t -> (o f) t")
+        nc.sync.dma_start(scale_pool[0:P:4, :].bitcast(I32), scale_rows)
+        nc.sync.dma_start(word_pool[:, T // 4 :].bitcast(I32), words[:, T // 4 :])
         lse_sb = keep.tile([P, PACK], F32, name="lse_sb")
         rw_sb = keep.tile([P, PACK], F32, name="rw_sb")
         nc.sync.dma_start(lse_sb[:], lse[0].rearrange("(p j) one -> p (j one)", j=PACK))
         nc.sync.dma_start(rw_sb[:], rw[0].rearrange("(p j) one -> p (j one)", j=PACK))
-        nc.sync.dma_start(q_raw[1][:, :Q_CUT], q_rows[1][:, :Q_CUT])
-        nc.sync.dma_start(q_raw[1][:, Q_CUT:], q_rows[1][:, Q_CUT:])
+        nc.sync.dma_start(q_raw[0][:], q_rows[0])
 
-        nc.vector.memset(k_plane[:].bitcast(I32), 0)
+        for k_plane in k_planes:
+            nc.vector.memset(k_plane[:].bitcast(I32), 0)
         for window in windows:
             nc.vector.memset(window[:].bitcast(I32), 0)
 
         scale_picked = keep.tile([P, N], U8, name="scale_picked", align_bytes=64)
         nc.vector.tensor_copy(scale_picked[:], scale_pool[:].indirect(offsets[:]))
-        for i in range(4):
-            nc.sync.dma_start(k_plane[i:P:32, :].bitcast(I32), scale_picked[8 * i + 4 : P : 32, :].bitcast(I32))
-        k_planes = [scale_picked, k_plane]
+
+        def plane_moves(o):
+            for i in range(4):
+                first = 64 * o + 4 * i
+                nc.sync.dma_start(k_planes[o][i:P:32, :].bitcast(I32), scale_picked[first : first + 49 : 16, :].bitcast(I32))
+
+        plane_moves(0)
+        q_raw.append(turns.tile([P, PACK * R], F32, name="q_raw1", offset=HEAD + 1024, align_bytes=64))
+        nc.sync.dma_start(q_raw[1][:, :Q_CUT], q_rows[1][:, :Q_CUT])
+        nc.sync.dma_start(q_raw[1][:, Q_CUT:], q_rows[1][:, Q_CUT:])
+        plane_moves(1)
         dom_raw = [
-            keep.tile([P, PACK, DV // 2], F32, name="dom_raw0", tag="scale_pool", align_bytes=64),
+            turns.tile([P, PACK, DV // 2], F32, name="dom_raw0", offset=HEAD - 3072, align_bytes=64),
             keep.tile([P, PACK, DV // 2], F32, name="dom_raw1", tag="word_pool", align_bytes=64),
         ]
         dom_rows = dom[0].rearrange("(p j) (h e) -> h p j e", j=PACK, h=2)
@@ -93,7 +101,8 @@ def tile_attend_gat_lse_v_kernel(tc, qT, k_words, k_scales, lse, rw, dom, offs, 
         q_plane = [keep.tile([P, R], U8, name=f"q_plane{o}", align_bytes=64) for o in range(PASSES)]
 
         q_bf = [
-            [keep.tile([P, 2 * R], BF16, name=f"q_bf{o}{u}", tag=f"q_bf{o}{u}", align_bytes=64) for u in range(2)] for o in range(PASSES)
+            [late.tile([P, 2 * R], BF16, name=f"q_bf{o}{u}", offset=Q_BF_AT[o][u], align_bytes=64) for u in range(2)]
+            for o in range(PASSES)
         ]
 
         def q_interleave(o, h, u, engine_copy):
@@ -144,7 +153,7 @@ def tile_attend_gat_lse_v_kernel(tc, qT, k_words, k_scales, lse, rw, dom, offs, 
             score_pass(1, j, 0, k_codes1[:])
         for j in range(PACK):
             score_pass(0, j, 1, k_codes0[:, HALF:])
-        k_codes_last = keep.tile([P, HALF], U16, name="k_codes_last", tag="q_bf11", align_bytes=64)
+        k_codes_last = late.tile([P, HALF], U16, name="k_codes_last", offset=SEAM, align_bytes=64)
         nc.vector.tensor_copy(k_codes_last[:], word_halves[:, 1, HALF:])
         for j in range(PACK):
             score_pass(1, j, 1, k_codes_last[:])
@@ -239,7 +248,7 @@ def tile_attend_gat_lse_v_kernel(tc, qT, k_words, k_scales, lse, rw, dom, offs, 
         grad10 = psum.tile([P, HALF], F32, name="grad10", tag="bank10")
         product(grad10[:], 1, halves[0])
         second_weights(p_second)
-        dom_late = keep.tile([P, 2 * PACK * P], BF16, name="dom_late", tag="q_bf11", align_bytes=64)
+        dom_late = late.tile([P, 2 * PACK * P], BF16, name="dom_late", offset=SEAM, align_bytes=64)
         nc.scalar.copy(
             dom_late[:].rearrange("p (c i j) -> p c j i", i=4, j=PACK), dom_raw[1][:].rearrange("p j (c i) -> p c j i", i=4)
         )
@@ -254,8 +263,9 @@ def tile_attend_gat_lse_v_kernel(tc, qT, k_words, k_scales, lse, rw, dom, offs, 
         grad10_sb = turns.tile([P, HALF], F32, name="grad10_sb", offset=1536, align_bytes=64)
         nc.vector.tensor_copy(grad10_sb[:], grad10[:])
         nc.scalar.activation(places(1, halves[0]), grad10_sb[:], ACT.Copy)
-        windows.append(keep.tile([P, T], F32, name="window3", tag="q_bf11", align_bytes=64))
-        nc.gpsimd.memset(windows[3][:].bitcast(I32), 0)
+        for w in range(WINDOWS, E_TILES):
+            windows.append(late.tile([P, T], F32, name=f"window{w}", offset=(w - WINDOWS) * 4 * T, align_bytes=64))
+            nc.gpsimd.memset(windows[w][:].bitcast(I32), 0)
 
         def half_product(e, h, bank):
             grad = psum.tile([P, HALF], F32, name=f"grad{e}{h}", tag=bank)

@@ -20,14 +20,11 @@ MULT = mybir.AluOpType.mult
 P = 128
 PACK = 4
 PASSES = D // (P * PACK)
-E_TILES = DV // P
 HALF = N // 2
-WINDOWS = 2
-WINDOW_OF = (0, 1, 2, 3)
-SEAM = 4 * T - 1024
-Q_BF_AT = ((0, 2048), (4096, SEAM))
-HEAD = 8192
+PIECES = (slice(0, HALF // 2), slice(HALF // 2, HALF))
+SCALE_ROW0 = P - 16 * PASSES
 Q_CUT = PACK * R - R // 2
+KIB = 1024
 
 
 def tile_attend_gat_lse_v_kernel(tc, qT, k_words, k_scales, lse, rw, dom, offs, out):
@@ -39,69 +36,64 @@ def tile_attend_gat_lse_v_kernel(tc, qT, k_words, k_scales, lse, rw, dom, offs, 
         psum = ctx.enter_context(tc.psum_pool(name="psum", bufs=1))
 
         offsets = keep.tile([P, N // 16], U16, name="offsets")
-        scale_pool = turns.tile([P, T], U8, name="scale_pool", offset=HEAD, align_bytes=64)
+        scale_pool = turns.tile([P, T], U8, name="scale_pool", offset=8 * KIB, align_bytes=64)
         word_pool = keep.tile([P, T], U32, name="word_pool", tag="word_pool", align_bytes=64)
         k_planes = [keep.tile([P, N], U8, name=f"k_plane{o}", align_bytes=64) for o in range(PASSES)]
+        windows = [keep.tile([P, T], F32, name=f"window{w}", align_bytes=64) for w in range(3)]
+        lse_sb = keep.tile([P, PACK], F32, name="lse_sb")
+        rw_sb = keep.tile([P, PACK], F32, name="rw_sb")
         neg_lse = keep.tile([P, PACK], F32, name="neg_lse")
-        windows = [keep.tile([P, T], F32, name=f"window{w}", align_bytes=64) for w in range(WINDOWS)]
-        pw_codes = keep.tile([P, N], U32, name="pw_codes", align_bytes=64)
-        pw_plane = keep.tile([P, N], U8, name="pw_plane", align_bytes=64)
 
-        nc.vector.memset(scale_pool[:].bitcast(I32), 0)
+        nc.gpsimd.memset(scale_pool[:SCALE_ROW0, :].bitcast(I32), 0)
+        for k_plane in k_planes:
+            nc.gpsimd.memset(k_plane[:].bitcast(I32), 0)
+        nc.vector.memset(windows[0][:].bitcast(I32), 0)
+        for window in windows[1:]:
+            nc.gpsimd.memset(window[:].bitcast(I32), 0)
 
         q_rows = qT[0].rearrange("(o p t) r -> o p (t r)", o=PASSES, t=PACK)
         q_raw = [keep.tile([P, PACK * R], F32, name="q_raw0", align_bytes=64)]
-
+        nc.sync.dma_start(scale_pool[SCALE_ROW0:, :].bitcast(I32), k_scales.bitcast(I32).rearrange("o f t -> (o f) t"))
         nc.sync.dma_start(offsets[:], offs)
-        words = k_words[0].rearrange("p t b -> p (t b)").bitcast(I32)
-        nc.sync.dma_start(word_pool[:, : T // 4].bitcast(I32), words[:, : T // 4])
-        scale_rows = k_scales.bitcast(I32).rearrange("o f t -> (o f) t")
-        nc.sync.dma_start(scale_pool[0:P:4, :].bitcast(I32), scale_rows)
-        nc.sync.dma_start(word_pool[:, T // 4 :].bitcast(I32), words[:, T // 4 :])
-        lse_sb = keep.tile([P, PACK], F32, name="lse_sb")
-        rw_sb = keep.tile([P, PACK], F32, name="rw_sb")
+        nc.sync.dma_start(word_pool[:].bitcast(I32), k_words[0].rearrange("p t b -> p (t b)").bitcast(I32))
         nc.sync.dma_start(lse_sb[:], lse[0].rearrange("(p j) one -> p (j one)", j=PACK))
         nc.sync.dma_start(rw_sb[:], rw[0].rearrange("(p j) one -> p (j one)", j=PACK))
         nc.sync.dma_start(q_raw[0][:], q_rows[0])
-
-        for k_plane in k_planes:
-            nc.vector.memset(k_plane[:].bitcast(I32), 0)
-        for window in windows:
-            nc.vector.memset(window[:].bitcast(I32), 0)
 
         scale_picked = keep.tile([P, N], U8, name="scale_picked", align_bytes=64)
         nc.vector.tensor_copy(scale_picked[:], scale_pool[:].indirect(offsets[:]))
 
         def plane_moves(o):
             for i in range(4):
-                first = 64 * o + 4 * i
-                nc.sync.dma_start(k_planes[o][i:P:32, :].bitcast(I32), scale_picked[first : first + 49 : 16, :].bitcast(I32))
+                first = SCALE_ROW0 + 16 * o + i
+                nc.sync.dma_start(k_planes[o][i:P:32, :].bitcast(I32), scale_picked[first : first + 13 : 4, :].bitcast(I32))
 
         plane_moves(0)
-        q_raw.append(turns.tile([P, PACK * R], F32, name="q_raw1", offset=HEAD + 1024, align_bytes=64))
+        q_raw.append(turns.tile([P, PACK * R], F32, name="q_raw1", offset=9 * KIB, align_bytes=64))
         nc.sync.dma_start(q_raw[1][:, :Q_CUT], q_rows[1][:, :Q_CUT])
         nc.sync.dma_start(q_raw[1][:, Q_CUT:], q_rows[1][:, Q_CUT:])
         plane_moves(1)
         dom_raw = [
-            turns.tile([P, PACK, DV // 2], F32, name="dom_raw0", offset=HEAD - 3072, align_bytes=64),
+            turns.tile([P, PACK, DV // 2], F32, name="dom_raw0", offset=5 * KIB, align_bytes=64),
             keep.tile([P, PACK, DV // 2], F32, name="dom_raw1", tag="word_pool", align_bytes=64),
         ]
         dom_rows = dom[0].rearrange("(p j) (h e) -> h p j e", j=PACK, h=2)
         nc.sync.dma_start(dom_raw[0][:], dom_rows[0])
 
-        word_picked = keep.tile([P, N], U32, name="word_picked", tag="word_picked", align_bytes=64)
-        k_codes0 = keep.tile([P, N], U16, name="k_codes0", align_bytes=64)
-        k_codes1 = keep.tile([P, HALF], U16, name="k_codes1", align_bytes=64)
+        word_picked = keep.tile([P, N], U32, name="word_picked", align_bytes=64)
         nc.vector.tensor_copy(word_picked[:], word_pool[:].indirect(offsets[:]))
         nc.sync.dma_start(dom_raw[1][:], dom_rows[1])
         word_halves = word_picked[:].bitcast(U16).rearrange("p (n o) -> p o n", o=PASSES)
+        k_codes0 = keep.tile([P, N], U16, name="k_codes0", align_bytes=64)
+        k_codes1 = keep.tile([P, HALF], U16, name="k_codes1", align_bytes=64)
         nc.vector.tensor_copy(k_codes0[:], word_halves[:, 0, :])
+        nc.vector.tensor_copy(k_codes1[:], word_halves[:, 1, :HALF])
+        nc.scalar.activation(neg_lse[:], lse_sb[:], ACT.Copy, scale=-1.0)
 
         q_codes = [keep.tile([P, R], U32, name=f"q_codes{o}", align_bytes=64) for o in range(PASSES)]
         q_plane = [keep.tile([P, R], U8, name=f"q_plane{o}", align_bytes=64) for o in range(PASSES)]
-
         q_bf = [
-            [late.tile([P, 2 * R], BF16, name=f"q_bf{o}{u}", offset=Q_BF_AT[o][u], align_bytes=64) for u in range(2)]
+            [late.tile([P, 2 * R], BF16, name=f"q_bf{o}{u}", offset=(4 * o + 2 * u) * KIB, align_bytes=64) for u in range(2)]
             for o in range(PASSES)
         ]
 
@@ -110,13 +102,10 @@ def tile_attend_gat_lse_v_kernel(tc, qT, k_words, k_scales, lse, rw, dom, offs, 
             dst = q_bf[o][u][:].rearrange("p (v h s t) -> p h s t v", t=PACK, v=2, h=2)[:, h]
             engine_copy(dst, src)
 
-        def q_quantize(o, first, last):
-            cols = slice(first * P, last * P)
-            u = first // 2
+        def q_quantize(o, j):
+            cols = slice(j * P, (j + 1) * P)
             nc.vector.quantize_mx(
-                q_codes[o][:, cols].bitcast(E4M3),
-                q_plane[o][:, cols],
-                q_bf[o][u][:, (first - 2 * u) * R : (last - 2 * u) * R],
+                q_codes[o][:, cols].bitcast(E4M3), q_plane[o][:, cols], q_bf[o][j // 2][:, (j % 2) * R : (j % 2 + 1) * R]
             )
 
         scores = [[psum.tile([P, HALF], F32, name=f"scores{j}{h}", tag=f"bank{j}{h}") for h in range(2)] for j in range(PACK)]
@@ -133,88 +122,64 @@ def tile_attend_gat_lse_v_kernel(tc, qT, k_words, k_scales, lse, rw, dom, offs, 
                 stop=(o == PASSES - 1),
             )
 
-        q_interleave(0, 0, 0, nc.scalar.copy)
-        q_interleave(0, 1, 0, nc.vector.tensor_copy)
-        for h in range(2):
-            q_interleave(0, h, 1, nc.scalar.copy)
-        q_quantize(0, 0, 1)
-        q_quantize(0, 1, 2)
-        q_quantize(0, 2, PACK)
+        q_interleave(0, 0, 0, nc.vector.tensor_copy)
+        q_interleave(0, 1, 0, nc.scalar.copy)
+        q_interleave(0, 0, 1, nc.vector.tensor_copy)
+        q_interleave(0, 1, 1, nc.scalar.copy)
         for j in range(PACK):
-            score_pass(0, j, 0, k_codes0[:, :HALF])
-        nc.vector.tensor_copy(k_codes1[:], word_halves[:, 1, :HALF])
+            q_quantize(0, j)
+        for j in range(PACK):
+            for h in range(2):
+                score_pass(0, j, h, k_codes0[:, h * HALF : (h + 1) * HALF])
         for h in range(2):
             q_interleave(1, h, 0, nc.vector.tensor_copy)
             q_interleave(1, h, 1, nc.scalar.copy)
-        nc.scalar.activation(neg_lse[:], lse_sb[:], ACT.Copy, scale=-1.0)
         for j in range(PACK):
-            q_quantize(1, j, j + 1)
+            q_quantize(1, j)
         for j in range(PACK):
             score_pass(1, j, 0, k_codes1[:])
-        for j in range(PACK):
-            score_pass(0, j, 1, k_codes0[:, HALF:])
-        k_codes_last = late.tile([P, HALF], U16, name="k_codes_last", offset=SEAM, align_bytes=64)
+        k_codes_last = late.tile([P, HALF], U16, name="k_codes_last", offset=6 * KIB, align_bytes=64)
         nc.vector.tensor_copy(k_codes_last[:], word_halves[:, 1, HALF:])
         for j in range(PACK):
             score_pass(1, j, 1, k_codes_last[:])
 
-        dom_codes = {}
+        dom_codes = [keep.tile([P, P], U32, name=f"dom_codes{e}", align_bytes=64) for e in range(DV // P)]
         dom_plane = keep.tile([P, DV], U8, name="dom_plane", align_bytes=64)
 
         def dom_interleave(e, engine_copy, dom_bf):
-            half = e // 2
-            raw = dom_raw[half][:, :, (e - 2 * half) * P : (e - 2 * half + 1) * P]
-            engine_copy(
-                dom_bf.rearrange("p (c i j) -> p c j i", i=4, j=PACK), raw.rearrange("p j (c i) -> p c j i", i=4)
-            )
+            raw = dom_raw[e // 2][:, :, (e % 2) * P : (e % 2 + 1) * P]
+            engine_copy(dom_bf.rearrange("p (c i j) -> p c j i", i=4, j=PACK), raw.rearrange("p j (c i) -> p c j i", i=4))
 
-        def dom_quantize(e, dom_bf, codes):
-            dom_codes.setdefault(e, codes)
-            nc.vector.quantize_mx(codes[:].bitcast(E5M2), dom_plane[:, e * P : (e + 1) * P], dom_bf)
+        def dom_quantize(e, dom_bf):
+            nc.vector.quantize_mx(dom_codes[e][:].bitcast(E5M2), dom_plane[:, e * P : (e + 1) * P], dom_bf)
 
-        pieces = (slice(0, HALF // 2), slice(HALF // 2, HALF))
+        dom_early = turns.tile([P, 2 * PACK * P], BF16, name="dom_early", offset=KIB, align_bytes=64)
+        dom_interleave(0, nc.vector.tensor_copy, dom_early[:, : PACK * P])
+        dom_quantize(0, dom_early[:, : PACK * P])
 
-        def exps(h):
-            p_rows = keep.tile([P, PACK, HALF], F32, name=f"p_rows{h}", align_bytes=64)
+        p_rows = [
+            keep.tile([P, PACK, HALF], F32, name="p_rows0", align_bytes=64),
+            keep.tile([P, PACK, HALF], F32, name="p_rows1", align_bytes=64),
+        ]
+        for h in range(2):
             for j in range(PACK):
-                for piece in pieces if j == PACK - 1 else (slice(0, HALF),):
-                    nc.scalar.activation(p_rows[:, j, piece], scores[j][h][:, piece], ACT.Exp, bias=neg_lse[:, j : j + 1])
-            return p_rows
+                for piece in PIECES if j == PACK - 1 else (slice(0, HALF),):
+                    nc.scalar.activation(p_rows[h][:, j, piece], scores[j][h][:, piece], ACT.Exp, bias=neg_lse[:, j : j + 1])
 
-        def weights_quantize(h, pw_bf, piece):
-            cols = slice(h * HALF + piece.start, h * HALF + piece.stop)
-            nc.vector.quantize_mx(
-                pw_codes[:, cols].bitcast(E4M3), pw_plane[:, cols], pw_bf[:, PACK * piece.start : PACK * piece.stop]
-            )
+        pw_codes = keep.tile([P, N], U32, name="pw_codes", align_bytes=64)
+        pw_plane = keep.tile([P, N], U8, name="pw_plane", align_bytes=64)
 
-        def first_weights(p_rows):
-            pw_rows = turns.tile([P, PACK, HALF], BF16, name="pw_rows0", offset=1024, align_bytes=64)
-            for j in range(PACK - 1):
-                nc.vector.tensor_scalar(pw_rows[:, j, :], p_rows[:, j, :], rw_sb[:, j : j + 1], None, MULT)
-            for piece in pieces:
-                nc.vector.tensor_scalar(pw_rows[:, PACK - 1, piece], p_rows[:, PACK - 1, piece], rw_sb[:, PACK - 1 :], None, MULT)
-            pw_bf = keep.tile([P, PACK * HALF], BF16, name="pw_bf0", tag="pw_bf0", align_bytes=64)
-            for piece in pieces:
-                nc.vector.tensor_copy(
-                    pw_bf[:, PACK * piece.start : PACK * piece.stop].rearrange("p (c i j) -> p c j i", j=PACK, i=4),
-                    pw_rows[:, :, piece].rearrange("p j (c i) -> p c j i", i=4),
+        def interleaved(pw_bf, piece):
+            return pw_bf[:, PACK * piece.start : PACK * piece.stop].rearrange("p (c i j) -> p c j i", j=PACK, i=4)
+
+        def weights_quantize(h, pw_bf):
+            for piece in PIECES:
+                cols = slice(h * HALF + piece.start, h * HALF + piece.stop)
+                nc.vector.quantize_mx(
+                    pw_codes[:, cols].bitcast(E4M3), pw_plane[:, cols], pw_bf[:, PACK * piece.start : PACK * piece.stop]
                 )
-            for piece in pieces:
-                weights_quantize(0, pw_bf, piece)
 
-        def second_weights(p_rows):
-            pw_bf = turns.tile([P, PACK * HALF], BF16, name="pw_bf1", offset=1024, align_bytes=64)
-            for piece in pieces:
-                nc.vector.tensor_tensor(
-                    pw_bf[:, PACK * piece.start : PACK * piece.stop].rearrange("p (c i j) -> p c j i", j=PACK, i=4),
-                    p_rows[:, :, piece].rearrange("p j (c i) -> p c j i", i=4),
-                    rw_sb[:].unsqueeze(1).unsqueeze(3).to_broadcast([P, HALF // 8, PACK, 4]),
-                    MULT,
-                )
-            for piece in pieces:
-                weights_quantize(1, pw_bf, piece)
-
-        def product(grad, e, slots):
+        def product(e, slots, grad):
             nc.tensor.matmul_mx(
                 grad,
                 lhsT=dom_codes[e][:].bitcast(E5M2),
@@ -225,78 +190,86 @@ def tile_attend_gat_lse_v_kernel(tc, qT, k_words, k_scales, lse, rw, dom, offs, 
                 stop=True,
             )
 
-        def places(e, slots):
-            return windows[WINDOW_OF[e]][:].indirect(offsets[:, slots.start // 16 : slots.stop // 16])
-
-        def store(e, queue):
-            queue.dma_start(out[e * P : (e + 1) * P, :], windows[WINDOW_OF[e]][:])
+        def bank(name, tag, width=HALF):
+            return psum.tile([P, width], F32, name=name, tag=tag)
 
         halves = (slice(0, HALF), slice(HALF, N))
         whole = slice(0, N)
 
-        dom_early = turns.tile([P, 2 * PACK * P], BF16, name="dom_early", offset=1024, align_bytes=64)
-        for e in range(2):
-            dom_interleave(e, nc.vector.tensor_copy, dom_early[:, e * PACK * P : (e + 1) * PACK * P])
-        for e in range(2):
-            codes = keep.tile([P, P], U32, name=f"dom_codes{e}", align_bytes=64)
-            dom_quantize(e, dom_early[:, e * PACK * P : (e + 1) * PACK * P], codes)
-        p_first = exps(0)
-        p_second = exps(1)
-        first_weights(p_first)
-        grad00 = psum.tile([P, HALF], F32, name="grad00", tag="bank00")
-        product(grad00[:], 0, halves[0])
-        grad10 = psum.tile([P, HALF], F32, name="grad10", tag="bank10")
-        product(grad10[:], 1, halves[0])
-        second_weights(p_second)
-        dom_late = late.tile([P, 2 * PACK * P], BF16, name="dom_late", offset=SEAM, align_bytes=64)
-        nc.scalar.copy(
-            dom_late[:].rearrange("p (c i j) -> p c j i", i=4, j=PACK), dom_raw[1][:].rearrange("p j (c i) -> p c j i", i=4)
-        )
-        grad00_sb = keep.tile([P, HALF], F32, name="grad00_sb", align_bytes=64)
-        nc.scalar.copy(grad00_sb[:], grad00[:])
-        nc.scalar.activation(places(0, halves[0]), grad00_sb[:], ACT.Copy)
+        def places(e, slots):
+            return windows[e][:].indirect(offsets[:, slots.start // 16 : slots.stop // 16])
 
-        codes2 = turns.tile([P, P], U32, name="dom_codes2", offset=2560, align_bytes=64)
-        dom_quantize(2, dom_late[:, : PACK * P], codes2)
-        codes3 = turns.tile([P, P], U32, name="dom_codes3", offset=1024, align_bytes=64)
-        dom_quantize(3, dom_late[:, PACK * P :], codes3)
-        grad10_sb = turns.tile([P, HALF], F32, name="grad10_sb", offset=1536, align_bytes=64)
+        def leave_bank(name, grad, engine_copy):
+            grad_sb = keep.tile(list(grad.shape), F32, name=name, align_bytes=64)
+            engine_copy(grad_sb[:], grad[:])
+            return grad_sb
+
+        def scalar_scatter(e, slots, grad_sb):
+            nc.scalar.activation(places(e, slots), grad_sb[:], ACT.Copy)
+
+        def vector_scatter(e, slots, grad_sb):
+            nc.vector.tensor_copy(places(e, slots), grad_sb[:])
+
+        def store(e, queue):
+            queue.dma_start(out[e * P : (e + 1) * P, :], windows[e][:])
+
+        pw_rows = late.tile([P, PACK, HALF], BF16, name="pw_rows0", offset=13 * KIB, align_bytes=64)
+        for j in range(PACK):
+            for piece in PIECES if j == PACK - 1 else (slice(0, HALF),):
+                nc.vector.tensor_scalar(pw_rows[:, j, piece], p_rows[0][:, j, piece], rw_sb[:, j : j + 1], None, MULT)
+        pw_bf0 = late.tile([P, PACK * HALF], BF16, name="pw_bf0", offset=10 * KIB, align_bytes=64)
+        for piece in PIECES:
+            nc.vector.tensor_copy(interleaved(pw_bf0, piece), pw_rows[:, :, piece].rearrange("p j (c i) -> p c j i", i=4))
+        weights_quantize(0, pw_bf0)
+        dom_interleave(1, nc.vector.tensor_copy, dom_early[:, PACK * P :])
+        dom_quantize(1, dom_early[:, PACK * P :])
+        grad00 = bank("grad00", "bank00")
+        product(0, halves[0], grad00[:])
+        grad10 = bank("grad10", "bank10")
+        product(1, halves[0], grad10[:])
+
+        pw_bf1 = late.tile([P, PACK * HALF], BF16, name="pw_bf1", offset=13 * KIB, align_bytes=64)
+        for piece in PIECES:
+            nc.vector.tensor_tensor(
+                interleaved(pw_bf1, piece),
+                p_rows[1][:, :, piece].rearrange("p j (c i) -> p c j i", i=4),
+                rw_sb[:].unsqueeze(1).unsqueeze(3).to_broadcast([P, HALF // 8, PACK, 4]),
+                MULT,
+            )
+        weights_quantize(1, pw_bf1)
+        grad01 = bank("grad01", "bank01")
+        product(0, halves[1], grad01[:])
+
+        dom_bf2 = late.tile([P, PACK * P], BF16, name="dom_bf2", offset=6 * KIB, align_bytes=64)
+        dom_interleave(2, nc.scalar.copy, dom_bf2[:])
+        scalar_scatter(0, halves[0], leave_bank("grad00_sb", grad00, nc.scalar.copy))
+
+        dom_bf3 = late.tile([P, PACK * P], BF16, name="dom_bf3", offset=10 * KIB, align_bytes=64)
+        dom_interleave(3, nc.vector.tensor_copy, dom_bf3[:])
+        dom_quantize(2, dom_bf2[:])
+        dom_quantize(3, dom_bf3[:])
+        windows.append(late.tile([P, T], F32, name="window3", offset=6 * KIB, align_bytes=64))
+        nc.gpsimd.memset(windows[3][:].bitcast(I32), 0)
+
+        grad11 = bank("grad11", "bank11")
+        product(1, halves[1], grad11[:])
+        grad30 = bank("grad30", "bank30")
+        product(3, halves[0], grad30[:])
+        grad10_sb = late.tile([P, HALF], F32, name="grad10_sb", offset=14 * KIB, align_bytes=64)
         nc.vector.tensor_copy(grad10_sb[:], grad10[:])
-        nc.scalar.activation(places(1, halves[0]), grad10_sb[:], ACT.Copy)
-        for w in range(WINDOWS, E_TILES):
-            windows.append(late.tile([P, T], F32, name=f"window{w}", offset=(w - WINDOWS) * 4 * T, align_bytes=64))
-            nc.gpsimd.memset(windows[w][:].bitcast(I32), 0)
-
-        def half_product(e, h, bank):
-            grad = psum.tile([P, HALF], F32, name=f"grad{e}{h}", tag=bank)
-            product(grad[:], e, halves[h])
-            return grad
-
-        grad01 = half_product(0, 1, "bank01")
-        grad11 = half_product(1, 1, "bank11")
-        grad20 = half_product(2, 0, "bank10")
-        grad21 = half_product(2, 1, "bank21")
-        grad30 = half_product(3, 0, "bank30")
-
-        grad01_sb = keep.tile([P, HALF], F32, name="grad01_sb", align_bytes=64)
-        nc.vector.tensor_copy(grad01_sb[:], grad01[:])
-        grad11_sb = keep.tile([P, HALF], F32, name="grad11_sb", align_bytes=64)
-        nc.vector.tensor_copy(grad11_sb[:], grad11[:])
-        nc.vector.tensor_copy(places(0, halves[1]), grad01_sb[:])
+        scalar_scatter(1, halves[0], grad10_sb)
+        vector_scatter(0, halves[1], leave_bank("grad01_sb", grad01, nc.vector.tensor_copy))
         store(0, nc.sync)
-        grad2_sb = keep.tile([P, N], F32, name="grad2_sb", align_bytes=64)
-        nc.scalar.copy(grad2_sb[:, halves[0]], grad20[:])
-        nc.scalar.activation(places(1, halves[1]), grad11_sb[:], ACT.Copy)
+        grad2 = bank("grad2", "bank01", N)
+        product(2, whole, grad2[:])
+        grad11_sb = leave_bank("grad11_sb", grad11, nc.scalar.copy)
+        grad30_sb = leave_bank("grad30_sb", grad30, nc.scalar.copy)
+        scalar_scatter(1, halves[1], grad11_sb)
         store(1, nc.scalar)
-
-        nc.vector.tensor_copy(grad2_sb[:, halves[1]], grad21[:])
-        grad3_sb = keep.tile([P, N], F32, name="grad3_sb", align_bytes=64)
-        nc.vector.tensor_copy(grad3_sb[:, halves[0]], grad30[:])
-        nc.vector.tensor_copy(places(2, whole), grad2_sb[:])
+        vector_scatter(2, whole, leave_bank("grad2_sb", grad2, nc.vector.tensor_copy))
         store(2, nc.sync)
-
-        grad31 = half_product(3, 1, "bank11")
-        nc.scalar.copy(grad3_sb[:, halves[1]], grad31[:])
-        for slots in halves:
-            nc.scalar.activation(places(3, slots), grad3_sb[:, slots], ACT.Copy)
+        grad31 = bank("grad31", "bank01")
+        product(3, halves[1], grad31[:])
+        scalar_scatter(3, halves[0], grad30_sb)
+        scalar_scatter(3, halves[1], leave_bank("grad31_sb", grad31, nc.scalar.copy))
         store(3, nc.scalar)

@@ -25,6 +25,7 @@ PIECES = (slice(0, HALF // 2), slice(HALF // 2, HALF))
 SCALE_ROW0 = P - 16 * PASSES
 Q_CUT = PACK * R - R // 2
 KIB = 1024
+Q_BF_AT = ((0, 2), (4, 12))
 
 
 def tile_attend_gat_lse_v_kernel(tc, qT, k_words, k_scales, lse, rw, dom, offs, out):
@@ -39,16 +40,15 @@ def tile_attend_gat_lse_v_kernel(tc, qT, k_words, k_scales, lse, rw, dom, offs, 
         scale_pool = turns.tile([P, T], U8, name="scale_pool", offset=8 * KIB, align_bytes=64)
         word_pool = keep.tile([P, T], U32, name="word_pool", tag="word_pool", align_bytes=64)
         k_planes = [keep.tile([P, N], U8, name=f"k_plane{o}", align_bytes=64) for o in range(PASSES)]
-        windows = [keep.tile([P, T], F32, name=f"window{w}", align_bytes=64) for w in range(3)]
+        windows = [keep.tile([P, T], F32, name=f"window{w}", align_bytes=64) for w in range(2)]
         lse_sb = keep.tile([P, PACK], F32, name="lse_sb")
-        rw_sb = keep.tile([P, PACK], F32, name="rw_sb")
+        rw_sb = late.tile([P, PACK], F32, name="rw_sb", offset=17 * KIB, align_bytes=64)
         neg_lse = keep.tile([P, PACK], F32, name="neg_lse")
 
         nc.gpsimd.memset(scale_pool[:SCALE_ROW0, :].bitcast(I32), 0)
         for k_plane in k_planes:
             nc.gpsimd.memset(k_plane[:].bitcast(I32), 0)
-        nc.vector.memset(windows[0][:].bitcast(I32), 0)
-        for window in windows[1:]:
+        for window in windows:
             nc.gpsimd.memset(window[:].bitcast(I32), 0)
 
         q_rows = qT[0].rearrange("(o p t) r -> o p (t r)", o=PASSES, t=PACK)
@@ -93,7 +93,7 @@ def tile_attend_gat_lse_v_kernel(tc, qT, k_words, k_scales, lse, rw, dom, offs, 
         q_codes = [keep.tile([P, R], U32, name=f"q_codes{o}", align_bytes=64) for o in range(PASSES)]
         q_plane = [keep.tile([P, R], U8, name=f"q_plane{o}", align_bytes=64) for o in range(PASSES)]
         q_bf = [
-            [late.tile([P, 2 * R], BF16, name=f"q_bf{o}{u}", offset=(4 * o + 2 * u) * KIB, align_bytes=64) for u in range(2)]
+            [late.tile([P, 2 * R], BF16, name=f"q_bf{o}{u}", offset=Q_BF_AT[o][u] * KIB, align_bytes=64) for u in range(2)]
             for o in range(PASSES)
         ]
 
@@ -138,12 +138,12 @@ def tile_attend_gat_lse_v_kernel(tc, qT, k_words, k_scales, lse, rw, dom, offs, 
             q_quantize(1, j)
         for j in range(PACK):
             score_pass(1, j, 0, k_codes1[:])
-        k_codes_last = late.tile([P, HALF], U16, name="k_codes_last", offset=6 * KIB, align_bytes=64)
+        k_codes_last = late.tile([P, HALF], U16, name="k_codes_last", offset=12 * KIB, align_bytes=64)
         nc.vector.tensor_copy(k_codes_last[:], word_halves[:, 1, HALF:])
         for j in range(PACK):
             score_pass(1, j, 1, k_codes_last[:])
 
-        dom_codes = [keep.tile([P, P], U32, name=f"dom_codes{e}", align_bytes=64) for e in range(DV // P)]
+        dom_codes = {e: keep.tile([P, P], U32, name=f"dom_codes{e}", align_bytes=64) for e in (0, 1, 3)}
         dom_plane = keep.tile([P, DV], U8, name="dom_plane", align_bytes=64)
 
         def dom_interleave(e, engine_copy, dom_bf):
@@ -159,7 +159,7 @@ def tile_attend_gat_lse_v_kernel(tc, qT, k_words, k_scales, lse, rw, dom, offs, 
 
         p_rows = [
             keep.tile([P, PACK, HALF], F32, name="p_rows0", align_bytes=64),
-            keep.tile([P, PACK, HALF], F32, name="p_rows1", align_bytes=64),
+            late.tile([P, PACK, HALF], F32, name="p_rows1", offset=8 * KIB, align_bytes=64),
         ]
         for h in range(2):
             for j in range(PACK):
@@ -213,22 +213,23 @@ def tile_attend_gat_lse_v_kernel(tc, qT, k_words, k_scales, lse, rw, dom, offs, 
         def store(e, queue):
             queue.dma_start(out[e * P : (e + 1) * P, :], windows[e][:])
 
-        pw_rows = late.tile([P, PACK, HALF], BF16, name="pw_rows0", offset=13 * KIB, align_bytes=64)
+        pw_rows = late.tile([P, PACK, HALF], BF16, name="pw_rows0", offset=14 * KIB, align_bytes=64)
         for j in range(PACK):
             for piece in PIECES if j == PACK - 1 else (slice(0, HALF),):
                 nc.vector.tensor_scalar(pw_rows[:, j, piece], p_rows[0][:, j, piece], rw_sb[:, j : j + 1], None, MULT)
-        pw_bf0 = late.tile([P, PACK * HALF], BF16, name="pw_bf0", offset=10 * KIB, align_bytes=64)
+        pw_bf0 = keep.tile([P, PACK * HALF], BF16, name="pw_bf0", align_bytes=64)
         for piece in PIECES:
             nc.vector.tensor_copy(interleaved(pw_bf0, piece), pw_rows[:, :, piece].rearrange("p j (c i) -> p c j i", i=4))
         weights_quantize(0, pw_bf0)
         dom_interleave(1, nc.vector.tensor_copy, dom_early[:, PACK * P :])
         dom_quantize(1, dom_early[:, PACK * P :])
-        grad00 = bank("grad00", "bank00")
-        product(0, halves[0], grad00[:])
+        grad00 = [bank(f"grad00{k}", f"bank{2 * k}0", HALF // 2) for k in range(2)]
+        for k, piece in enumerate(PIECES):
+            product(0, piece, grad00[k][:])
         grad10 = bank("grad10", "bank10")
         product(1, halves[0], grad10[:])
 
-        pw_bf1 = late.tile([P, PACK * HALF], BF16, name="pw_bf1", offset=13 * KIB, align_bytes=64)
+        pw_bf1 = late.tile([P, PACK * HALF], BF16, name="pw_bf1", offset=14 * KIB, align_bytes=64)
         for piece in PIECES:
             nc.vector.tensor_tensor(
                 interleaved(pw_bf1, piece),
@@ -240,24 +241,28 @@ def tile_attend_gat_lse_v_kernel(tc, qT, k_words, k_scales, lse, rw, dom, offs, 
         grad01 = bank("grad01", "bank01")
         product(0, halves[1], grad01[:])
 
-        dom_bf2 = late.tile([P, PACK * P], BF16, name="dom_bf2", offset=6 * KIB, align_bytes=64)
+        dom_bf2 = late.tile([P, PACK * P], BF16, name="dom_bf2", offset=12 * KIB, align_bytes=64)
         dom_interleave(2, nc.scalar.copy, dom_bf2[:])
-        scalar_scatter(0, halves[0], leave_bank("grad00_sb", grad00, nc.scalar.copy))
+        grad00_sb = keep.tile([P, HALF], F32, name="grad00_sb", align_bytes=64)
+        for k, piece in enumerate(PIECES):
+            nc.scalar.copy(grad00_sb[:, piece], grad00[k][:])
+        grad10_sb = leave_bank("grad10_sb", grad10, nc.scalar.copy)
+        scalar_scatter(0, halves[0], grad00_sb)
+        scalar_scatter(1, halves[0], grad10_sb)
 
-        dom_bf3 = late.tile([P, PACK * P], BF16, name="dom_bf3", offset=10 * KIB, align_bytes=64)
+        dom_bf3 = late.tile([P, PACK * P], BF16, name="dom_bf3", offset=17 * KIB, align_bytes=64)
         dom_interleave(3, nc.vector.tensor_copy, dom_bf3[:])
+        dom_codes.setdefault(2, late.tile([P, P], U32, name="dom_codes2", offset=9 * KIB, align_bytes=64))
         dom_quantize(2, dom_bf2[:])
         dom_quantize(3, dom_bf3[:])
-        windows.append(late.tile([P, T], F32, name="window3", offset=6 * KIB, align_bytes=64))
-        nc.gpsimd.memset(windows[3][:].bitcast(I32), 0)
+        for e in (2, 3):
+            windows.append(late.tile([P, T], F32, name=f"window{e}", offset=(8 * e - 7) * KIB + KIB // 2, align_bytes=64))
+            nc.gpsimd.memset(windows[e][:].bitcast(I32), 0)
 
         grad11 = bank("grad11", "bank11")
         product(1, halves[1], grad11[:])
         grad30 = bank("grad30", "bank30")
         product(3, halves[0], grad30[:])
-        grad10_sb = late.tile([P, HALF], F32, name="grad10_sb", offset=14 * KIB, align_bytes=64)
-        nc.vector.tensor_copy(grad10_sb[:], grad10[:])
-        scalar_scatter(1, halves[0], grad10_sb)
         vector_scatter(0, halves[1], leave_bank("grad01_sb", grad01, nc.vector.tensor_copy))
         store(0, nc.sync)
         grad2 = bank("grad2", "bank01", N)

@@ -26,6 +26,7 @@ SCALE_ROW0 = P - 16 * PASSES
 Q_CUT = PACK * R - R // 2
 KIB = 1024
 Q_BF_AT = ((0, 2), (4, 12))
+P_ROWS_AT = ((20, 14), (17, 8))
 
 
 def tile_attend_gat_lse_v_kernel(tc, qT, k_words, k_scales, lse, rw, dom, offs, out):
@@ -42,7 +43,7 @@ def tile_attend_gat_lse_v_kernel(tc, qT, k_words, k_scales, lse, rw, dom, offs, 
         k_planes = [keep.tile([P, N], U8, name=f"k_plane{o}", align_bytes=64) for o in range(PASSES)]
         windows = [keep.tile([P, T], F32, name=f"window{w}", align_bytes=64) for w in range(2)]
         lse_sb = keep.tile([P, PACK], F32, name="lse_sb")
-        rw_sb = late.tile([P, PACK], F32, name="rw_sb", offset=17 * KIB, align_bytes=64)
+        rw_sb = keep.tile([P, PACK], F32, name="rw_sb")
         neg_lse = keep.tile([P, PACK], F32, name="neg_lse")
 
         nc.gpsimd.memset(scale_pool[:SCALE_ROW0, :].bitcast(I32), 0)
@@ -143,7 +144,7 @@ def tile_attend_gat_lse_v_kernel(tc, qT, k_words, k_scales, lse, rw, dom, offs, 
         for j in range(PACK):
             score_pass(1, j, 1, k_codes_last[:])
 
-        dom_codes = {e: keep.tile([P, P], U32, name=f"dom_codes{e}", align_bytes=64) for e in (0, 1, 3)}
+        dom_codes = {e: keep.tile([P, P], U32, name=f"dom_codes{e}", align_bytes=64) for e in (0, 1)}
         dom_plane = keep.tile([P, DV], U8, name="dom_plane", align_bytes=64)
 
         def dom_interleave(e, engine_copy, dom_bf):
@@ -154,17 +155,18 @@ def tile_attend_gat_lse_v_kernel(tc, qT, k_words, k_scales, lse, rw, dom, offs, 
             nc.vector.quantize_mx(dom_codes[e][:].bitcast(E5M2), dom_plane[:, e * P : (e + 1) * P], dom_bf)
 
         dom_early = turns.tile([P, 2 * PACK * P], BF16, name="dom_early", offset=KIB, align_bytes=64)
-        dom_interleave(0, nc.vector.tensor_copy, dom_early[:, : PACK * P])
+        for e in range(2):
+            dom_interleave(e, nc.vector.tensor_copy, dom_early[:, e * PACK * P : (e + 1) * PACK * P])
         dom_quantize(0, dom_early[:, : PACK * P])
 
         p_rows = [
-            keep.tile([P, PACK, HALF], F32, name="p_rows0", align_bytes=64),
-            late.tile([P, PACK, HALF], F32, name="p_rows1", offset=8 * KIB, align_bytes=64),
+            [late.tile([P, PACK, P], F32, name=f"p_rows{h}{k}", offset=P_ROWS_AT[h][k] * KIB, align_bytes=64) for k in range(2)]
+            for h in range(2)
         ]
         for h in range(2):
-            for j in range(PACK):
-                for piece in PIECES if j == PACK - 1 else (slice(0, HALF),):
-                    nc.scalar.activation(p_rows[h][:, j, piece], scores[j][h][:, piece], ACT.Exp, bias=neg_lse[:, j : j + 1])
+            for k, piece in enumerate(PIECES):
+                for j in range(PACK):
+                    nc.scalar.activation(p_rows[h][k][:, j, :], scores[j][h][:, piece], ACT.Exp, bias=neg_lse[:, j : j + 1])
 
         pw_codes = keep.tile([P, N], U32, name="pw_codes", align_bytes=64)
         pw_plane = keep.tile([P, N], U8, name="pw_plane", align_bytes=64)
@@ -213,33 +215,28 @@ def tile_attend_gat_lse_v_kernel(tc, qT, k_words, k_scales, lse, rw, dom, offs, 
         def store(e, queue):
             queue.dma_start(out[e * P : (e + 1) * P, :], windows[e][:])
 
-        pw_rows = late.tile([P, PACK, HALF], BF16, name="pw_rows0", offset=14 * KIB, align_bytes=64)
-        for j in range(PACK):
-            for piece in PIECES if j == PACK - 1 else (slice(0, HALF),):
-                nc.vector.tensor_scalar(pw_rows[:, j, piece], p_rows[0][:, j, piece], rw_sb[:, j : j + 1], None, MULT)
-        pw_bf0 = keep.tile([P, PACK * HALF], BF16, name="pw_bf0", align_bytes=64)
-        for piece in PIECES:
-            nc.vector.tensor_copy(interleaved(pw_bf0, piece), pw_rows[:, :, piece].rearrange("p j (c i) -> p c j i", i=4))
-        weights_quantize(0, pw_bf0)
-        dom_interleave(1, nc.vector.tensor_copy, dom_early[:, PACK * P :])
-        dom_quantize(1, dom_early[:, PACK * P :])
+        def weights(h, pw_bf):
+            for k, piece in enumerate(PIECES):
+                nc.vector.tensor_tensor(
+                    interleaved(pw_bf, piece),
+                    p_rows[h][k][:].rearrange("p j (c i) -> p c j i", i=4),
+                    rw_sb[:].unsqueeze(1).unsqueeze(3).to_broadcast([P, HALF // 8, PACK, 4]),
+                    MULT,
+                )
+            weights_quantize(h, pw_bf)
+
+        weights(0, keep.tile([P, PACK * HALF], BF16, name="pw_bf0", align_bytes=64))
         grad00 = [bank(f"grad00{k}", f"bank{2 * k}0", HALF // 2) for k in range(2)]
         for k, piece in enumerate(PIECES):
             product(0, piece, grad00[k][:])
+        dom_quantize(1, dom_early[:, PACK * P :])
         grad10 = bank("grad10", "bank10")
         product(1, halves[0], grad10[:])
 
-        pw_bf1 = late.tile([P, PACK * HALF], BF16, name="pw_bf1", offset=14 * KIB, align_bytes=64)
-        for piece in PIECES:
-            nc.vector.tensor_tensor(
-                interleaved(pw_bf1, piece),
-                p_rows[1][:, :, piece].rearrange("p j (c i) -> p c j i", i=4),
-                rw_sb[:].unsqueeze(1).unsqueeze(3).to_broadcast([P, HALF // 8, PACK, 4]),
-                MULT,
-            )
-        weights_quantize(1, pw_bf1)
-        grad01 = bank("grad01", "bank01")
-        product(0, halves[1], grad01[:])
+        weights(1, late.tile([P, PACK * HALF], BF16, name="pw_bf1", offset=14 * KIB, align_bytes=64))
+        grad01 = [bank(f"grad01{k}", f"bank{2 * k}1", HALF // 2) for k in range(2)]
+        for k, piece in enumerate(PIECES):
+            product(0, slice(HALF + piece.start, HALF + piece.stop), grad01[k][:])
 
         dom_bf2 = late.tile([P, PACK * P], BF16, name="dom_bf2", offset=12 * KIB, align_bytes=64)
         dom_interleave(2, nc.scalar.copy, dom_bf2[:])
@@ -252,7 +249,8 @@ def tile_attend_gat_lse_v_kernel(tc, qT, k_words, k_scales, lse, rw, dom, offs, 
 
         dom_bf3 = late.tile([P, PACK * P], BF16, name="dom_bf3", offset=17 * KIB, align_bytes=64)
         dom_interleave(3, nc.vector.tensor_copy, dom_bf3[:])
-        dom_codes.setdefault(2, late.tile([P, P], U32, name="dom_codes2", offset=9 * KIB, align_bytes=64))
+        for e in (2, 3):
+            dom_codes.setdefault(e, late.tile([P, P], U32, name=f"dom_codes{e}", offset=8 * KIB + e * KIB // 2 - KIB // 2, align_bytes=64))
         dom_quantize(2, dom_bf2[:])
         dom_quantize(3, dom_bf3[:])
         for e in (2, 3):
@@ -263,9 +261,12 @@ def tile_attend_gat_lse_v_kernel(tc, qT, k_words, k_scales, lse, rw, dom, offs, 
         product(1, halves[1], grad11[:])
         grad30 = bank("grad30", "bank30")
         product(3, halves[0], grad30[:])
-        vector_scatter(0, halves[1], leave_bank("grad01_sb", grad01, nc.vector.tensor_copy))
+        grad01_sb = keep.tile([P, HALF], F32, name="grad01_sb", align_bytes=64)
+        for k, piece in enumerate(PIECES):
+            nc.vector.tensor_copy(grad01_sb[:, piece], grad01[k][:])
+        vector_scatter(0, halves[1], grad01_sb)
         store(0, nc.sync)
-        grad2 = bank("grad2", "bank01", N)
+        grad2 = bank("grad2", "bank21", N)
         product(2, whole, grad2[:])
         grad11_sb = leave_bank("grad11_sb", grad11, nc.scalar.copy)
         grad30_sb = leave_bank("grad30_sb", grad30, nc.scalar.copy)
@@ -273,7 +274,7 @@ def tile_attend_gat_lse_v_kernel(tc, qT, k_words, k_scales, lse, rw, dom, offs, 
         store(1, nc.scalar)
         vector_scatter(2, whole, leave_bank("grad2_sb", grad2, nc.vector.tensor_copy))
         store(2, nc.sync)
-        grad31 = bank("grad31", "bank01")
+        grad31 = bank("grad31", "bank21")
         product(3, halves[1], grad31[:])
         scalar_scatter(3, halves[0], grad30_sb)
         scalar_scatter(3, halves[1], leave_bank("grad31_sb", grad31, nc.scalar.copy))

@@ -25,8 +25,13 @@ PIECES = (slice(0, HALF // 2), slice(HALF // 2, HALF))
 SCALE_ROW0 = P - 16 * PASSES
 Q_CUT = PACK * R - R // 2
 KIB = 1024
-Q_BF_AT = ((0, 2), (4, 12))
-P_ROWS_AT = ((20, 14), (17, 8))
+WINDOW2 = 10 * KIB
+WINDOW3 = WINDOW2 + 4 * T
+P_ROWS1 = WINDOW2 - 7 * KIB // 2
+Q_LAST = P_ROWS1 + 4 * KIB
+P_ROWS0 = Q_LAST + 2 * KIB
+DOM_EARLY = P_ROWS0 + 4 * KIB
+Q_BF_AT = ((0, 2 * KIB), (Q_LAST, 4 * KIB))
 
 
 def tile_attend_gat_lse_v_kernel(tc, qT, k_words, k_scales, lse, rw, dom, offs, out):
@@ -94,13 +99,13 @@ def tile_attend_gat_lse_v_kernel(tc, qT, k_words, k_scales, lse, rw, dom, offs, 
         q_codes = [keep.tile([P, R], U32, name=f"q_codes{o}", align_bytes=64) for o in range(PASSES)]
         q_plane = [keep.tile([P, R], U8, name=f"q_plane{o}", align_bytes=64) for o in range(PASSES)]
         q_bf = [
-            [late.tile([P, 2 * R], BF16, name=f"q_bf{o}{u}", offset=Q_BF_AT[o][u] * KIB, align_bytes=64) for u in range(2)]
+            [late.tile([P, 2 * R], BF16, name=f"q_bf{o}{u}", offset=Q_BF_AT[o][u], align_bytes=64) for u in range(2)]
             for o in range(PASSES)
         ]
 
-        def q_interleave(o, h, u, engine_copy):
-            src = q_raw[o][:].rearrange("p (t h s u v) -> p h u s t v", t=PACK, h=2, u=2, v=2)[:, h, u]
-            dst = q_bf[o][u][:].rearrange("p (v h s t) -> p h s t v", t=PACK, v=2, h=2)[:, h]
+        def q_interleave(o, rows, u, engine_copy):
+            src = q_raw[o][:].rearrange("p (t s u v) -> p u s t v", t=PACK, u=2, v=2)[:, u, rows]
+            dst = q_bf[o][u][:].rearrange("p (v s t) -> p s t v", t=PACK, v=2)[:, rows]
             engine_copy(dst, src)
 
         def q_quantize(o, j):
@@ -123,23 +128,25 @@ def tile_attend_gat_lse_v_kernel(tc, qT, k_words, k_scales, lse, rw, dom, offs, 
                 stop=(o == PASSES - 1),
             )
 
-        q_interleave(0, 0, 0, nc.vector.tensor_copy)
-        q_interleave(0, 1, 0, nc.scalar.copy)
-        q_interleave(0, 0, 1, nc.vector.tensor_copy)
-        q_interleave(0, 1, 1, nc.scalar.copy)
+        low, high = slice(0, P // 2), slice(P // 2, P)
+        for u in range(2):
+            q_interleave(0, low, u, nc.vector.tensor_copy)
+            q_interleave(0, high, u, nc.scalar.copy)
         for j in range(PACK):
             q_quantize(0, j)
         for j in range(PACK):
             for h in range(2):
                 score_pass(0, j, h, k_codes0[:, h * HALF : (h + 1) * HALF])
-        for h in range(2):
-            q_interleave(1, h, 0, nc.vector.tensor_copy)
-            q_interleave(1, h, 1, nc.scalar.copy)
+        for rows in (low, high):
+            q_interleave(1, rows, 0, nc.vector.tensor_copy)
+        q_interleave(1, low, 1, nc.scalar.copy)
+        q_interleave(1, slice(P // 2, 3 * P // 4), 1, nc.scalar.copy)
+        q_interleave(1, slice(3 * P // 4, P), 1, nc.vector.tensor_copy)
         for j in range(PACK):
             q_quantize(1, j)
         for j in range(PACK):
             score_pass(1, j, 0, k_codes1[:])
-        k_codes_last = late.tile([P, HALF], U16, name="k_codes_last", offset=12 * KIB, align_bytes=64)
+        k_codes_last = late.tile([P, HALF], U16, name="k_codes_last", offset=Q_LAST, align_bytes=64)
         nc.vector.tensor_copy(k_codes_last[:], word_halves[:, 1, HALF:])
         for j in range(PACK):
             score_pass(1, j, 1, k_codes_last[:])
@@ -154,19 +161,24 @@ def tile_attend_gat_lse_v_kernel(tc, qT, k_words, k_scales, lse, rw, dom, offs, 
         def dom_quantize(e, dom_bf):
             nc.vector.quantize_mx(dom_codes[e][:].bitcast(E5M2), dom_plane[:, e * P : (e + 1) * P], dom_bf)
 
-        dom_early = turns.tile([P, 2 * PACK * P], BF16, name="dom_early", offset=KIB, align_bytes=64)
+        dom_early = late.tile([P, 2 * PACK * P], BF16, name="dom_early", offset=DOM_EARLY, align_bytes=64)
         for e in range(2):
             dom_interleave(e, nc.vector.tensor_copy, dom_early[:, e * PACK * P : (e + 1) * PACK * P])
         dom_quantize(0, dom_early[:, : PACK * P])
 
         p_rows = [
-            [late.tile([P, PACK, P], F32, name=f"p_rows{h}{k}", offset=P_ROWS_AT[h][k] * KIB, align_bytes=64) for k in range(2)]
-            for h in range(2)
+            late.tile([P, PACK, HALF], F32, name=f"p_rows{h}", offset=at, align_bytes=64)
+            for h, at in enumerate((P_ROWS0, P_ROWS1))
         ]
-        for h in range(2):
-            for k, piece in enumerate(PIECES):
-                for j in range(PACK):
-                    nc.scalar.activation(p_rows[h][k][:, j, :], scores[j][h][:, piece], ACT.Exp, bias=neg_lse[:, j : j + 1])
+
+        def exps(h, tiles, piece):
+            for j in tiles:
+                nc.scalar.activation(p_rows[h][:, j, piece], scores[j][h][:, piece], ACT.Exp, bias=neg_lse[:, j : j + 1])
+
+        exps(0, (0, 1), slice(0, HALF))
+        for piece in PIECES:
+            exps(0, (2, 3), piece)
+        exps(1, range(PACK), slice(0, HALF))
 
         pw_codes = keep.tile([P, N], U32, name="pw_codes", align_bytes=64)
         pw_plane = keep.tile([P, N], U8, name="pw_plane", align_bytes=64)
@@ -216,10 +228,10 @@ def tile_attend_gat_lse_v_kernel(tc, qT, k_words, k_scales, lse, rw, dom, offs, 
             queue.dma_start(out[e * P : (e + 1) * P, :], windows[e][:])
 
         def weights(h, pw_bf):
-            for k, piece in enumerate(PIECES):
+            for piece in PIECES:
                 nc.vector.tensor_tensor(
                     interleaved(pw_bf, piece),
-                    p_rows[h][k][:].rearrange("p j (c i) -> p c j i", i=4),
+                    p_rows[h][:, :, piece].rearrange("p j (c i) -> p c j i", i=4),
                     rw_sb[:].unsqueeze(1).unsqueeze(3).to_broadcast([P, HALF // 8, PACK, 4]),
                     MULT,
                 )
@@ -233,12 +245,12 @@ def tile_attend_gat_lse_v_kernel(tc, qT, k_words, k_scales, lse, rw, dom, offs, 
         grad10 = bank("grad10", "bank10")
         product(1, halves[0], grad10[:])
 
-        weights(1, late.tile([P, PACK * HALF], BF16, name="pw_bf1", offset=14 * KIB, align_bytes=64))
+        weights(1, late.tile([P, PACK * HALF], BF16, name="pw_bf1", offset=P_ROWS0, align_bytes=64))
         grad01 = [bank(f"grad01{k}", f"bank{2 * k}1", HALF // 2) for k in range(2)]
         for k, piece in enumerate(PIECES):
             product(0, slice(HALF + piece.start, HALF + piece.stop), grad01[k][:])
 
-        dom_bf2 = late.tile([P, PACK * P], BF16, name="dom_bf2", offset=12 * KIB, align_bytes=64)
+        dom_bf2 = late.tile([P, PACK * P], BF16, name="dom_bf2", offset=Q_LAST, align_bytes=64)
         dom_interleave(2, nc.scalar.copy, dom_bf2[:])
         grad00_sb = keep.tile([P, HALF], F32, name="grad00_sb", align_bytes=64)
         for k, piece in enumerate(PIECES):
@@ -247,14 +259,14 @@ def tile_attend_gat_lse_v_kernel(tc, qT, k_words, k_scales, lse, rw, dom, offs, 
         scalar_scatter(0, halves[0], grad00_sb)
         scalar_scatter(1, halves[0], grad10_sb)
 
-        dom_bf3 = late.tile([P, PACK * P], BF16, name="dom_bf3", offset=17 * KIB, align_bytes=64)
+        dom_bf3 = late.tile([P, PACK * P], BF16, name="dom_bf3", offset=DOM_EARLY + KIB, align_bytes=64)
         dom_interleave(3, nc.vector.tensor_copy, dom_bf3[:])
         for e in (2, 3):
-            dom_codes.setdefault(e, late.tile([P, P], U32, name=f"dom_codes{e}", offset=8 * KIB + e * KIB // 2 - KIB // 2, align_bytes=64))
+            dom_codes.setdefault(e, late.tile([P, P], U32, name=f"dom_codes{e}", offset=P_ROWS1 + (e - 2) * KIB // 2, align_bytes=64))
         dom_quantize(2, dom_bf2[:])
         dom_quantize(3, dom_bf3[:])
-        for e in (2, 3):
-            windows.append(late.tile([P, T], F32, name=f"window{e}", offset=(8 * e - 7) * KIB + KIB // 2, align_bytes=64))
+        for e, at in ((2, WINDOW2), (3, WINDOW3)):
+            windows.append(late.tile([P, T], F32, name=f"window{e}", offset=at, align_bytes=64))
             nc.gpsimd.memset(windows[e][:].bitcast(I32), 0)
 
         grad11 = bank("grad11", "bank11")

@@ -69,16 +69,16 @@ def tile_attend_gat_lse_v_kernel(tc, qT, k_words, k_scales, lse, rw, dom, offs, 
         scale_picked = keep.tile([P, N], U8, name="scale_picked", align_bytes=64)
         nc.vector.tensor_copy(scale_picked[:], scale_pool[:].indirect(offsets[:]))
 
-        def plane_moves(o):
-            for i in range(4):
+        def plane_moves(o, queues):
+            for i, queue in enumerate(queues):
                 first = SCALE_ROW0 + 16 * o + i
-                nc.sync.dma_start(k_planes[o][i:P:32, :].bitcast(I32), scale_picked[first : first + 13 : 4, :].bitcast(I32))
+                queue.dma_start(k_planes[o][i:P:32, :].bitcast(I32), scale_picked[first : first + 13 : 4, :].bitcast(I32))
 
-        plane_moves(0)
+        plane_moves(0, (nc.scalar,) * 4)
         q_raw.append(turns.tile([P, PACK * R], F32, name="q_raw1", offset=9 * KIB, align_bytes=64))
         nc.sync.dma_start(q_raw[1][:, :Q_CUT], q_rows[1][:, :Q_CUT])
         nc.sync.dma_start(q_raw[1][:, Q_CUT:], q_rows[1][:, Q_CUT:])
-        plane_moves(1)
+        plane_moves(1, (nc.sync,) * 4)
         dom_raw = [
             turns.tile([P, PACK, DV // 2], F32, name="dom_raw0", offset=5 * KIB, align_bytes=64),
             keep.tile([P, PACK, DV // 2], F32, name="dom_raw1", tag="word_pool", align_bytes=64),

@@ -175,9 +175,9 @@ def tile_attend_gat_lse_v_kernel(tc, qT, k_words, k_scales, lse, rw, dom, offs, 
             for j in tiles:
                 nc.scalar.activation(p_rows[h][:, j, piece], scores[j][h][:, piece], ACT.Exp, bias=neg_lse[:, j : j + 1])
 
-        exps(0, (0, 1), slice(0, HALF))
+        exps(0, (0,), slice(0, HALF))
         for piece in PIECES:
-            exps(0, (2, 3), piece)
+            exps(0, (1, 2, 3), piece)
         exps(1, range(PACK), slice(0, HALF))
 
         pw_codes = keep.tile([P, N], U32, name="pw_codes", align_bytes=64)

from contextlib import ExitStack

import concourse.mybir as mybir

N, T, D, DV, R = 512, 2048, 1024, 512, 512
FLOPS = 2 * R * N * D + 2 * DV * N * R

F32 = mybir.dt.float32
BF16 = mybir.dt.bfloat16
I32 = mybir.dt.int32
U32 = mybir.dt.uint32
U16 = mybir.dt.uint16
U8 = mybir.dt.uint8
E4M3 = mybir.dt.float8_e4m3fn_x4
E5M2 = mybir.dt.float8_e5m2_x4
E2M1 = mybir.dt.float4_e2m1fn_x4
ACT = mybir.ActivationFunctionType
MULT = mybir.AluOpType.mult

P = 128
PACK = 4
PASSES = D // (P * PACK)
HALF = N // 2
PIECES = (slice(0, HALF // 2), slice(HALF // 2, HALF))
SCALE_ROW0 = P - 16 * PASSES
Q_CUT = PACK * R - R // 2
KIB = 1024
WINDOW2 = 10 * KIB
WINDOW3 = WINDOW2 + 4 * T
P_ROWS1 = WINDOW2 - 7 * KIB // 2
Q_LAST = P_ROWS1 + 4 * KIB
P_ROWS0 = Q_LAST + 2 * KIB
DOM_EARLY = P_ROWS0 + 4 * KIB
Q_BF_AT = ((0, 2 * KIB), (Q_LAST, 4 * KIB))


def tile_attend_gat_lse_v_kernel(tc, qT, k_words, k_scales, lse, rw, dom, offs, out):
    nc = tc.nc
    with ExitStack() as ctx:
        keep = ctx.enter_context(tc.tile_pool(name="keep", bufs=1))
        turns = ctx.enter_context(tc.tile_pool(name="turns", bufs=1))
        late = ctx.enter_context(tc.tile_pool(name="late", bufs=1))
        psum = ctx.enter_context(tc.psum_pool(name="psum", bufs=1))

        offsets = keep.tile([P, N // 16], U16, name="offsets")
        scale_pool = turns.tile([P, T], U8, name="scale_pool", offset=8 * KIB, align_bytes=64)
        word_pool = keep.tile([P, T], U32, name="word_pool", tag="word_pool", align_bytes=64)
        k_planes = [keep.tile([P, N], U8, name=f"k_plane{o}", align_bytes=64) for o in range(PASSES)]
        windows = [keep.tile([P, T], F32, name=f"window{w}", align_bytes=64) for w in range(2)]
        lse_sb = keep.tile([P, PACK], F32, name="lse_sb")
        rw_sb = keep.tile([P, PACK], F32, name="rw_sb")
        neg_lse = keep.tile([P, PACK], F32, name="neg_lse")

        nc.gpsimd.memset(scale_pool[:SCALE_ROW0, :].bitcast(I32), 0)
        for k_plane in k_planes:
            nc.gpsimd.memset(k_plane[:].bitcast(I32), 0)
        for window in windows:
            nc.gpsimd.memset(window[:].bitcast(I32), 0)

        q_rows = qT[0].rearrange("(o p t) r -> o p (t r)", o=PASSES, t=PACK)
        q_raw = [keep.tile([P, PACK * R], F32, name="q_raw0", align_bytes=64)]
        nc.sync.dma_start(scale_pool[SCALE_ROW0:, :].bitcast(I32), k_scales.bitcast(I32).rearrange("o f t -> (o f) t"))
        nc.sync.dma_start(offsets[:], offs)
        nc.sync.dma_start(word_pool[:].bitcast(I32), k_words[0].rearrange("p t b -> p (t b)").bitcast(I32))
        nc.sync.dma_start(lse_sb[:], lse[0].rearrange("(p j) one -> p (j one)", j=PACK))
        nc.sync.dma_start(rw_sb[:], rw[0].rearrange("(p j) one -> p (j one)", j=PACK))
        nc.sync.dma_start(q_raw[0][:], q_rows[0])

        scale_picked = keep.tile([P, N], U8, name="scale_picked", align_bytes=64)
        nc.vector.tensor_copy(scale_picked[:], scale_pool[:].indirect(offsets[:]))

        def plane_moves(o, queues):
            for i, queue in enumerate(queues):
                first = SCALE_ROW0 + 16 * o + i
                queue.dma_start(k_planes[o][i:P:32, :].bitcast(I32), scale_picked[first : first + 13 : 4, :].bitcast(I32))

        plane_moves(0, (nc.scalar,) * 4)
        q_raw.append(turns.tile([P, PACK * R], F32, name="q_raw1", offset=9 * KIB, align_bytes=64))
        nc.sync.dma_start(q_raw[1][:, :Q_CUT], q_rows[1][:, :Q_CUT])
        nc.sync.dma_start(q_raw[1][:, Q_CUT:], q_rows[1][:, Q_CUT:])
        plane_moves(1, (nc.sync,) * 4)
        dom_raw = [
            turns.tile([P, PACK, DV // 2], F32, name="dom_raw0", offset=5 * KIB, align_bytes=64),
            keep.tile([P, PACK, DV // 2], F32, name="dom_raw1", tag="word_pool", align_bytes=64),
        ]
        dom_rows = dom[0].rearrange("(p j) (h e) -> h p j e", j=PACK, h=2)
        nc.sync.dma_start(dom_raw[0][:], dom_rows[0])

        word_picked = keep.tile([P, N], U32, name="word_picked", align_bytes=64)
        nc.vector.tensor_copy(word_picked[:], word_pool[:].indirect(offsets[:]))
        nc.sync.dma_start(dom_raw[1][:], dom_rows[1])
        word_halves = word_picked[:].bitcast(U16).rearrange("p (n o) -> p o n", o=PASSES)
        k_codes0 = keep.tile([P, N], U16, name="k_codes0", align_bytes=64)
        k_codes1 = keep.tile([P, HALF], U16, name="k_codes1", align_bytes=64)
        nc.vector.tensor_copy(k_codes0[:], word_halves[:, 0, :])
        nc.vector.tensor_copy(k_codes1[:], word_halves[:, 1, :HALF])
        nc.scalar.activation(neg_lse[:], lse_sb[:], ACT.Copy, scale=-1.0)

        q_codes = [keep.tile([P, R], U32, name=f"q_codes{o}", align_bytes=64) for o in range(PASSES)]
        q_plane = [keep.tile([P, R], U8, name=f"q_plane{o}", align_bytes=64) for o in range(PASSES)]
        q_bf = [
            [late.tile([P, 2 * R], BF16, name=f"q_bf{o}{u}", offset=Q_BF_AT[o][u], align_bytes=64) for u in range(2)]
            for o in range(PASSES)
        ]

        def q_interleave(o, rows, u, engine_copy):
            src = q_raw[o][:].rearrange("p (t s u v) -> p u s t v", t=PACK, u=2, v=2)[:, u, rows]
            dst = q_bf[o][u][:].rearrange("p (v s t) -> p s t v", t=PACK, v=2)[:, rows]
            engine_copy(dst, src)

        def q_quantize(o, j):
            cols = slice(j * P, (j + 1) * P)
            nc.vector.quantize_mx(
                q_codes[o][:, cols].bitcast(E4M3), q_plane[o][:, cols], q_bf[o][j // 2][:, (j % 2) * R : (j % 2 + 1) * R]
            )

        scores = [[psum.tile([P, HALF], F32, name=f"scores{j}{h}", tag=f"bank{j}{h}") for h in range(2)] for j in range(PACK)]

        def score_pass(o, j, h, codes):
            cols = slice(j * P, (j + 1) * P)
            nc.tensor.matmul_mx(
                scores[j][h][:],
                lhsT=q_codes[o][:, cols].bitcast(E4M3),
                lhsT_scale=q_plane[o][:, cols],
                rhs=codes.bitcast(E2M1),
                rhs_scale=k_planes[o][:, h * HALF : (h + 1) * HALF],
                start=(o == 0),
                stop=(o == PASSES - 1),
            )

        low, high = slice(0, P // 2), slice(P // 2, P)
        for u in range(2):
            q_interleave(0, low, u, nc.vector.tensor_copy)
            q_interleave(0, high, u, nc.scalar.copy)
        for j in range(PACK):
            q_quantize(0, j)
        for j in range(PACK):
            for h in range(2):
                score_pass(0, j, h, k_codes0[:, h * HALF : (h + 1) * HALF])
        for rows in (low, high):
            q_interleave(1, rows, 0, nc.vector.tensor_copy)
        q_interleave(1, low, 1, nc.scalar.copy)
        q_interleave(1, slice(P // 2, 3 * P // 4), 1, nc.scalar.copy)
        q_interleave(1, slice(3 * P // 4, P), 1, nc.vector.tensor_copy)
        for j in range(PACK):
            q_quantize(1, j)
        for j in range(PACK):
            score_pass(1, j, 0, k_codes1[:])
        k_codes_last = late.tile([P, HALF], U16, name="k_codes_last", offset=Q_LAST, align_bytes=64)
        nc.vector.tensor_copy(k_codes_last[:], word_halves[:, 1, HALF:])
        for j in range(PACK):
            score_pass(1, j, 1, k_codes_last[:])

        dom_codes = {e: keep.tile([P, P], U32, name=f"dom_codes{e}", align_bytes=64) for e in (0, 1)}
        dom_plane = keep.tile([P, DV], U8, name="dom_plane", align_bytes=64)

        def dom_interleave(e, engine_copy, dom_bf):
            raw = dom_raw[e // 2][:, :, (e % 2) * P : (e % 2 + 1) * P]
            engine_copy(dom_bf.rearrange("p (c i j) -> p c j i", i=4, j=PACK), raw.rearrange("p j (c i) -> p c j i", i=4))

        def dom_quantize(e, dom_bf):
            nc.vector.quantize_mx(dom_codes[e][:].bitcast(E5M2), dom_plane[:, e * P : (e + 1) * P], dom_bf)

        dom_early = late.tile([P, 2 * PACK * P], BF16, name="dom_early", offset=DOM_EARLY, align_bytes=64)
        for e in range(2):
            dom_interleave(e, nc.vector.tensor_copy, dom_early[:, e * PACK * P : (e + 1) * PACK * P])
        dom_quantize(0, dom_early[:, : PACK * P])

        p_rows = [
            late.tile([P, PACK, HALF], F32, name=f"p_rows{h}", offset=at, align_bytes=64)
            for h, at in enumerate((P_ROWS0, P_ROWS1))
        ]

        def exps(h, tiles, piece):
            for j in tiles:
                nc.scalar.activation(p_rows[h][:, j, piece], scores[j][h][:, piece], ACT.Exp, bias=neg_lse[:, j : j + 1])

        exps(0, (0,), slice(0, HALF))
        for piece in PIECES:
            exps(0, (1, 2, 3), piece)
        exps(1, range(PACK), slice(0, HALF))

        pw_codes = keep.tile([P, N], U32, name="pw_codes", align_bytes=64)
        pw_plane = keep.tile([P, N], U8, name="pw_plane", align_bytes=64)

        def interleaved(pw_bf, piece):
            return pw_bf[:, PACK * piece.start : PACK * piece.stop].rearrange("p (c i j) -> p c j i", j=PACK, i=4)

        def weights_quantize(h, pw_bf):
            for piece in PIECES:
                cols = slice(h * HALF + piece.start, h * HALF + piece.stop)
                nc.vector.quantize_mx(
                    pw_codes[:, cols].bitcast(E4M3), pw_plane[:, cols], pw_bf[:, PACK * piece.start : PACK * piece.stop]
                )

        def product(e, slots, grad):
            nc.tensor.matmul_mx(
                grad,
                lhsT=dom_codes[e][:].bitcast(E5M2),
                lhsT_scale=dom_plane[:, e * P : (e + 1) * P],
                rhs=pw_codes[:, slots].bitcast(E4M3),
                rhs_scale=pw_plane[:, slots],
                start=True,
                stop=True,
            )

        def bank(name, tag, width=HALF):
            return psum.tile([P, width], F32, name=name, tag=tag)

        halves = (slice(0, HALF), slice(HALF, N))
        whole = slice(0, N)

        def places(e, slots):
            return windows[e][:].indirect(offsets[:, slots.start // 16 : slots.stop // 16])

        def leave_bank(name, grad, engine_copy):
            grad_sb = keep.tile(list(grad.shape), F32, name=name, align_bytes=64)
            engine_copy(grad_sb[:], grad[:])
            return grad_sb

        def scalar_scatter(e, slots, grad_sb):
            nc.scalar.activation(places(e, slots), grad_sb[:], ACT.Copy)

        def vector_scatter(e, slots, grad_sb):
            nc.vector.tensor_copy(places(e, slots), grad_sb[:])

        def store(e, queue):
            queue.dma_start(out[e * P : (e + 1) * P, :], windows[e][:])

        def weights(h, pw_bf):
            for piece in PIECES:
                nc.vector.tensor_tensor(
                    interleaved(pw_bf, piece),
                    p_rows[h][:, :, piece].rearrange("p j (c i) -> p c j i", i=4),
                    rw_sb[:].unsqueeze(1).unsqueeze(3).to_broadcast([P, HALF // 8, PACK, 4]),
                    MULT,
                )
            weights_quantize(h, pw_bf)

        weights(0, keep.tile([P, PACK * HALF], BF16, name="pw_bf0", align_bytes=64))
        grad00 = [bank(f"grad00{k}", f"bank{2 * k}0", HALF // 2) for k in range(2)]
        for k, piece in enumerate(PIECES):
            product(0, piece, grad00[k][:])
        dom_quantize(1, dom_early[:, PACK * P :])
        grad10 = bank("grad10", "bank10")
        product(1, halves[0], grad10[:])

        weights(1, late.tile([P, PACK * HALF], BF16, name="pw_bf1", offset=P_ROWS0, align_bytes=64))
        grad01 = [bank(f"grad01{k}", f"bank{2 * k}1", HALF // 2) for k in range(2)]
        for k, piece in enumerate(PIECES):
            product(0, slice(HALF + piece.start, HALF + piece.stop), grad01[k][:])

        dom_bf2 = late.tile([P, PACK * P], BF16, name="dom_bf2", offset=Q_LAST, align_bytes=64)
        dom_interleave(2, nc.scalar.copy, dom_bf2[:])
        grad00_sb = keep.tile([P, HALF], F32, name="grad00_sb", align_bytes=64)
        for k, piece in enumerate(PIECES):
            nc.scalar.copy(grad00_sb[:, piece], grad00[k][:])
        grad10_sb = leave_bank("grad10_sb", grad10, nc.scalar.copy)
        scalar_scatter(0, halves[0], grad00_sb)
        scalar_scatter(1, halves[0], grad10_sb)

        dom_bf3 = late.tile([P, PACK * P], BF16, name="dom_bf3", offset=DOM_EARLY + KIB, align_bytes=64)
        dom_interleave(3, nc.vector.tensor_copy, dom_bf3[:])
        for e in (2, 3):
            dom_codes.setdefault(e, late.tile([P, P], U32, name=f"dom_codes{e}", offset=P_ROWS1 + (e - 2) * KIB // 2, align_bytes=64))
        dom_quantize(2, dom_bf2[:])
        dom_quantize(3, dom_bf3[:])
        for e, at in ((2, WINDOW2), (3, WINDOW3)):
            windows.append(late.tile([P, T], F32, name=f"window{e}", offset=at, align_bytes=64))
            nc.gpsimd.memset(windows[e][:].bitcast(I32), 0)

        grad11 = bank("grad11", "bank11")
        product(1, halves[1], grad11[:])
        grad30 = bank("grad30", "bank30")
        product(3, halves[0], grad30[:])
        grad01_sb = keep.tile([P, HALF], F32, name="grad01_sb", align_bytes=64)
        for k, piece in enumerate(PIECES):
            nc.vector.tensor_copy(grad01_sb[:, piece], grad01[k][:])
        vector_scatter(0, halves[1], grad01_sb)
        store(0, nc.sync)
        grad2 = bank("grad2", "bank21", N)
        product(2, whole, grad2[:])
        grad11_sb = leave_bank("grad11_sb", grad11, nc.scalar.copy)
        grad30_sb = leave_bank("grad30_sb", grad30, nc.scalar.copy)
        scalar_scatter(1, halves[1], grad11_sb)
        store(1, nc.scalar)
        vector_scatter(2, whole, leave_bank("grad2_sb", grad2, nc.vector.tensor_copy))
        store(2, nc.sync)
        grad31 = bank("grad31", "bank21")
        product(3, halves[1], grad31[:])
        scalar_scatter(3, halves[0], grad30_sb)
        scalar_scatter(3, halves[1], leave_bank("grad31_sb", grad31, nc.scalar.copy))
        store(3, nc.scalar)
